import numpy as np
import ml_dtypes


def mxq(x, axis, fmt="e4m3"):
    dtype, down = {"e4m3": (ml_dtypes.float8_e4m3fn, 7), "e5m2": (ml_dtypes.float8_e5m2, 14)}[fmt]
    v = np.moveaxis(np.asarray(x, np.float32).astype(ml_dtypes.bfloat16).astype(np.float64), axis, -1)
    blocks = v.reshape(v.shape[:-1] + (-1, 32))
    amax = np.abs(blocks).max(-1, keepdims=True)
    byte = np.maximum(np.where(amax > 0, np.frexp(amax)[1] - 1 + 127, 0) - down, 1)
    scale = np.exp2(byte - 127.0)
    codes = (blocks / scale).astype(np.float32).astype(dtype).astype(np.float64)
    return np.moveaxis((codes * scale).reshape(v.shape), -1, axis)


WIDE = False


def mx_kscale(k):
    if not WIDE:
        return np.ones(k)
    levels = np.array([24, -24, 12, -12, 0])
    if k % 512:
        return np.exp2(np.random.permutation(np.resize(levels, k // 32))).repeat(32)
    a = np.empty((k // 512, 16))
    for p in range(k // 512):
        a[p, :8] = np.random.permutation(np.resize(levels, 8))
        for g in range(8):
            far = levels[np.abs(levels - a[p, g]) >= 10]
            a[p, g + 8] = far[np.random.randint(len(far))]
    return np.exp2(a.ravel()).repeat(32)


def f64(x):
    return np.asarray(x).astype(np.float64)


def striped(idx):
    return np.tile(idx.reshape(-1, 16).T, (8, 1)).astype(np.uint16)


def unstriped(offs):
    return offs[:16].T.reshape(-1).astype(np.int64)


def striped8(idx):
    return np.concatenate([v.reshape(-1, 16).T for v in idx]).astype(np.uint16)


def unstriped8(offs):
    return np.stack([offs[16 * g:16 * g + 16].T.reshape(-1) for g in range(8)]).astype(np.int64)


E2M1 = np.array([0.0, 0.5, 1.0, 1.5, 2.0, 3.0, 4.0, 6.0, -0.0, -0.5, -1.0, -1.5, -2.0, -3.0, -4.0, -6.0])


def pack_weight(w, fmt):
    k, n = w.shape
    w = f64(np.asarray(w, np.float32).astype(ml_dtypes.bfloat16)).reshape(k // 32, 32, n)
    amax = np.abs(w).max(1)
    if fmt == "e4m3":
        byte = np.frexp(amax)[1] - 1 + 127 - 7
    else:
        mant, ex = np.frexp(amax / 6.0)
        byte = np.where(mant > 0.5, ex, ex - 1) + 127
    byte = np.clip(np.where(amax > 0, byte, 1), 1, 254)
    scaled = (w * np.exp2(127.0 - byte)[:, None, :]).reshape(k, n).astype(np.float32)
    by_word = np.ascontiguousarray(scaled.reshape(k // 512, 128, 4, n).transpose(0, 1, 3, 2))
    if fmt == "e4m3":
        words = by_word.astype(ml_dtypes.float8_e4m3fn).view(np.uint8)
    else:
        c = by_word.astype(ml_dtypes.float4_e2m1fn).view(np.uint8) & 0xF
        words = (c[..., 0::2] | (c[..., 1::2] << 4)).reshape(k // 512, 128, 2 * n)
    return np.ascontiguousarray(words), np.ascontiguousarray(byte.astype(np.uint8).reshape(k // 512, 16, n))


def unpack_weight(words, scales, fmt):
    g, _, n = scales.shape
    words = np.ascontiguousarray(words).reshape(g, 128, n, -1)
    if fmt == "e4m3":
        vals = words.view(ml_dtypes.float8_e4m3fn).astype(np.float64)
    else:
        nib = np.empty((g, 128, n, 4), np.uint8)
        nib[..., 0::2] = words & 0xF
        nib[..., 1::2] = words >> 4
        vals = E2M1[nib]
    vals = vals * np.repeat(np.exp2(scales.astype(np.float64) - 127.0), 8, axis=1)[..., None]
    return vals.transpose(0, 1, 3, 2).reshape(g * 512, n)


def pack_table4(v):
    words, scales = pack_weight(v, "e2m1")
    g, t = words.shape[0] // 2, v.shape[1]
    return np.ascontiguousarray(words.reshape(g, 2, 128, t, 2).transpose(0, 2, 3, 1, 4).reshape(g, 128, t, 4)), scales


def unpack_table4(words, scales):
    g, _, t, _ = words.shape
    return unpack_weight(words.reshape(g, 128, t, 2, 2).transpose(0, 3, 1, 2, 4).reshape(2 * g, 128, 2 * t), scales, "e2m1")


def planes(y):
    n, m = y.shape
    v = y.astype(np.float32).astype(ml_dtypes.bfloat16).astype(np.float64).reshape(n // 32, 32, m)
    top = np.abs(v).max(1)
    byte = np.clip(np.where(top > 0, np.frexp(top)[1] - 1 + 127 - 7, 1), 1, 254)
    codes = (v * np.exp2(127.0 - byte)[:, None, :]).reshape(n, m).astype(np.float32).astype(ml_dtypes.float8_e4m3fn).view(np.uint8)
    words = codes.reshape(n // 512, 128, 4, m).transpose(0, 1, 3, 2)
    return np.ascontiguousarray(words), np.ascontiguousarray(byte.astype(np.uint8).reshape(n // 512, 16, m))


K, L, R, N, T, J = 512, 1024, 512, 512, 2048, 1024


def setup_inputs():
    n = np.random.standard_normal
    s = mx_kscale(K)[:, None]
    s2 = mx_kscale(L)[:, None]
    u = mx_kscale(R)[:, None]
    p_tab = pack_table4(n((L, T)) * s2)
    p_wa = pack_weight(n((K, R)) / np.sqrt(K) / s * u.T, "e2m1")
    p_wb = pack_weight(n((L, R)) / np.sqrt(L) / s2 * u.T, "e2m1")
    p_wd = pack_weight(n((R, N)) / np.sqrt(R) / u, "e2m1")
    return {
        "tab_words": p_tab[0],
        "tab_scales": p_tab[1],
        "xT": (n((K, T)) * s).astype(np.float32),
        "wgt2": np.repeat(np.random.uniform(0.5, 2.0, (8, J)), 16, axis=0).astype(np.float32),
        "wa_words": p_wa[0],
        "wa_scales": p_wa[1],
        "wb_words": p_wb[0],
        "wb_scales": p_wb[1],
        "wd_words": p_wd[0],
        "wd_scales": p_wd[1],
        "b": (0.3 * n(N)).astype(np.float32),
        "offs": striped(np.random.permutation(T)[:J]),
        "offs2": striped8(np.stack([np.random.permutation(T)[:J] for _ in range(8)])),
    }


def reference(tab_words, tab_scales, xT, wgt2, wa_words, wa_scales, wb_words, wb_scales, wd_words, wd_scales, b, offs, offs2):
    idx = unstriped(offs)
    idx2 = unstriped8(offs2)
    tab_ = unpack_table4(tab_words, tab_scales)[:, idx]
    rows = np.arange(K)
    xg = f64(wgt2)[rows // 4 % 128] * f64(xT)[rows[:, None], idx2[rows % 512 // 64]]
    xT_ = mxq(xg, 0, "e4m3")
    wa_ = unpack_weight(wa_words, wa_scales, "e2m1")
    wb_ = unpack_weight(wb_words, wb_scales, "e2m1")
    ya = wa_.T @ xT_
    yb = wb_.T @ tab_
    h = np.maximum(ya, yb)
    h_ = mxq(h, 0, "e4m3")
    wd_ = unpack_weight(wd_words, wd_scales, "e2m1")
    y = wd_.T @ h_
    out_0 = y + f64(b)[:, None]
    return (out_0,) + planes(out_0)

@@ -1,0 +1,236 @@
+from contextlib import ExitStack
+
+import concourse.mybir as mybir
+
+K, L, R, N, T, J = 512, 1024, 512, 512, 2048, 1024
+FLOPS = 2 * J * (K * R + L * R + R * N)
+
+F32 = mybir.dt.float32
+BF16 = mybir.dt.bfloat16
+I32 = mybir.dt.int32
+U32 = mybir.dt.uint32
+U16 = mybir.dt.uint16
+U8 = mybir.dt.uint8
+FP8X4 = mybir.dt.float8_e4m3fn_x4
+FP4X4 = mybir.dt.float4_e2m1fn_x4
+ALU = mybir.AluOpType
+IDENTITY = mybir.ActivationFunctionType.Identity
+
+P = 128
+PACK = 4
+QUADS = 4
+UNIT = 128
+UNITS = J // UNIT
+WIDE = 256
+HALF = 512
+
+
+def tile_list_htabg_max_biasP_kernel(
+    tc, tab_words, tab_scales, xT, wgt2, wa_words, wa_scales, wb_words, wb_scales,
+    wd_words, wd_scales, b, offs, offs2, out_0, out_1, out_2,
+):
+    nc = tc.nc
+    with ExitStack() as ctx:
+        keep = ctx.enter_context(tc.tile_pool(name="keep", bufs=1))
+        psum = ctx.enter_context(tc.psum_pool(name="psum", bufs=1))
+
+        def sb(name, shape, dtype):
+            return keep.tile(shape, dtype, name=name, align_bytes=64)
+
+        def cols(i, width):
+            return slice(i * width, (i + 1) * width)
+
+        def entries(i, width):
+            return slice(i * width // 16, (i + 1) * width // 16)
+
+        tab_list = keep.tile([P, J // 16], U16, name="tab_list")
+        head_lists = keep.tile([P, J // 16], U16, name="head_lists")
+
+        def slot(tag, name, shape, dtype):
+            return keep.tile(shape, dtype, name=name, tag=tag, align_bytes=64)
+
+        tab_sc = slot("slot_w", "tab_sc", [P, T], U8)
+        tab_w = sb("tab_w", [P, T], I32)
+        bias = sb("bias", [P, PACK], F32)
+        sc1 = [sb(f"sc1_{h}", [P, HALF], U8) for h in range(J // HALF)]
+        raw_sc = sb("raw_sc", [P, 2 * R], U8)
+        nc.vector.memset(tab_sc[:].bitcast(I32), 0)
+        nc.gpsimd.memset(raw_sc[:].bitcast(I32), 0)
+        for h in range(J // HALF):
+            nc.vector.memset(sc1[h][:].bitcast(I32), 0)
+
+        def load_words(t, words, passes):
+            nc.sync.dma_start(
+                out=t.bitcast(I32).rearrange("p (a c) -> p a c", a=passes),
+                in_=words.bitcast(I32).rearrange("a p c -> p a c"),
+            )
+
+        def load_scales(engine, t, scales, passes):
+            for q in range(QUADS):
+                engine.dma_start(
+                    out=t[32 * q : 32 * q + 4, :].bitcast(I32).rearrange("r (a c) -> r a c", a=passes),
+                    in_=scales[:, 4 * q : 4 * q + 4, :].bitcast(I32).rearrange("a r c -> r a c"),
+                )
+
+        x_planes = []
+
+        def load_plane(i):
+            plane = slot(f"slot_x{i}", f"x{i}", [P, T], F32)
+            nc.sync.dma_start(out=plane[:], in_=xT.rearrange("(p i) t -> p i t", i=PACK)[:, i, :])
+            x_planes.append(plane)
+
+        nc.sync.dma_start(tab_list[:], offs)
+        nc.sync.dma_start(head_lists[:], offs2)
+        nc.sync.dma_start(out=bias[:], in_=b.rearrange("(p t) -> p t", t=PACK))
+        wb_raw = slot("slot_x0", "wb_raw", [P, 2 * 2 * R], U8)
+        load_words(wb_raw[:], wb_words, 2)
+        nc.sync.dma_start(out=tab_w[:], in_=tab_words[0].rearrange("p t b -> p (t b)").bitcast(I32))
+        for q in range(QUADS):
+            nc.scalar.dma_start(
+                out=tab_sc[32 * q : 32 * q + 8, :].bitcast(I32),
+                in_=tab_scales[:, 4 * q : 4 * q + 4, :].bitcast(I32),
+            )
+        load_scales(nc.scalar, raw_sc, wb_scales, 2)
+
+        def deal(name, raw, passes, dtype):
+            dealt = sb(name, list(raw.shape), U8)
+            nc.vector.tensor_copy(
+                out=dealt[:].bitcast(dtype).rearrange("p (a t m) -> p a t m", a=passes, t=PACK),
+                in_=raw.bitcast(dtype).rearrange("p (a m t) -> p a t m", a=passes, t=PACK),
+            )
+            return dealt
+
+        def stationary(w, a, t):
+            words, scales = w
+            s = a * PACK + t
+            return dict(lhsT=words[:, cols(s, 2 * P)].bitcast(FP4X4), lhsT_scale=scales[:, cols(s, P)])
+
+        wb_dealt = deal("wb", wb_raw[:], 2, U16)
+        load_plane(0)
+        sc0 = []
+        for h in range(J // HALF):
+            g = sb(f"sc0_{h}", [P, HALF], U8)
+            nc.vector.tensor_copy(out=g[:], in_=tab_sc[:].indirect(tab_list[:, entries(h, HALF)]))
+            nc.scalar.dma_start(out=sc1[h][0:112, :].bitcast(I32), in_=g[4:116, :].bitcast(I32))
+            sc0.append(g)
+        wgt = slot("slot_w", "wgt", [P, J], F32)
+        nc.sync.dma_start(out=wgt[:], in_=wgt2)
+        wb = (wb_dealt, deal("wb_sc", raw_sc[:], 2, U8))
+
+        yb = []
+        for c in range(J // WIDE):
+            picked = slot(f"slot_x{c + 1}", f"picked{c}", [P, WIDE], U32)
+            nc.vector.tensor_copy(out=picked[:], in_=tab_w[:].bitcast(U32).indirect(tab_list[:, entries(c, WIDE)]))
+            parted = sb(f"parted{c}", [P, 2 * 2 * WIDE], U8)
+            nc.vector.tensor_copy(
+                out=parted[:].bitcast(U16).rearrange("p (d j) -> p d j", d=2),
+                in_=picked[:].bitcast(U16).rearrange("p (j d) -> p d j", d=2),
+            )
+            if c + 1 < PACK:
+                load_plane(c + 1)
+            if c == 0:
+                load_scales(nc.sync, raw_sc[:, 0:R], wa_scales, 1)
+            if c == 1:
+                load_scales(nc.sync, raw_sc[:, R : 2 * R], wd_scales, 1)
+            for s in range(WIDE // UNIT):
+                u = c * (WIDE // UNIT) + s
+                h, hu = divmod(u, HALF // UNIT)
+                bank = psum.tile([P, PACK, UNIT], F32, name="yb_bank", bufs=3)
+                for t in range(PACK):
+                    for a in range(2):
+                        nc.tensor.matmul_mx(
+                            out=bank[:, t, :],
+                            rhs=parted[:, cols(a * (WIDE // UNIT) + s, 2 * UNIT)].bitcast(FP4X4),
+                            rhs_scale=(sc0, sc1)[a][h][:, cols(hu, UNIT)],
+                            start=(a == 0), stop=(a == 1),
+                            **stationary(wb, a, t),
+                        )
+                staged = sb(f"yb{u}", [P, UNIT, PACK], F32)
+                nc.scalar.activation(out=staged[:], in_=bank[:].rearrange("p t j -> p j t"), func=IDENTITY)
+                yb.append(staged)
+
+        ad_raw = slot("slot_x4", "ad_raw", [P, 2 * 2 * R], U8)
+        load_words(ad_raw[:, 0 : 2 * R], wa_words, 1)
+        load_words(ad_raw[:, 2 * R : 4 * R], wd_words, 1)
+
+        x_il = [sb(f"x_il{u}", [P, UNIT, PACK], BF16) for u in range(UNITS)]
+
+        def gather_pair(name, first, c, width):
+            g = sb(name, [P, 2, width], F32)
+            for e in range(2):
+                nc.vector.tensor_tensor(
+                    g[:, e, :], x_planes[first + e][:].indirect(head_lists[:, entries(c, width)]),
+                    wgt[:, cols(c, width)], ALU.mult,
+                )
+            return g
+
+        def weave_pair(u, first, g):
+            nc.scalar.copy(out=x_il[u][:, :, first : first + 2], in_=g.rearrange("p e j -> p j e"))
+
+        for c in range(J // WIDE):
+            g = gather_pair(f"g01_{c}", 0, c, WIDE)
+            for s in range(WIDE // UNIT):
+                weave_pair(c * (WIDE // UNIT) + s, 0, g[:, :, cols(s, UNIT)])
+
+        wa = (deal("wa", ad_raw[:, 0 : 2 * R], 1, U16), deal("wa_sc", raw_sc[:, 0:R], 1, U8))
+        wd = (deal("wd", ad_raw[:, 2 * R : 4 * R], 1, U16), deal("wd_sc", raw_sc[:, R : 2 * R], 1, U8))
+
+        def quantise(name, src):
+            codes = sb(name, [P, UNIT], U32)
+            scales = sb(name + "_sc", [P, UNIT], U8)
+            nc.vector.quantize_mx(out=codes[:].bitcast(FP8X4), scales=scales[:], in_=src[:].rearrange("p j t -> p (j t)"))
+            return codes, scales
+
+        def project(bank, w, q):
+            for t in range(PACK):
+                nc.tensor.matmul_mx(
+                    out=bank[:, t, :], rhs=q[0][:].bitcast(FP8X4), rhs_scale=q[1][:],
+                    start=True, stop=True, **stationary(w, 0, t),
+                )
+
+        y_codes = sb("y_codes", [P, J], I32)
+        y_scales = sb("y_scales", [P, J], U8)
+        y_rows = out_0.rearrange("(p t) j -> p t j", t=PACK)
+        code_rows = out_1[0].rearrange("p j i -> p (j i)").bitcast(I32)
+        ya, h_il, y_il = {}, {}, {}
+
+        def stage_pick(u):
+            weave_pair(u, 2, gather_pair(f"g23_{u}", 2, u, UNIT)[:])
+
+        def stage_ya(u):
+            ya[u] = psum.tile([P, PACK, UNIT], F32, name="ya_bank", bufs=2)
+            project(ya[u], wa, quantise(f"xq{u}", x_il[u]))
+
+        def stage_max(u):
+            h_il[u] = sb(f"h_il{u}", [P, UNIT, PACK], BF16)
+            nc.vector.tensor_tensor(h_il[u][:], ya[u][:].rearrange("p t j -> p j t"), yb[u][:], ALU.max)
+
+        def stage_y(u):
+            bank = psum.tile([P, PACK, UNIT], F32, name="y_bank", bufs=3)
+            project(bank, wd, quantise(f"hq{u}", h_il[u]))
+            y = sb(f"y{u}", [P, PACK, UNIT], F32)
+            for t in range(PACK):
+                nc.scalar.activation(out=y[:, t, :], in_=bank[:, t, :], func=IDENTITY, bias=bias[:, t : t + 1])
+            nc.sync.dma_start(out=y_rows[:, :, cols(u, UNIT)], in_=y[:])
+            y_il[u] = sb(f"y_il{u}", [P, UNIT, PACK], BF16)
+            nc.scalar.copy(out=y_il[u][:], in_=y[:].rearrange("p t j -> p j t"))
+
+        def stage_planes(u):
+            nc.vector.quantize_mx(
+                out=y_codes[:, cols(u, UNIT)].bitcast(FP8X4), scales=y_scales[:, cols(u, UNIT)],
+                in_=y_il[u][:].rearrange("p j t -> p (j t)"),
+            )
+            if u % 2 == 1:
+                nc.sync.dma_start(out=code_rows[:, cols(u // 2, 2 * UNIT)], in_=y_codes[:, cols(u // 2, 2 * UNIT)])
+
+        stages = (stage_pick, stage_ya, stage_max, stage_y, stage_planes)
+        for step in range(UNITS + len(stages) - 1):
+            for lag, stage in enumerate(stages):
+                if 0 <= step - lag < UNITS:
+                    stage(step - lag)
+
+        for q in range(QUADS):
+            nc.sync.dma_start(
+                out=out_2[0, 4 * q : 4 * q + 4, :].bitcast(I32),
+                in_=y_scales[32 * q : 32 * q + 4, :].bitcast(I32),
+            )

@@ -23,6 +23,7 @@ UNIT = 128
 UNITS = J // UNIT
 WIDE = 256
 HALF = 512
+WIDTHS = (128, 256, 256, 256, 128)
 
 
 def tile_list_htabg_max_biasP_kernel(
@@ -49,15 +50,14 @@ def tile_list_htabg_max_biasP_kernel(
         def slot(tag, name, shape, dtype):
             return keep.tile(shape, dtype, name=name, tag=tag, align_bytes=64)
 
-        tab_sc = slot("slot_w", "tab_sc", [P, T], U8)
+        def zeroed(engine, t):
+            engine.memset(t[:].bitcast(I32), 0)
+            return t
+
+        tab_sc = zeroed(nc.vector, slot("slot_x1", "tab_sc", [P, T], U8))
         tab_w = sb("tab_w", [P, T], I32)
-        bias = sb("bias", [P, PACK], F32)
-        sc1 = [sb(f"sc1_{h}", [P, HALF], U8) for h in range(J // HALF)]
-        raw_sc = sb("raw_sc", [P, 2 * R], U8)
-        nc.vector.memset(tab_sc[:].bitcast(I32), 0)
-        nc.gpsimd.memset(raw_sc[:].bitcast(I32), 0)
-        for h in range(J // HALF):
-            nc.vector.memset(sc1[h][:].bitcast(I32), 0)
+        wb_sc_raw = zeroed(nc.gpsimd, sb("wb_sc_raw", [P, 2 * R], U8))
+        sc1 = [zeroed(nc.vector, sb(f"sc1_{h}", [P, HALF], U8)) for h in range(J // HALF)]
 
         def load_words(t, words, passes):
             nc.sync.dma_start(
@@ -65,12 +65,16 @@ def tile_list_htabg_max_biasP_kernel(
                 in_=words.bitcast(I32).rearrange("a p c -> p a c"),
             )
 
-        def load_scales(engine, t, scales, passes):
+        def load_scales(engine, t, scales, first):
+            rows = 4 * scales.shape[0]
             for q in range(QUADS):
                 engine.dma_start(
-                    out=t[32 * q : 32 * q + 4, :].bitcast(I32).rearrange("r (a c) -> r a c", a=passes),
-                    in_=scales[:, 4 * q : 4 * q + 4, :].bitcast(I32).rearrange("a r c -> r a c"),
+                    out=t[32 * q + first : 32 * q + first + rows, :].bitcast(I32),
+                    in_=scales[:, 4 * q : 4 * q + 4, :].bitcast(I32),
                 )
+
+        def lower(dst, src):
+            nc.scalar.dma_start(out=dst[0:112, :].bitcast(I32), in_=src[4:116, :].bitcast(I32))
 
         x_planes = []
 
@@ -81,16 +85,23 @@ def tile_list_htabg_max_biasP_kernel(
 
         nc.sync.dma_start(tab_list[:], offs)
         nc.sync.dma_start(head_lists[:], offs2)
-        nc.sync.dma_start(out=bias[:], in_=b.rearrange("(p t) -> p t", t=PACK))
-        wb_raw = slot("slot_x0", "wb_raw", [P, 2 * 2 * R], U8)
+        wb_raw = sb("wb_raw", [P, 2 * 2 * R], U8)
         load_words(wb_raw[:], wb_words, 2)
+        load_scales(nc.sync, tab_sc, tab_scales, 0)
         nc.sync.dma_start(out=tab_w[:], in_=tab_words[0].rearrange("p t b -> p (t b)").bitcast(I32))
         for q in range(QUADS):
-            nc.scalar.dma_start(
-                out=tab_sc[32 * q : 32 * q + 8, :].bitcast(I32),
-                in_=tab_scales[:, 4 * q : 4 * q + 4, :].bitcast(I32),
+            nc.sync.dma_start(
+                out=wb_sc_raw[32 * q : 32 * q + 4, :].bitcast(I32).rearrange("r (a c) -> r a c", a=2),
+                in_=wb_scales[:, 4 * q : 4 * q + 4, :].bitcast(I32).rearrange("a r c -> r a c"),
             )
-        load_scales(nc.scalar, raw_sc, wb_scales, 2)
+        load_plane(0)
+        wgt = sb("wgt", [P, J], F32)
+        nc.sync.dma_start(out=wgt[:], in_=wgt2)
+        ad_raw = sb("ad_raw", [P, 2 * 2 * R], U8)
+        load_words(ad_raw[:, 0 : 2 * R], wa_words, 1)
+        load_words(ad_raw[:, 2 * R : 4 * R], wd_words, 1)
+        bias = sb("bias", [P, PACK], F32)
+        nc.sync.dma_start(out=bias[:], in_=b.rearrange("(p t) -> p t", t=PACK))
 
         def deal(name, raw, passes, dtype):
             dealt = sb(name, list(raw.shape), U8)
@@ -100,42 +111,35 @@ def tile_list_htabg_max_biasP_kernel(
             )
             return dealt
 
-        def stationary(w, a, t):
-            words, scales = w
-            s = a * PACK + t
-            return dict(lhsT=words[:, cols(s, 2 * P)].bitcast(FP4X4), lhsT_scale=scales[:, cols(s, P)])
+        def stationary(words, scales, t):
+            return dict(lhsT=words[:, cols(t, 2 * P)].bitcast(FP4X4), lhsT_scale=scales[:, cols(t, P)])
 
-        wb_dealt = deal("wb", wb_raw[:], 2, U16)
-        load_plane(0)
+        wb = deal("wb", wb_raw[:], 2, U16)
         sc0 = []
         for h in range(J // HALF):
             g = sb(f"sc0_{h}", [P, HALF], U8)
             nc.vector.tensor_copy(out=g[:], in_=tab_sc[:].indirect(tab_list[:, entries(h, HALF)]))
-            nc.scalar.dma_start(out=sc1[h][0:112, :].bitcast(I32), in_=g[4:116, :].bitcast(I32))
+            lower(sc1[h], g)
             sc0.append(g)
-        wgt = slot("slot_w", "wgt", [P, J], F32)
-        nc.sync.dma_start(out=wgt[:], in_=wgt2)
-        wb = (wb_dealt, deal("wb_sc", raw_sc[:], 2, U8))
+        load_plane(1)
+        wb_sc = deal("wb_sc", wb_sc_raw[:], 2, U8)
+        load_scales(nc.sync, wb_sc_raw[:, 0:R], wa_scales, 0)
 
         yb = []
         for c in range(J // WIDE):
-            picked = slot(f"slot_x{c + 1}", f"picked{c}", [P, WIDE], U32)
+            picked = slot(f"slot_x{c + 2}", f"picked{c}", [P, WIDE], U32)
             nc.vector.tensor_copy(out=picked[:], in_=tab_w[:].bitcast(U32).indirect(tab_list[:, entries(c, WIDE)]))
             parted = sb(f"parted{c}", [P, 2 * 2 * WIDE], U8)
             nc.vector.tensor_copy(
                 out=parted[:].bitcast(U16).rearrange("p (d j) -> p d j", d=2),
                 in_=picked[:].bitcast(U16).rearrange("p (j d) -> p d j", d=2),
             )
-            if c + 1 < PACK:
-                load_plane(c + 1)
-            if c == 0:
-                load_scales(nc.sync, raw_sc[:, 0:R], wa_scales, 1)
-            if c == 1:
-                load_scales(nc.sync, raw_sc[:, R : 2 * R], wd_scales, 1)
+            if c + 2 < PACK:
+                load_plane(c + 2)
             for s in range(WIDE // UNIT):
                 u = c * (WIDE // UNIT) + s
                 h, hu = divmod(u, HALF // UNIT)
-                bank = psum.tile([P, PACK, UNIT], F32, name="yb_bank", bufs=3)
+                bank = psum.tile([P, PACK, UNIT], F32, name="yb_bank", bufs=2)
                 for t in range(PACK):
                     for a in range(2):
                         nc.tensor.matmul_mx(
@@ -143,50 +147,46 @@ def tile_list_htabg_max_biasP_kernel(
                             rhs=parted[:, cols(a * (WIDE // UNIT) + s, 2 * UNIT)].bitcast(FP4X4),
                             rhs_scale=(sc0, sc1)[a][h][:, cols(hu, UNIT)],
                             start=(a == 0), stop=(a == 1),
-                            **stationary(wb, a, t),
+                            **stationary(wb[:, cols(a, 2 * R)], wb_sc[:, cols(a, R)], t),
                         )
                 staged = sb(f"yb{u}", [P, UNIT, PACK], F32)
                 nc.scalar.activation(out=staged[:], in_=bank[:].rearrange("p t j -> p j t"), func=IDENTITY)
                 yb.append(staged)
 
-        ad_raw = slot("slot_x4", "ad_raw", [P, 2 * 2 * R], U8)
-        load_words(ad_raw[:, 0 : 2 * R], wa_words, 1)
-        load_words(ad_raw[:, 2 * R : 4 * R], wd_words, 1)
+        starts = [sum(WIDTHS[:u]) for u in range(len(WIDTHS))]
+        spans = [slice(s, s + w) for s, w in zip(starts, WIDTHS)]
+        x_il = [sb(f"x_il{u}", [P, w, PACK], BF16) for u, w in enumerate(WIDTHS)]
 
-        x_il = [sb(f"x_il{u}", [P, UNIT, PACK], BF16) for u in range(UNITS)]
-
-        def gather_pair(name, first, c, width):
-            g = sb(name, [P, 2, width], F32)
+        def pick_pair(u, first):
+            g = sb(f"g{first}_{u}", [P, 2, WIDTHS[u]], F32)
+            listed = head_lists[:, spans[u].start // 16 : spans[u].stop // 16]
             for e in range(2):
-                nc.vector.tensor_tensor(
-                    g[:, e, :], x_planes[first + e][:].indirect(head_lists[:, entries(c, width)]),
-                    wgt[:, cols(c, width)], ALU.mult,
-                )
-            return g
+                nc.vector.tensor_tensor(g[:, e, :], x_planes[first + e][:].indirect(listed), wgt[:, spans[u]], ALU.mult)
+            nc.scalar.copy(out=x_il[u][:, :, first : first + 2], in_=g[:].rearrange("p e j -> p j e"))
 
-        def weave_pair(u, first, g):
-            nc.scalar.copy(out=x_il[u][:, :, first : first + 2], in_=g.rearrange("p e j -> p j e"))
+        ad = deal("ad", ad_raw[:], 2, U16)
+        wa_sc = deal("wa_sc", wb_sc_raw[:, 0:R], 1, U8)
+        load_scales(nc.sync, wb_sc_raw[:, 0:R], wd_scales, 0)
+        for u in range(len(WIDTHS)):
+            pick_pair(u, 0)
+        wd_sc = deal("wd_sc", wb_sc_raw[:, 0:R], 1, U8)
+        wa = (ad[:, cols(0, 2 * R)], wa_sc)
+        wd = (ad[:, cols(1, 2 * R)], wd_sc)
 
-        for c in range(J // WIDE):
-            g = gather_pair(f"g01_{c}", 0, c, WIDE)
-            for s in range(WIDE // UNIT):
-                weave_pair(c * (WIDE // UNIT) + s, 0, g[:, :, cols(s, UNIT)])
-
-        wa = (deal("wa", ad_raw[:, 0 : 2 * R], 1, U16), deal("wa_sc", raw_sc[:, 0:R], 1, U8))
-        wd = (deal("wd", ad_raw[:, 2 * R : 4 * R], 1, U16), deal("wd_sc", raw_sc[:, R : 2 * R], 1, U8))
-
-        def quantise(name, src):
-            codes = sb(name, [P, UNIT], U32)
-            scales = sb(name + "_sc", [P, UNIT], U8)
+        def quantise(name, src, width):
+            codes = sb(name, [P, width], U32)
+            scales = sb(name + "_sc", [P, width], U8)
             nc.vector.quantize_mx(out=codes[:].bitcast(FP8X4), scales=scales[:], in_=src[:].rearrange("p j t -> p (j t)"))
             return codes, scales
 
-        def project(bank, w, q):
+        def project(name, bufs, w, q, s):
+            bank = psum.tile([P, PACK, UNIT], F32, name=name, bufs=bufs)
             for t in range(PACK):
                 nc.tensor.matmul_mx(
-                    out=bank[:, t, :], rhs=q[0][:].bitcast(FP8X4), rhs_scale=q[1][:],
-                    start=True, stop=True, **stationary(w, 0, t),
+                    out=bank[:, t, :], rhs=q[0][:, cols(s, UNIT)].bitcast(FP8X4), rhs_scale=q[1][:, cols(s, UNIT)],
+                    start=True, stop=True, **stationary(*w, t),
                 )
+            return bank
 
         y_codes = sb("y_codes", [P, J], I32)
         y_scales = sb("y_scales", [P, J], U8)
@@ -195,42 +195,58 @@ def tile_list_htabg_max_biasP_kernel(
         ya, h_il, y_il = {}, {}, {}
 
         def stage_pick(u):
-            weave_pair(u, 2, gather_pair(f"g23_{u}", 2, u, UNIT)[:])
+            pick_pair(u, 2)
 
         def stage_ya(u):
-            ya[u] = psum.tile([P, PACK, UNIT], F32, name="ya_bank", bufs=2)
-            project(ya[u], wa, quantise(f"xq{u}", x_il[u]))
+            q = quantise(f"xq{u}", x_il[u], WIDTHS[u])
+            ya[u] = [project("ya_bank", 3, wa, q, s) for s in range(WIDTHS[u] // UNIT)]
 
         def stage_max(u):
-            h_il[u] = sb(f"h_il{u}", [P, UNIT, PACK], BF16)
-            nc.vector.tensor_tensor(h_il[u][:], ya[u][:].rearrange("p t j -> p j t"), yb[u][:], ALU.max)
+            h_il[u] = sb(f"h_il{u}", [P, WIDTHS[u], PACK], BF16)
+            for s, bank in enumerate(ya[u]):
+                nc.vector.tensor_tensor(
+                    h_il[u][:, cols(s, UNIT), :], bank[:].rearrange("p t j -> p j t"), yb[starts[u] // UNIT + s][:], ALU.max
+                )
 
         def stage_y(u):
-            bank = psum.tile([P, PACK, UNIT], F32, name="y_bank", bufs=3)
-            project(bank, wd, quantise(f"hq{u}", h_il[u]))
-            y = sb(f"y{u}", [P, PACK, UNIT], F32)
-            for t in range(PACK):
-                nc.scalar.activation(out=y[:, t, :], in_=bank[:, t, :], func=IDENTITY, bias=bias[:, t : t + 1])
-            nc.sync.dma_start(out=y_rows[:, :, cols(u, UNIT)], in_=y[:])
-            y_il[u] = sb(f"y_il{u}", [P, UNIT, PACK], BF16)
-            nc.scalar.copy(out=y_il[u][:], in_=y[:].rearrange("p t j -> p j t"))
+            q = quantise(f"hq{u}", h_il[u], WIDTHS[u])
+            y = sb(f"y{u}", [P, PACK, WIDTHS[u]], F32)
+            width = WIDTHS[u]
+            per_bank = 512 // width
+            for k in range(PACK // per_bank):
+                bank = psum.tile([P, per_bank, width], F32, name="y_bank", bufs=3)
+                for e in range(per_bank):
+                    nc.tensor.matmul_mx(
+                        out=bank[:, e, :], rhs=q[0][:].bitcast(FP8X4), rhs_scale=q[1][:],
+                        start=True, stop=True, **stationary(*wd, k * per_bank + e),
+                    )
+                for e in range(per_bank):
+                    t = k * per_bank + e
+                    nc.scalar.activation(out=y[:, t, :], in_=bank[:, e, :], func=IDENTITY, bias=bias[:, t : t + 1])
+            nc.sync.dma_start(out=y_rows[:, :, spans[u]], in_=y[:])
+            y_il[u] = sb(f"y_il{u}", [P, width, PACK], BF16)
+            dst = y_il[u][:].rearrange("p (c i) t -> p c t i", i=PACK)
+            src = y[:].rearrange("p t (c i) -> p c t i", i=PACK)
+            if u == len(WIDTHS) - 1:
+                nc.vector.tensor_copy(out=dst, in_=src)
+            else:
+                nc.scalar.copy(out=dst, in_=src)
 
         def stage_planes(u):
             nc.vector.quantize_mx(
-                out=y_codes[:, cols(u, UNIT)].bitcast(FP8X4), scales=y_scales[:, cols(u, UNIT)],
+                out=y_codes[:, spans[u]].bitcast(FP8X4), scales=y_scales[:, spans[u]],
                 in_=y_il[u][:].rearrange("p j t -> p (j t)"),
             )
-            if u % 2 == 1:
-                nc.sync.dma_start(out=code_rows[:, cols(u // 2, 2 * UNIT)], in_=y_codes[:, cols(u // 2, 2 * UNIT)])
+            nc.sync.dma_start(out=code_rows[:, spans[u]], in_=y_codes[:, spans[u]])
 
         stages = (stage_pick, stage_ya, stage_max, stage_y, stage_planes)
-        for step in range(UNITS + len(stages) - 1):
+        for step in range(len(WIDTHS) + len(stages) - 1):
             for lag, stage in enumerate(stages):
-                if 0 <= step - lag < UNITS:
+                if 0 <= step - lag < len(WIDTHS):
                     stage(step - lag)
 
         for q in range(QUADS):
-            nc.sync.dma_start(
+            (nc.sync, nc.scalar)[q % 2].dma_start(
                 out=out_2[0, 4 * q : 4 * q + 4, :].bitcast(I32),
                 in_=y_scales[32 * q : 32 * q + 4, :].bitcast(I32),
             )

@@ -23,6 +23,8 @@ UNIT = 128
 UNITS = J // UNIT
 WIDE = 256
 HALF = 512
+AHEAD = 3
+STAGED = 2
 WIDTHS = (128, 256, 256, 256, 128)
 
 
@@ -56,8 +58,8 @@ def tile_list_htabg_max_biasP_kernel(
 
         tab_sc = zeroed(nc.vector, slot("slot_x1", "tab_sc", [P, T], U8))
         tab_w = sb("tab_w", [P, T], I32)
-        wb_sc_raw = zeroed(nc.gpsimd, sb("wb_sc_raw", [P, 2 * R], U8))
-        sc1 = [zeroed(nc.vector, sb(f"sc1_{h}", [P, HALF], U8)) for h in range(J // HALF)]
+        wb_sc_raw = zeroed(nc.gpsimd, slot("slot_bias", "wb_sc_raw", [P, 2 * R], U8))
+        sc1 = [zeroed(nc.gpsimd, sb(f"sc1_{h}", [P, HALF], U8)) for h in range(J // HALF)]
 
         def load_words(t, words, passes):
             nc.sync.dma_start(
@@ -72,6 +74,13 @@ def tile_list_htabg_max_biasP_kernel(
                     out=t[32 * q + first : 32 * q + first + rows, :].bitcast(I32),
                     in_=scales[:, 4 * q : 4 * q + 4, :].bitcast(I32),
                 )
+
+        def load_weight(name, words, scales):
+            raw = slot("slot_" + name, name + "_raw", [P, 3 * R], U8)
+            zeroed(nc.vector, raw[:, 2 * R : 3 * R])
+            load_words(raw[:, 0 : 2 * R], words, 1)
+            load_scales(nc.sync, raw[:, 2 * R : 3 * R], scales, 0)
+            return raw
 
         def lower(dst, src):
             nc.scalar.dma_start(out=dst[0:112, :].bitcast(I32), in_=src[4:116, :].bitcast(I32))
@@ -97,24 +106,21 @@ def tile_list_htabg_max_biasP_kernel(
         load_plane(0)
         wgt = sb("wgt", [P, J], F32)
         nc.sync.dma_start(out=wgt[:], in_=wgt2)
-        ad_raw = sb("ad_raw", [P, 2 * 2 * R], U8)
-        load_words(ad_raw[:, 0 : 2 * R], wa_words, 1)
-        load_words(ad_raw[:, 2 * R : 4 * R], wd_words, 1)
-        bias = sb("bias", [P, PACK], F32)
-        nc.sync.dma_start(out=bias[:], in_=b.rearrange("(p t) -> p t", t=PACK))
 
-        def deal(name, raw, passes, dtype):
-            dealt = sb(name, list(raw.shape), U8)
+        def deal(dealt, raw, passes, dtype):
             nc.vector.tensor_copy(
                 out=dealt[:].bitcast(dtype).rearrange("p (a t m) -> p a t m", a=passes, t=PACK),
                 in_=raw.bitcast(dtype).rearrange("p (a m t) -> p a t m", a=passes, t=PACK),
             )
             return dealt
 
+        def deal_weight(dealt, raw):
+            return deal(dealt[:, 0 : 2 * R], raw[:, 0 : 2 * R], 1, U16), deal(dealt[:, 2 * R : 3 * R], raw[:, 2 * R : 3 * R], 1, U8)
+
         def stationary(words, scales, t):
             return dict(lhsT=words[:, cols(t, 2 * P)].bitcast(FP4X4), lhsT_scale=scales[:, cols(t, P)])
 
-        wb = deal("wb", wb_raw[:], 2, U16)
+        wb = deal(sb("wb", [P, 4 * R], U8), wb_raw[:], 2, U16)
         sc0 = []
         for h in range(J // HALF):
             g = sb(f"sc0_{h}", [P, HALF], U8)
@@ -122,24 +128,31 @@ def tile_list_htabg_max_biasP_kernel(
             lower(sc1[h], g)
             sc0.append(g)
         load_plane(1)
-        wb_sc = deal("wb_sc", wb_sc_raw[:], 2, U8)
-        load_scales(nc.sync, wb_sc_raw[:, 0:R], wa_scales, 0)
+        wb_sc = deal(sb("wb_sc", [P, 2 * R], U8), wb_sc_raw[:], 2, U8)
+        bias = slot("slot_bias", "bias", [P, PACK], F32)
+        nc.sync.dma_start(out=bias[:], in_=b.rearrange("(p t) -> p t", t=PACK))
 
-        yb = []
+        yb = sb("yb", [P, J, PACK], BF16)
         for c in range(J // WIDE):
-            picked = slot(f"slot_x{c + 2}", f"picked{c}", [P, WIDE], U32)
+            picked = slot(("slot_x2", "slot_wa", "slot_x3", "slot_wd")[c], f"picked{c}", [P, WIDE], U32)
             nc.vector.tensor_copy(out=picked[:], in_=tab_w[:].bitcast(U32).indirect(tab_list[:, entries(c, WIDE)]))
-            parted = sb(f"parted{c}", [P, 2 * 2 * WIDE], U8)
+            parted = slot(f"parted{c}", f"parted{c}", [P, 2 * 2 * WIDE], U8)
             nc.vector.tensor_copy(
                 out=parted[:].bitcast(U16).rearrange("p (d j) -> p d j", d=2),
                 in_=picked[:].bitcast(U16).rearrange("p (j d) -> p d j", d=2),
             )
-            if c + 2 < PACK:
-                load_plane(c + 2)
+            if c == 0:
+                load_plane(2)
+            if c == 1:
+                wa_raw = load_weight("wa", wa_words, wa_scales)
+            if c == 2:
+                load_plane(3)
+            if c == 3:
+                wd_raw = load_weight("wd", wd_words, wd_scales)
             for s in range(WIDE // UNIT):
                 u = c * (WIDE // UNIT) + s
                 h, hu = divmod(u, HALF // UNIT)
-                bank = psum.tile([P, PACK, UNIT], F32, name="yb_bank", bufs=2)
+                bank = psum.tile([P, PACK, UNIT], F32, name="yb_bank", tag="y_bank", bufs=5)
                 for t in range(PACK):
                     for a in range(2):
                         nc.tensor.matmul_mx(
@@ -149,29 +162,21 @@ def tile_list_htabg_max_biasP_kernel(
                             start=(a == 0), stop=(a == 1),
                             **stationary(wb[:, cols(a, 2 * R)], wb_sc[:, cols(a, R)], t),
                         )
-                staged = sb(f"yb{u}", [P, UNIT, PACK], F32)
-                nc.scalar.activation(out=staged[:], in_=bank[:].rearrange("p t j -> p j t"), func=IDENTITY)
-                yb.append(staged)
+                nc.scalar.activation(out=yb[:, cols(u, UNIT), :], in_=bank[:].rearrange("p t j -> p j t"), func=IDENTITY)
 
         starts = [sum(WIDTHS[:u]) for u in range(len(WIDTHS))]
         spans = [slice(s, s + w) for s, w in zip(starts, WIDTHS)]
-        x_il = [sb(f"x_il{u}", [P, w, PACK], BF16) for u, w in enumerate(WIDTHS)]
+        x_il = [slot(f"x_il{u}", f"x_il{u}", [P, w, PACK], BF16) for u, w in enumerate(WIDTHS)]
 
-        def pick_pair(u, first):
-            g = sb(f"g{first}_{u}", [P, 2, WIDTHS[u]], F32)
+        def stage_pick(u):
+            g = keep.tile([P, PACK, WIDTHS[u]], F32, name=f"g{u}", tag="picks", bufs=AHEAD, align_bytes=64)
             listed = head_lists[:, spans[u].start // 16 : spans[u].stop // 16]
-            for e in range(2):
-                nc.vector.tensor_tensor(g[:, e, :], x_planes[first + e][:].indirect(listed), wgt[:, spans[u]], ALU.mult)
-            nc.scalar.copy(out=x_il[u][:, :, first : first + 2], in_=g[:].rearrange("p e j -> p j e"))
-
-        ad = deal("ad", ad_raw[:], 2, U16)
-        wa_sc = deal("wa_sc", wb_sc_raw[:, 0:R], 1, U8)
-        load_scales(nc.sync, wb_sc_raw[:, 0:R], wd_scales, 0)
-        for u in range(len(WIDTHS)):
-            pick_pair(u, 0)
-        wd_sc = deal("wd_sc", wb_sc_raw[:, 0:R], 1, U8)
-        wa = (ad[:, cols(0, 2 * R)], wa_sc)
-        wd = (ad[:, cols(1, 2 * R)], wd_sc)
+            for i in range(PACK):
+                nc.vector.tensor_tensor(g[:, i, :], x_planes[i][:].indirect(listed), wgt[:, spans[u]], ALU.mult)
+            nc.scalar.copy(
+                out=x_il[u][:].rearrange("p (c i) t -> p c t i", i=PACK),
+                in_=g[:].rearrange("p t (c i) -> p c t i", i=PACK),
+            )
 
         def quantise(name, src, width):
             codes = sb(name, [P, width], U32)
@@ -194,19 +199,23 @@ def tile_list_htabg_max_biasP_kernel(
         code_rows = out_1[0].rearrange("p j i -> p (j i)").bitcast(I32)
         ya, h_il, y_il = {}, {}, {}
 
-        def stage_pick(u):
-            pick_pair(u, 2)
-
         def stage_ya(u):
             q = quantise(f"xq{u}", x_il[u], WIDTHS[u])
             ya[u] = [project("ya_bank", 3, wa, q, s) for s in range(WIDTHS[u] // UNIT)]
 
         def stage_max(u):
             h_il[u] = sb(f"h_il{u}", [P, WIDTHS[u], PACK], BF16)
-            for s, bank in enumerate(ya[u]):
-                nc.vector.tensor_tensor(
-                    h_il[u][:, cols(s, UNIT), :], bank[:].rearrange("p t j -> p j t"), yb[starts[u] // UNIT + s][:], ALU.max
-                )
+            if u < STAGED:
+                staged = sb(f"ya{u}", [P, WIDTHS[u], PACK], BF16)
+                for s, bank in enumerate(ya[u]):
+                    nc.scalar.copy(out=staged[:, cols(s, UNIT), :], in_=bank[:].rearrange("p t j -> p j t"))
+                nc.vector.tensor_tensor(h_il[u][:], staged[:], yb[:, spans[u], :], ALU.max)
+            else:
+                for s, bank in enumerate(ya[u]):
+                    nc.vector.tensor_tensor(
+                        h_il[u][:, cols(s, UNIT), :], bank[:].rearrange("p t j -> p j t"),
+                        yb[:, cols(starts[u] // UNIT + s, UNIT), :], ALU.max,
+                    )
 
         def stage_y(u):
             q = quantise(f"hq{u}", h_il[u], WIDTHS[u])
@@ -214,7 +223,7 @@ def tile_list_htabg_max_biasP_kernel(
             width = WIDTHS[u]
             per_bank = 512 // width
             for k in range(PACK // per_bank):
-                bank = psum.tile([P, per_bank, width], F32, name="y_bank", bufs=3)
+                bank = psum.tile([P, per_bank, width], F32, name="y_bank", tag="y_bank", bufs=5)
                 for e in range(per_bank):
                     nc.tensor.matmul_mx(
                         out=bank[:, e, :], rhs=q[0][:].bitcast(FP8X4), rhs_scale=q[1][:],
@@ -241,6 +250,10 @@ def tile_list_htabg_max_biasP_kernel(
 
         stages = (stage_pick, stage_ya, stage_max, stage_y, stage_planes)
         for step in range(len(WIDTHS) + len(stages) - 1):
+            if step == 1:
+                wa = deal_weight(slot("parted3", "wa", [P, 3 * R], U8), wa_raw)
+            if step == 2:
+                wd = deal_weight(slot("x_il0", "wd", [P, 3 * R], U8), wd_raw)
             for lag, stage in enumerate(stages):
                 if 0 <= step - lag < len(WIDTHS):
                     stage(step - lag)

@@ -21,11 +21,12 @@ PACK = 4
 QUADS = 4
 UNIT = 128
 UNITS = J // UNIT
-WIDE = 256
+WIDE = 512
 HALF = 512
 AHEAD = 3
 STAGED = 2
-WIDTHS = (128, 256, 256, 256, 128)
+WOVEN_BY_SCALAR = 2
+WIDTHS = (256, 256, 256, 128, 128)
 
 
 def tile_list_htabg_max_biasP_kernel(
@@ -58,7 +59,7 @@ def tile_list_htabg_max_biasP_kernel(
 
         tab_sc = zeroed(nc.vector, slot("slot_x1", "tab_sc", [P, T], U8))
         tab_w = sb("tab_w", [P, T], I32)
-        wb_sc_raw = zeroed(nc.gpsimd, slot("slot_bias", "wb_sc_raw", [P, 2 * R], U8))
+        wb_sc_raw = zeroed(nc.gpsimd, sb("wb_sc_raw", [P, 2 * R], U8))
         sc1 = [zeroed(nc.gpsimd, sb(f"sc1_{h}", [P, HALF], U8)) for h in range(J // HALF)]
 
         def load_words(t, words, passes):
@@ -76,8 +77,8 @@ def tile_list_htabg_max_biasP_kernel(
                 )
 
         def load_weight(name, words, scales):
-            raw = slot("slot_" + name, name + "_raw", [P, 3 * R], U8)
-            zeroed(nc.vector, raw[:, 2 * R : 3 * R])
+            raw = slot("parted0", name + "_raw", [P, 3 * R], U8)
+            zeroed(nc.gpsimd, raw[:, 2 * R : 3 * R])
             load_words(raw[:, 0 : 2 * R], words, 1)
             load_scales(nc.sync, raw[:, 2 * R : 3 * R], scales, 0)
             return raw
@@ -94,7 +95,7 @@ def tile_list_htabg_max_biasP_kernel(
 
         nc.sync.dma_start(tab_list[:], offs)
         nc.sync.dma_start(head_lists[:], offs2)
-        wb_raw = sb("wb_raw", [P, 2 * 2 * R], U8)
+        wb_raw = slot("raw_words", "wb_raw", [P, 2 * 2 * R], U8)
         load_words(wb_raw[:], wb_words, 2)
         load_scales(nc.sync, tab_sc, tab_scales, 0)
         nc.sync.dma_start(out=tab_w[:], in_=tab_words[0].rearrange("p t b -> p (t b)").bitcast(I32))
@@ -106,6 +107,8 @@ def tile_list_htabg_max_biasP_kernel(
         load_plane(0)
         wgt = sb("wgt", [P, J], F32)
         nc.sync.dma_start(out=wgt[:], in_=wgt2)
+        bias = sb("bias", [P, PACK], F32)
+        nc.sync.dma_start(out=bias[:], in_=b.rearrange("(p t) -> p t", t=PACK))
 
         def deal(dealt, raw, passes, dtype):
             nc.vector.tensor_copy(
@@ -121,6 +124,8 @@ def tile_list_htabg_max_biasP_kernel(
             return dict(lhsT=words[:, cols(t, 2 * P)].bitcast(FP4X4), lhsT_scale=scales[:, cols(t, P)])
 
         wb = deal(sb("wb", [P, 4 * R], U8), wb_raw[:], 2, U16)
+        wa_raw = slot("raw_words", "wa_raw", [P, 2 * R], U8)
+        load_words(wa_raw[:], wa_words, 1)
         sc0 = []
         for h in range(J // HALF):
             g = sb(f"sc0_{h}", [P, HALF], U8)
@@ -129,26 +134,18 @@ def tile_list_htabg_max_biasP_kernel(
             sc0.append(g)
         load_plane(1)
         wb_sc = deal(sb("wb_sc", [P, 2 * R], U8), wb_sc_raw[:], 2, U8)
-        bias = slot("slot_bias", "bias", [P, PACK], F32)
-        nc.sync.dma_start(out=bias[:], in_=b.rearrange("(p t) -> p t", t=PACK))
+        load_scales(nc.sync, wb_sc_raw[:, 0:R], wa_scales, 0)
 
         yb = sb("yb", [P, J, PACK], BF16)
         for c in range(J // WIDE):
-            picked = slot(("slot_x2", "slot_wa", "slot_x3", "slot_wd")[c], f"picked{c}", [P, WIDE], U32)
+            picked = slot(f"slot_x{c + 2}", f"picked{c}", [P, WIDE], U32)
             nc.vector.tensor_copy(out=picked[:], in_=tab_w[:].bitcast(U32).indirect(tab_list[:, entries(c, WIDE)]))
             parted = slot(f"parted{c}", f"parted{c}", [P, 2 * 2 * WIDE], U8)
             nc.vector.tensor_copy(
                 out=parted[:].bitcast(U16).rearrange("p (d j) -> p d j", d=2),
                 in_=picked[:].bitcast(U16).rearrange("p (j d) -> p d j", d=2),
             )
-            if c == 0:
-                load_plane(2)
-            if c == 1:
-                wa_raw = load_weight("wa", wa_words, wa_scales)
-            if c == 2:
-                load_plane(3)
-            if c == 3:
-                wd_raw = load_weight("wd", wd_words, wd_scales)
+            load_plane(c + 2)
             for s in range(WIDE // UNIT):
                 u = c * (WIDE // UNIT) + s
                 h, hu = divmod(u, HALF // UNIT)
@@ -164,18 +161,31 @@ def tile_list_htabg_max_biasP_kernel(
                         )
                 nc.scalar.activation(out=yb[:, cols(u, UNIT), :], in_=bank[:].rearrange("p t j -> p j t"), func=IDENTITY)
 
+        wd_raw = load_weight("wd", wd_words, wd_scales)
         starts = [sum(WIDTHS[:u]) for u in range(len(WIDTHS))]
         spans = [slice(s, s + w) for s, w in zip(starts, WIDTHS)]
         x_il = [slot(f"x_il{u}", f"x_il{u}", [P, w, PACK], BF16) for u, w in enumerate(WIDTHS)]
 
+        def pick(g, i, span, origin):
+            nc.vector.tensor_tensor(
+                g[:, i, span.start - origin : span.stop - origin],
+                x_planes[i][:].indirect(head_lists[:, span.start // 16 : span.stop // 16]), wgt[:, span], ALU.mult,
+            )
+
+        batches = {}
+
         def stage_pick(u):
-            g = keep.tile([P, PACK, WIDTHS[u]], F32, name=f"g{u}", tag="picks", bufs=AHEAD, align_bytes=64)
-            listed = head_lists[:, spans[u].start // 16 : spans[u].stop // 16]
-            for i in range(PACK):
-                nc.vector.tensor_tensor(g[:, i, :], x_planes[i][:].indirect(listed), wgt[:, spans[u]], ALU.mult)
+            first, last = (0, AHEAD) if u < AHEAD else (AHEAD, len(WIDTHS))
+            origin, end = starts[first], spans[last - 1].stop
+            if u == first:
+                batches[first] = slot("first_batch" if first == 0 else "x_il0", f"g{first}", [P, PACK, end - origin], F32)
+                for i in range(PACK - 1):
+                    pick(batches[first], i, slice(origin, end), origin)
+            g = batches[first]
+            pick(g, PACK - 1, spans[u], origin)
             nc.scalar.copy(
                 out=x_il[u][:].rearrange("p (c i) t -> p c t i", i=PACK),
-                in_=g[:].rearrange("p t (c i) -> p c t i", i=PACK),
+                in_=g[:, :, spans[u].start - origin : spans[u].stop - origin].rearrange("p t (c i) -> p c t i", i=PACK),
             )
 
         def quantise(name, src, width):
@@ -229,14 +239,17 @@ def tile_list_htabg_max_biasP_kernel(
                         out=bank[:, e, :], rhs=q[0][:].bitcast(FP8X4), rhs_scale=q[1][:],
                         start=True, stop=True, **stationary(*wd, k * per_bank + e),
                     )
-                for e in range(per_bank):
-                    t = k * per_bank + e
-                    nc.scalar.activation(out=y[:, t, :], in_=bank[:, e, :], func=IDENTITY, bias=bias[:, t : t + 1])
+                if u == len(WIDTHS) - 1:
+                    nc.vector.tensor_tensor(y[:], bank[:], bias[:].unsqueeze(2).to_broadcast([P, PACK, width]), ALU.add)
+                else:
+                    for e in range(per_bank):
+                        t = k * per_bank + e
+                        nc.scalar.activation(out=y[:, t, :], in_=bank[:, e, :], func=IDENTITY, bias=bias[:, t : t + 1])
             nc.sync.dma_start(out=y_rows[:, :, spans[u]], in_=y[:])
             y_il[u] = sb(f"y_il{u}", [P, width, PACK], BF16)
             dst = y_il[u][:].rearrange("p (c i) t -> p c t i", i=PACK)
             src = y[:].rearrange("p t (c i) -> p c t i", i=PACK)
-            if u == len(WIDTHS) - 1:
+            if u >= WOVEN_BY_SCALAR:
                 nc.vector.tensor_copy(out=dst, in_=src)
             else:
                 nc.scalar.copy(out=dst, in_=src)
@@ -246,14 +259,17 @@ def tile_list_htabg_max_biasP_kernel(
                 out=y_codes[:, spans[u]].bitcast(FP8X4), scales=y_scales[:, spans[u]],
                 in_=y_il[u][:].rearrange("p j t -> p (j t)"),
             )
-            nc.sync.dma_start(out=code_rows[:, spans[u]], in_=y_codes[:, spans[u]])
+            if u in (AHEAD - 1, len(WIDTHS) - 1):
+                done = slice(0 if u < AHEAD else starts[AHEAD], spans[u].stop)
+                nc.sync.dma_start(out=code_rows[:, done], in_=y_codes[:, done])
 
         stages = (stage_pick, stage_ya, stage_max, stage_y, stage_planes)
         for step in range(len(WIDTHS) + len(stages) - 1):
             if step == 1:
-                wa = deal_weight(slot("parted3", "wa", [P, 3 * R], U8), wa_raw)
-            if step == 2:
-                wd = deal_weight(slot("x_il0", "wd", [P, 3 * R], U8), wd_raw)
+                dealt = sb("wa", [P, 3 * R], U8)
+                wa = (deal(dealt[:, 0 : 2 * R], wa_raw[:], 1, U16), deal(dealt[:, 2 * R : 3 * R], wb_sc_raw[:, 0:R], 1, U8))
+            if step == 3:
+                wd = deal_weight(slot("x_il1", "wd", [P, 3 * R], U8), wd_raw)
             for lag, stage in enumerate(stages):
                 if 0 <= step - lag < len(WIDTHS):
                     stage(step - lag)

@@ -23,7 +23,7 @@ UNIT = 128
 UNITS = J // UNIT
 WIDE = 512
 HALF = 512
-AHEAD = 3
+AHEAD = 2
 STAGED = 2
 WOVEN_BY_SCALAR = 2
 WIDTHS = (256, 256, 256, 128, 128)
@@ -36,6 +36,7 @@ def tile_list_htabg_max_biasP_kernel(
     nc = tc.nc
     with ExitStack() as ctx:
         keep = ctx.enter_context(tc.tile_pool(name="keep", bufs=1))
+        arena = ctx.enter_context(tc.tile_pool(name="arena", bufs=1))
         psum = ctx.enter_context(tc.psum_pool(name="psum", bufs=1))
 
         def sb(name, shape, dtype):
@@ -53,14 +54,27 @@ def tile_list_htabg_max_biasP_kernel(
         def slot(tag, name, shape, dtype):
             return keep.tile(shape, dtype, name=name, tag=tag, align_bytes=64)
 
+        def placed(offset, name, shape, dtype):
+            return arena.tile(shape, dtype, name=name, offset=offset, align_bytes=64)
+
         def zeroed(engine, t):
             engine.memset(t[:].bitcast(I32), 0)
             return t
 
-        tab_sc = zeroed(nc.vector, slot("slot_x1", "tab_sc", [P, T], U8))
-        tab_w = sb("tab_w", [P, T], I32)
-        wb_sc_raw = zeroed(nc.gpsimd, sb("wb_sc_raw", [P, 2 * R], U8))
-        sc1 = [zeroed(nc.gpsimd, sb(f"sc1_{h}", [P, HALF], U8)) for h in range(J // HALF)]
+        plane_bytes = 4 * T
+        at_x0 = plane_bytes
+        at_words = at_x0 + plane_bytes
+        at_x1 = at_words + 4 * R
+        at_wgt = at_x1 + plane_bytes
+        tab_sc = zeroed(nc.vector, placed(at_wgt - 64, "tab_sc", [P, T], U8))
+        zeros = zeroed(nc.vector, placed(0, "zeros", [P, J], U8))
+        sc1 = [sb(f"sc1_{h}", [P, HALF], U8) for h in range(J // HALF)]
+        for h in range(J // HALF):
+            nc.vector.tensor_copy(out=sc1[h][:].bitcast(I32), in_=zeros[:, cols(h, HALF)].bitcast(I32))
+        tab_w = placed(0, "tab_w", [P, T], I32)
+        wb_sc_raw = zeroed(nc.vector, slot("slot_x2", "wb_sc_raw", [P, 2 * R], U8))
+        wa_sc_raw = zeroed(nc.gpsimd, sb("wa_sc_raw", [P, R], U8))
+        wd_sc_raw = zeroed(nc.gpsimd, sb("wd_sc_raw", [P, R], U8))
 
         def load_words(t, words, passes):
             nc.sync.dma_start(
@@ -76,39 +90,39 @@ def tile_list_htabg_max_biasP_kernel(
                     in_=scales[:, 4 * q : 4 * q + 4, :].bitcast(I32),
                 )
 
-        def load_weight(name, words, scales):
-            raw = slot("parted0", name + "_raw", [P, 3 * R], U8)
-            zeroed(nc.gpsimd, raw[:, 2 * R : 3 * R])
-            load_words(raw[:, 0 : 2 * R], words, 1)
-            load_scales(nc.sync, raw[:, 2 * R : 3 * R], scales, 0)
-            return raw
-
         def lower(dst, src):
-            nc.scalar.dma_start(out=dst[0:112, :].bitcast(I32), in_=src[4:116, :].bitcast(I32))
+            nc.scalar.dma_start(out=dst[0:112, :].bitcast(I32), in_=src[16:128, :].bitcast(I32))
 
         x_planes = []
 
         def load_plane(i):
-            plane = slot(f"slot_x{i}", f"x{i}", [P, T], F32)
+            if i < 2:
+                plane = placed((at_x0, at_x1)[i], f"x{i}", [P, T], F32)
+            else:
+                plane = slot(f"slot_x{i}", f"x{i}", [P, T], F32)
             nc.sync.dma_start(out=plane[:], in_=xT.rearrange("(p i) t -> p i t", i=PACK)[:, i, :])
             x_planes.append(plane)
 
         nc.sync.dma_start(tab_list[:], offs)
-        nc.sync.dma_start(head_lists[:], offs2)
-        wb_raw = slot("raw_words", "wb_raw", [P, 2 * 2 * R], U8)
+        wb_raw = placed(at_words - 64, "wb_raw", [P, 2 * 2 * R], U8)
         load_words(wb_raw[:], wb_words, 2)
-        load_scales(nc.sync, tab_sc, tab_scales, 0)
+        nc.sync.dma_start(head_lists[:], offs2)
+        for r in range(4):
+            nc.sync.dma_start(
+                out=tab_sc[r:P:16, :].bitcast(I32),
+                in_=tab_scales.bitcast(I32).rearrange("a (q r) c -> r q a c", r=4)[r],
+            )
         nc.sync.dma_start(out=tab_w[:], in_=tab_words[0].rearrange("p t b -> p (t b)").bitcast(I32))
         for q in range(QUADS):
-            nc.sync.dma_start(
+            nc.scalar.dma_start(
                 out=wb_sc_raw[32 * q : 32 * q + 4, :].bitcast(I32).rearrange("r (a c) -> r a c", a=2),
                 in_=wb_scales[:, 4 * q : 4 * q + 4, :].bitcast(I32).rearrange("a r c -> r a c"),
             )
-        load_plane(0)
-        wgt = sb("wgt", [P, J], F32)
-        nc.sync.dma_start(out=wgt[:], in_=wgt2)
+        split = sum(WIDTHS[:AHEAD])
         bias = sb("bias", [P, PACK], F32)
-        nc.sync.dma_start(out=bias[:], in_=b.rearrange("(p t) -> p t", t=PACK))
+        load_scales(nc.gpsimd, wa_sc_raw, wa_scales, 0)
+        nc.gpsimd.dma_start(out=bias[:], in_=b.rearrange("(p t) -> p t", t=PACK))
+        load_scales(nc.gpsimd, wd_sc_raw, wd_scales, 0)
 
         def deal(dealt, raw, passes, dtype):
             nc.vector.tensor_copy(
@@ -117,35 +131,38 @@ def tile_list_htabg_max_biasP_kernel(
             )
             return dealt
 
-        def deal_weight(dealt, raw):
-            return deal(dealt[:, 0 : 2 * R], raw[:, 0 : 2 * R], 1, U16), deal(dealt[:, 2 * R : 3 * R], raw[:, 2 * R : 3 * R], 1, U8)
-
         def stationary(words, scales, t):
             return dict(lhsT=words[:, cols(t, 2 * P)].bitcast(FP4X4), lhsT_scale=scales[:, cols(t, P)])
 
         wb = deal(sb("wb", [P, 4 * R], U8), wb_raw[:], 2, U16)
-        wa_raw = slot("raw_words", "wa_raw", [P, 2 * R], U8)
+        load_plane(0)
+        wa_raw = placed(at_words, "wa_raw", [P, 2 * R], U8)
         load_words(wa_raw[:], wa_words, 1)
+        wd_raw = placed(at_words + 2 * R, "wd_raw", [P, 2 * R], U8)
+        load_words(wd_raw[:], wd_words, 1)
         sc0 = []
         for h in range(J // HALF):
             g = sb(f"sc0_{h}", [P, HALF], U8)
             nc.vector.tensor_copy(out=g[:], in_=tab_sc[:].indirect(tab_list[:, entries(h, HALF)]))
             lower(sc1[h], g)
             sc0.append(g)
+        wgt_first = placed(at_wgt, "wgt_first", [P, split], F32)
+        nc.sync.dma_start(out=wgt_first[:], in_=wgt2[:, 0:split])
         load_plane(1)
         wb_sc = deal(sb("wb_sc", [P, 2 * R], U8), wb_sc_raw[:], 2, U8)
-        load_scales(nc.sync, wb_sc_raw[:, 0:R], wa_scales, 0)
+        load_plane(2)
 
         yb = sb("yb", [P, J, PACK], BF16)
         for c in range(J // WIDE):
-            picked = slot(f"slot_x{c + 2}", f"picked{c}", [P, WIDE], U32)
+            picked = slot(("slot_x3", "wgt_rest")[c], f"picked{c}", [P, WIDE], U32)
             nc.vector.tensor_copy(out=picked[:], in_=tab_w[:].bitcast(U32).indirect(tab_list[:, entries(c, WIDE)]))
             parted = slot(f"parted{c}", f"parted{c}", [P, 2 * 2 * WIDE], U8)
             nc.vector.tensor_copy(
                 out=parted[:].bitcast(U16).rearrange("p (d j) -> p d j", d=2),
                 in_=picked[:].bitcast(U16).rearrange("p (j d) -> p d j", d=2),
             )
-            load_plane(c + 2)
+            if c == 0:
+                load_plane(3)
             for s in range(WIDE // UNIT):
                 u = c * (WIDE // UNIT) + s
                 h, hu = divmod(u, HALF // UNIT)
@@ -161,15 +178,20 @@ def tile_list_htabg_max_biasP_kernel(
                         )
                 nc.scalar.activation(out=yb[:, cols(u, UNIT), :], in_=bank[:].rearrange("p t j -> p j t"), func=IDENTITY)
 
-        wd_raw = load_weight("wd", wd_words, wd_scales)
+        wa_w = deal(sb("wa", [P, 2 * R], U8), wa_raw[:], 1, U16)
+        wd_w = deal(sb("wd", [P, 2 * R], U8), wd_raw[:], 1, U16)
+        wgt_rest = slot("wgt_rest", "wgt_rest", [P, J - split], F32)
+        nc.sync.dma_start(out=wgt_rest[:], in_=wgt2[:, split:J])
         starts = [sum(WIDTHS[:u]) for u in range(len(WIDTHS))]
         spans = [slice(s, s + w) for s, w in zip(starts, WIDTHS)]
         x_il = [slot(f"x_il{u}", f"x_il{u}", [P, w, PACK], BF16) for u, w in enumerate(WIDTHS)]
 
         def pick(g, i, span, origin):
+            local = slice(span.start - origin, span.stop - origin)
             nc.vector.tensor_tensor(
-                g[:, i, span.start - origin : span.stop - origin],
-                x_planes[i][:].indirect(head_lists[:, span.start // 16 : span.stop // 16]), wgt[:, span], ALU.mult,
+                g[:, i, local],
+                x_planes[i][:].indirect(head_lists[:, span.start // 16 : span.stop // 16]),
+                (wgt_first if origin == 0 else wgt_rest)[:, local], ALU.mult,
             )
 
         batches = {}
@@ -178,7 +200,7 @@ def tile_list_htabg_max_biasP_kernel(
             first, last = (0, AHEAD) if u < AHEAD else (AHEAD, len(WIDTHS))
             origin, end = starts[first], spans[last - 1].stop
             if u == first:
-                batches[first] = slot("first_batch" if first == 0 else "x_il0", f"g{first}", [P, PACK, end - origin], F32)
+                batches[first] = sb(f"g{first}", [P, PACK, end - origin], F32)
                 for i in range(PACK - 1):
                     pick(batches[first], i, slice(origin, end), origin)
             g = batches[first]
@@ -209,7 +231,11 @@ def tile_list_htabg_max_biasP_kernel(
         code_rows = out_1[0].rearrange("p j i -> p (j i)").bitcast(I32)
         ya, h_il, y_il = {}, {}, {}
 
+        wa = []
+
         def stage_ya(u):
+            if u == 0:
+                wa.extend((wa_w, deal(placed(at_wgt, "wa_sc", [P, R], U8), wa_sc_raw[:], 1, U8)))
             q = quantise(f"xq{u}", x_il[u], WIDTHS[u])
             ya[u] = [project("ya_bank", 3, wa, q, s) for s in range(WIDTHS[u] // UNIT)]
 
@@ -259,17 +285,14 @@ def tile_list_htabg_max_biasP_kernel(
                 out=y_codes[:, spans[u]].bitcast(FP8X4), scales=y_scales[:, spans[u]],
                 in_=y_il[u][:].rearrange("p j t -> p (j t)"),
             )
-            if u in (AHEAD - 1, len(WIDTHS) - 1):
-                done = slice(0 if u < AHEAD else starts[AHEAD], spans[u].stop)
+            if u in (2, len(WIDTHS) - 1):
+                done = slice(0 if u == 2 else starts[3], spans[u].stop)
                 nc.sync.dma_start(out=code_rows[:, done], in_=y_codes[:, done])
 
         stages = (stage_pick, stage_ya, stage_max, stage_y, stage_planes)
         for step in range(len(WIDTHS) + len(stages) - 1):
-            if step == 1:
-                dealt = sb("wa", [P, 3 * R], U8)
-                wa = (deal(dealt[:, 0 : 2 * R], wa_raw[:], 1, U16), deal(dealt[:, 2 * R : 3 * R], wb_sc_raw[:, 0:R], 1, U8))
             if step == 3:
-                wd = deal_weight(slot("x_il1", "wd", [P, 3 * R], U8), wd_raw)
+                wd = (wd_w, deal(slot("x_il1", "wd_sc", [P, R], U8), wd_sc_raw[:], 1, U8))
             for lag, stage in enumerate(stages):
                 if 0 <= step - lag < len(WIDTHS):
                     stage(step - lag)

@@ -23,7 +23,7 @@ UNIT = 128
 UNITS = J // UNIT
 WIDE = 512
 HALF = 512
-AHEAD = 2
+AHEAD = 3
 STAGED = 2
 WOVEN_BY_SCALAR = 2
 WIDTHS = (256, 256, 256, 128, 128)
@@ -104,9 +104,9 @@ def tile_list_htabg_max_biasP_kernel(
             x_planes.append(plane)
 
         nc.sync.dma_start(tab_list[:], offs)
+        nc.sync.dma_start(head_lists[:], offs2)
         wb_raw = placed(at_words - 64, "wb_raw", [P, 2 * 2 * R], U8)
         load_words(wb_raw[:], wb_words, 2)
-        nc.sync.dma_start(head_lists[:], offs2)
         for r in range(4):
             nc.sync.dma_start(
                 out=tab_sc[r:P:16, :].bitcast(I32),
@@ -114,7 +114,7 @@ def tile_list_htabg_max_biasP_kernel(
             )
         nc.sync.dma_start(out=tab_w[:], in_=tab_words[0].rearrange("p t b -> p (t b)").bitcast(I32))
         for q in range(QUADS):
-            nc.scalar.dma_start(
+            nc.sync.dma_start(
                 out=wb_sc_raw[32 * q : 32 * q + 4, :].bitcast(I32).rearrange("r (a c) -> r a c", a=2),
                 in_=wb_scales[:, 4 * q : 4 * q + 4, :].bitcast(I32).rearrange("a r c -> r a c"),
             )

@@ -25,7 +25,7 @@ WIDE = 512
 HALF = 512
 AHEAD = 3
 STAGED = 2
-WOVEN_BY_SCALAR = 2
+WOVEN_BY_SCALAR = 0
 WIDTHS = (256, 256, 256, 128, 128)
 
 

@@ -136,10 +136,6 @@ def tile_list_htabg_max_biasP_kernel(
 
         wb = deal(sb("wb", [P, 4 * R], U8), wb_raw[:], 2, U16)
         load_plane(0)
-        wa_raw = placed(at_words, "wa_raw", [P, 2 * R], U8)
-        load_words(wa_raw[:], wa_words, 1)
-        wd_raw = placed(at_words + 2 * R, "wd_raw", [P, 2 * R], U8)
-        load_words(wd_raw[:], wd_words, 1)
         sc0 = []
         for h in range(J // HALF):
             g = sb(f"sc0_{h}", [P, HALF], U8)
@@ -178,6 +174,10 @@ def tile_list_htabg_max_biasP_kernel(
                         )
                 nc.scalar.activation(out=yb[:, cols(u, UNIT), :], in_=bank[:].rearrange("p t j -> p j t"), func=IDENTITY)
 
+        wa_raw = placed(0, "wa_raw", [P, 2 * R], U8)
+        load_words(wa_raw[:], wa_words, 1)
+        wd_raw = placed(2 * R, "wd_raw", [P, 2 * R], U8)
+        load_words(wd_raw[:], wd_words, 1)
         wa_w = deal(sb("wa", [P, 2 * R], U8), wa_raw[:], 1, U16)
         wd_w = deal(sb("wd", [P, 2 * R], U8), wd_raw[:], 1, U16)
         wgt_rest = slot("wgt_rest", "wgt_rest", [P, J - split], F32)

@@ -22,7 +22,6 @@ QUADS = 4
 UNIT = 128
 UNITS = J // UNIT
 WIDE = 512
-HALF = 512
 AHEAD = 3
 STAGED = 2
 WOVEN_BY_SCALAR = 0
@@ -63,16 +62,16 @@ def tile_list_htabg_max_biasP_kernel(
 
         plane_bytes = 4 * T
         at_x0 = plane_bytes
-        at_words = at_x0 + plane_bytes
-        at_x1 = at_words + 4 * R
-        at_wgt = at_x1 + plane_bytes
-        tab_sc = zeroed(nc.vector, placed(at_wgt - 64, "tab_sc", [P, T], U8))
+        at_wgt = at_x0 + plane_bytes
+        at_x1 = at_wgt + plane_bytes
+        at_rest = at_x1 + plane_bytes
+        at_x3 = at_rest + 4 * WIDE
+        tab_sc = zeroed(nc.vector, placed(at_x1, "tab_sc", [P, T], U8))
         zeros = zeroed(nc.vector, placed(0, "zeros", [P, J], U8))
-        sc1 = [sb(f"sc1_{h}", [P, HALF], U8) for h in range(J // HALF)]
-        for h in range(J // HALF):
-            nc.vector.tensor_copy(out=sc1[h][:].bitcast(I32), in_=zeros[:, cols(h, HALF)].bitcast(I32))
+        sc1 = sb("sc1", [P, J], U8)
+        nc.vector.tensor_copy(out=sc1[:].bitcast(I32), in_=zeros[:].bitcast(I32))
         tab_w = placed(0, "tab_w", [P, T], I32)
-        wb_sc_raw = zeroed(nc.vector, slot("slot_x2", "wb_sc_raw", [P, 2 * R], U8))
+        wb_sc_raw = zeroed(nc.vector, placed(at_x3 - R, "wb_sc_raw", [P, 2 * R], U8))
         wa_sc_raw = zeroed(nc.gpsimd, sb("wa_sc_raw", [P, R], U8))
         wd_sc_raw = zeroed(nc.gpsimd, sb("wd_sc_raw", [P, R], U8))
 
@@ -90,22 +89,19 @@ def tile_list_htabg_max_biasP_kernel(
                     in_=scales[:, 4 * q : 4 * q + 4, :].bitcast(I32),
                 )
 
-        def lower(dst, src):
-            nc.scalar.dma_start(out=dst[0:112, :].bitcast(I32), in_=src[16:128, :].bitcast(I32))
-
         x_planes = []
 
         def load_plane(i):
-            if i < 2:
-                plane = placed((at_x0, at_x1)[i], f"x{i}", [P, T], F32)
+            if i == 2:
+                plane = slot("slot_x2", "x2", [P, T], F32)
             else:
-                plane = slot(f"slot_x{i}", f"x{i}", [P, T], F32)
+                plane = placed((at_x0, at_x1, None, at_x3)[i], f"x{i}", [P, T], F32)
             nc.sync.dma_start(out=plane[:], in_=xT.rearrange("(p i) t -> p i t", i=PACK)[:, i, :])
             x_planes.append(plane)
 
         nc.sync.dma_start(tab_list[:], offs)
         nc.sync.dma_start(head_lists[:], offs2)
-        wb_raw = placed(at_words - 64, "wb_raw", [P, 2 * 2 * R], U8)
+        wb_raw = placed(at_wgt - 64, "wb_raw", [P, 2 * 2 * R], U8)
         load_words(wb_raw[:], wb_words, 2)
         for r in range(4):
             nc.sync.dma_start(
@@ -136,21 +132,20 @@ def tile_list_htabg_max_biasP_kernel(
 
         wb = deal(sb("wb", [P, 4 * R], U8), wb_raw[:], 2, U16)
         load_plane(0)
-        sc0 = []
-        for h in range(J // HALF):
-            g = sb(f"sc0_{h}", [P, HALF], U8)
-            nc.vector.tensor_copy(out=g[:], in_=tab_sc[:].indirect(tab_list[:, entries(h, HALF)]))
-            lower(sc1[h], g)
-            sc0.append(g)
         wgt_first = placed(at_wgt, "wgt_first", [P, split], F32)
         nc.sync.dma_start(out=wgt_first[:], in_=wgt2[:, 0:split])
+        sc0 = sb("sc0", [P, J], U8)
+        nc.vector.tensor_copy(out=sc0[:], in_=tab_sc[:].indirect(tab_list[:]))
+        nc.sync.dma_start(out=sc1[0:112, :].bitcast(I32), in_=sc0[16:128, :].bitcast(I32))
         load_plane(1)
         wb_sc = deal(sb("wb_sc", [P, 2 * R], U8), wb_sc_raw[:], 2, U8)
-        load_plane(2)
 
         yb = sb("yb", [P, J, PACK], BF16)
         for c in range(J // WIDE):
-            picked = slot(("slot_x3", "wgt_rest")[c], f"picked{c}", [P, WIDE], U32)
+            if c == 0:
+                picked = slot("slot_x2", "picked0", [P, WIDE], U32)
+            else:
+                picked = placed(at_rest, "picked1", [P, WIDE], U32)
             nc.vector.tensor_copy(out=picked[:], in_=tab_w[:].bitcast(U32).indirect(tab_list[:, entries(c, WIDE)]))
             parted = slot(f"parted{c}", f"parted{c}", [P, 2 * 2 * WIDE], U8)
             nc.vector.tensor_copy(
@@ -158,17 +153,17 @@ def tile_list_htabg_max_biasP_kernel(
                 in_=picked[:].bitcast(U16).rearrange("p (j d) -> p d j", d=2),
             )
             if c == 0:
+                load_plane(2)
                 load_plane(3)
             for s in range(WIDE // UNIT):
                 u = c * (WIDE // UNIT) + s
-                h, hu = divmod(u, HALF // UNIT)
                 bank = psum.tile([P, PACK, UNIT], F32, name="yb_bank", tag="y_bank", bufs=5)
                 for t in range(PACK):
                     for a in range(2):
                         nc.tensor.matmul_mx(
                             out=bank[:, t, :],
                             rhs=parted[:, cols(a * (WIDE // UNIT) + s, 2 * UNIT)].bitcast(FP4X4),
-                            rhs_scale=(sc0, sc1)[a][h][:, cols(hu, UNIT)],
+                            rhs_scale=(sc0, sc1)[a][:, cols(u, UNIT)],
                             start=(a == 0), stop=(a == 1),
                             **stationary(wb[:, cols(a, 2 * R)], wb_sc[:, cols(a, R)], t),
                         )
@@ -180,7 +175,7 @@ def tile_list_htabg_max_biasP_kernel(
         load_words(wd_raw[:], wd_words, 1)
         wa_w = deal(sb("wa", [P, 2 * R], U8), wa_raw[:], 1, U16)
         wd_w = deal(sb("wd", [P, 2 * R], U8), wd_raw[:], 1, U16)
-        wgt_rest = slot("wgt_rest", "wgt_rest", [P, J - split], F32)
+        wgt_rest = placed(at_rest, "wgt_rest", [P, J - split], F32)
         nc.sync.dma_start(out=wgt_rest[:], in_=wgt2[:, split:J])
         starts = [sum(WIDTHS[:u]) for u in range(len(WIDTHS))]
         spans = [slice(s, s + w) for s, w in zip(starts, WIDTHS)]

@@ -72,8 +72,7 @@ def tile_list_htabg_max_biasP_kernel(
         nc.vector.tensor_copy(out=sc1[:].bitcast(I32), in_=zeros[:].bitcast(I32))
         tab_w = placed(0, "tab_w", [P, T], I32)
         wb_sc_raw = zeroed(nc.vector, placed(at_x3 - R, "wb_sc_raw", [P, 2 * R], U8))
-        wa_sc_raw = zeroed(nc.gpsimd, sb("wa_sc_raw", [P, R], U8))
-        wd_sc_raw = zeroed(nc.gpsimd, sb("wd_sc_raw", [P, R], U8))
+        late_sc_raw = zeroed(nc.gpsimd, sb("late_sc_raw", [P, R], U8))
 
         def load_words(t, words, passes):
             nc.sync.dma_start(
@@ -116,9 +115,10 @@ def tile_list_htabg_max_biasP_kernel(
             )
         split = sum(WIDTHS[:AHEAD])
         bias = sb("bias", [P, PACK], F32)
-        load_scales(nc.gpsimd, wa_sc_raw, wa_scales, 0)
+        load_scales(nc.gpsimd, late_sc_raw, wa_scales, 0)
+        load_scales(nc.gpsimd, late_sc_raw, wd_scales, 4)
         nc.gpsimd.dma_start(out=bias[:], in_=b.rearrange("(p t) -> p t", t=PACK))
-        load_scales(nc.gpsimd, wd_sc_raw, wd_scales, 0)
+        wd_sc = zeroed(nc.gpsimd, sb("wd_sc", [P, R], U8))
 
         def deal(dealt, raw, passes, dtype):
             nc.vector.tensor_copy(
@@ -227,10 +227,12 @@ def tile_list_htabg_max_biasP_kernel(
         ya, h_il, y_il = {}, {}, {}
 
         wa = []
+        wd = (wd_w, wd_sc)
 
         def stage_ya(u):
             if u == 0:
-                wa.extend((wa_w, deal(placed(at_wgt, "wa_sc", [P, R], U8), wa_sc_raw[:], 1, U8)))
+                wa.extend((wa_w, deal(placed(at_wgt, "wa_sc", [P, R], U8), late_sc_raw[:], 1, U8)))
+                nc.sync.dma_start(out=wd_sc[0:112, :].bitcast(I32), in_=wa[1][4:116, :].bitcast(I32))
             q = quantise(f"xq{u}", x_il[u], WIDTHS[u])
             ya[u] = [project("ya_bank", 3, wa, q, s) for s in range(WIDTHS[u] // UNIT)]
 
@@ -280,14 +282,10 @@ def tile_list_htabg_max_biasP_kernel(
                 out=y_codes[:, spans[u]].bitcast(FP8X4), scales=y_scales[:, spans[u]],
                 in_=y_il[u][:].rearrange("p j t -> p (j t)"),
             )
-            if u in (2, len(WIDTHS) - 1):
-                done = slice(0 if u == 2 else starts[3], spans[u].stop)
-                nc.sync.dma_start(out=code_rows[:, done], in_=y_codes[:, done])
+            nc.sync.dma_start(out=code_rows[:, spans[u]], in_=y_codes[:, spans[u]])
 
         stages = (stage_pick, stage_ya, stage_max, stage_y, stage_planes)
         for step in range(len(WIDTHS) + len(stages) - 1):
-            if step == 3:
-                wd = (wd_w, deal(slot("x_il1", "wd_sc", [P, R], U8), wd_sc_raw[:], 1, U8))
             for lag, stage in enumerate(stages):
                 if 0 <= step - lag < len(WIDTHS):
                     stage(step - lag)

@@ -23,7 +23,7 @@ UNIT = 128
 UNITS = J // UNIT
 WIDE = 512
 AHEAD = 3
-STAGED = 2
+STAGED = 3
 WOVEN_BY_SCALAR = 0
 WIDTHS = (256, 256, 256, 128, 128)
 

@@ -23,8 +23,7 @@ UNIT = 128
 UNITS = J // UNIT
 WIDE = 512
 AHEAD = 3
-STAGED = 3
-WOVEN_BY_SCALAR = 0
+STAGED = 2
 WIDTHS = (256, 256, 256, 128, 128)
 
 
@@ -61,17 +60,22 @@ def tile_list_htabg_max_biasP_kernel(
             return t
 
         plane_bytes = 4 * T
-        at_x0 = plane_bytes
-        at_wgt = at_x0 + plane_bytes
-        at_x1 = at_wgt + plane_bytes
-        at_rest = at_x1 + plane_bytes
-        at_x3 = at_rest + 4 * WIDE
+        split = sum(WIDTHS[:AHEAD])
+        at_x2 = 0
+        at_tab = plane_bytes - 64
+        at_late = plane_bytes
+        at_x3 = at_tab + plane_bytes - 64
+        at_wgt = at_x3 + plane_bytes
+        at_x0 = at_wgt + 4 * split
+        at_x1 = at_x0 + plane_bytes
+        at_zeros = at_x3 - 64
         tab_sc = zeroed(nc.vector, placed(at_x1, "tab_sc", [P, T], U8))
-        zeros = zeroed(nc.vector, placed(0, "zeros", [P, J], U8))
+        zeros = placed(at_zeros, "zeros", [P, at_x0 + 64 - at_zeros], U8)
+        nc.gpsimd.memset(zeros[:, 0:J].bitcast(I32), 0)
         sc1 = sb("sc1", [P, J], U8)
-        nc.vector.tensor_copy(out=sc1[:].bitcast(I32), in_=zeros[:].bitcast(I32))
-        tab_w = placed(0, "tab_w", [P, T], I32)
-        wb_sc_raw = zeroed(nc.vector, placed(at_x3 - R, "wb_sc_raw", [P, 2 * R], U8))
+        nc.vector.tensor_copy(out=sc1[:].bitcast(I32), in_=zeros[:, 0:J].bitcast(I32))
+        tab_w = placed(at_tab, "tab_w", [P, T], I32)
+        wb_sc_raw = zeroed(nc.vector, sb("wb_sc_raw", [P, 2 * R], U8))
         late_sc_raw = zeroed(nc.gpsimd, sb("late_sc_raw", [P, R], U8))
 
         def load_words(t, words, passes):
@@ -91,16 +95,13 @@ def tile_list_htabg_max_biasP_kernel(
         x_planes = []
 
         def load_plane(i):
-            if i == 2:
-                plane = slot("slot_x2", "x2", [P, T], F32)
-            else:
-                plane = placed((at_x0, at_x1, None, at_x3)[i], f"x{i}", [P, T], F32)
+            plane = placed((at_x0, at_x1, at_x2, at_x3)[i], f"x{i}", [P, T], F32)
             nc.sync.dma_start(out=plane[:], in_=xT.rearrange("(p i) t -> p i t", i=PACK)[:, i, :])
             x_planes.append(plane)
 
         nc.sync.dma_start(tab_list[:], offs)
         nc.sync.dma_start(head_lists[:], offs2)
-        wb_raw = placed(at_wgt - 64, "wb_raw", [P, 2 * 2 * R], U8)
+        wb_raw = sb("wb_raw", [P, 2 * 2 * R], U8)
         load_words(wb_raw[:], wb_words, 2)
         for r in range(4):
             nc.sync.dma_start(
@@ -108,12 +109,14 @@ def tile_list_htabg_max_biasP_kernel(
                 in_=tab_scales.bitcast(I32).rearrange("a (q r) c -> r q a c", r=4)[r],
             )
         nc.sync.dma_start(out=tab_w[:], in_=tab_words[0].rearrange("p t b -> p (t b)").bitcast(I32))
+        load_plane(0)
         for q in range(QUADS):
             nc.sync.dma_start(
                 out=wb_sc_raw[32 * q : 32 * q + 4, :].bitcast(I32).rearrange("r (a c) -> r a c", a=2),
                 in_=wb_scales[:, 4 * q : 4 * q + 4, :].bitcast(I32).rearrange("a r c -> r a c"),
             )
-        split = sum(WIDTHS[:AHEAD])
+        wgt_first = placed(at_wgt, "wgt_first", [P, split], F32)
+        nc.sync.dma_start(out=wgt_first[:], in_=wgt2[:, 0:split])
         bias = sb("bias", [P, PACK], F32)
         load_scales(nc.gpsimd, late_sc_raw, wa_scales, 0)
         load_scales(nc.gpsimd, late_sc_raw, wd_scales, 4)
@@ -131,9 +134,6 @@ def tile_list_htabg_max_biasP_kernel(
             return dict(lhsT=words[:, cols(t, 2 * P)].bitcast(FP4X4), lhsT_scale=scales[:, cols(t, P)])
 
         wb = deal(sb("wb", [P, 4 * R], U8), wb_raw[:], 2, U16)
-        load_plane(0)
-        wgt_first = placed(at_wgt, "wgt_first", [P, split], F32)
-        nc.sync.dma_start(out=wgt_first[:], in_=wgt2[:, 0:split])
         sc0 = sb("sc0", [P, J], U8)
         nc.vector.tensor_copy(out=sc0[:], in_=tab_sc[:].indirect(tab_list[:]))
         nc.sync.dma_start(out=sc1[0:112, :].bitcast(I32), in_=sc0[16:128, :].bitcast(I32))
@@ -141,68 +141,72 @@ def tile_list_htabg_max_biasP_kernel(
         wb_sc = deal(sb("wb_sc", [P, 2 * R], U8), wb_sc_raw[:], 2, U8)
 
         yb = sb("yb", [P, J, PACK], BF16)
+        picks = []
         for c in range(J // WIDE):
-            if c == 0:
-                picked = slot("slot_x2", "picked0", [P, WIDE], U32)
-            else:
-                picked = placed(at_rest, "picked1", [P, WIDE], U32)
+            picked = sb(f"picked{c}", [P, WIDE], U32)
             nc.vector.tensor_copy(out=picked[:], in_=tab_w[:].bitcast(U32).indirect(tab_list[:, entries(c, WIDE)]))
+            picks.append(picked)
+        load_plane(2)
+        load_plane(3)
+        for c, picked in enumerate(picks):
             parted = slot(f"parted{c}", f"parted{c}", [P, 2 * 2 * WIDE], U8)
             nc.vector.tensor_copy(
                 out=parted[:].bitcast(U16).rearrange("p (d j) -> p d j", d=2),
                 in_=picked[:].bitcast(U16).rearrange("p (j d) -> p d j", d=2),
             )
-            if c == 0:
-                load_plane(2)
-                load_plane(3)
             for s in range(WIDE // UNIT):
                 u = c * (WIDE // UNIT) + s
                 bank = psum.tile([P, PACK, UNIT], F32, name="yb_bank", tag="y_bank", bufs=5)
                 for t in range(PACK):
-                    for a in range(2):
+                    for a in (1, 0):
                         nc.tensor.matmul_mx(
                             out=bank[:, t, :],
                             rhs=parted[:, cols(a * (WIDE // UNIT) + s, 2 * UNIT)].bitcast(FP4X4),
                             rhs_scale=(sc0, sc1)[a][:, cols(u, UNIT)],
-                            start=(a == 0), stop=(a == 1),
+                            start=(a == 1), stop=(a == 0),
                             **stationary(wb[:, cols(a, 2 * R)], wb_sc[:, cols(a, R)], t),
                         )
                 nc.scalar.activation(out=yb[:, cols(u, UNIT), :], in_=bank[:].rearrange("p t j -> p j t"), func=IDENTITY)
 
-        wa_raw = placed(0, "wa_raw", [P, 2 * R], U8)
+        wa_raw = placed(at_late, "wa_raw", [P, 2 * R], U8)
         load_words(wa_raw[:], wa_words, 1)
-        wd_raw = placed(2 * R, "wd_raw", [P, 2 * R], U8)
+        wd_raw = placed(at_late + 2 * R, "wd_raw", [P, 2 * R], U8)
         load_words(wd_raw[:], wd_words, 1)
         wa_w = deal(sb("wa", [P, 2 * R], U8), wa_raw[:], 1, U16)
         wd_w = deal(sb("wd", [P, 2 * R], U8), wd_raw[:], 1, U16)
-        wgt_rest = placed(at_rest, "wgt_rest", [P, J - split], F32)
+        wgt_rest = placed(at_late + 4 * R, "wgt_rest", [P, J - split], F32)
         nc.sync.dma_start(out=wgt_rest[:], in_=wgt2[:, split:J])
         starts = [sum(WIDTHS[:u]) for u in range(len(WIDTHS))]
         spans = [slice(s, s + w) for s, w in zip(starts, WIDTHS)]
         x_il = [slot(f"x_il{u}", f"x_il{u}", [P, w, PACK], BF16) for u, w in enumerate(WIDTHS)]
 
-        def pick(g, i, span, origin):
-            local = slice(span.start - origin, span.stop - origin)
+        def pick(g, i, span):
+            origin = 0 if span.start < split else split
             nc.vector.tensor_tensor(
-                g[:, i, local],
+                g,
                 x_planes[i][:].indirect(head_lists[:, span.start // 16 : span.stop // 16]),
-                (wgt_first if origin == 0 else wgt_rest)[:, local], ALU.mult,
+                (wgt_first if origin == 0 else wgt_rest)[:, span.start - origin : span.stop - origin], ALU.mult,
             )
 
-        batches = {}
+        ring_width = max(WIDTHS[0], J - split)
+        g_first = slot("g_ring", "g_first", [P, PACK, ring_width], F32)
+        g_next = sb("g_next", [P, PACK, split - WIDTHS[0]], F32)
+        for i in range(PACK - 1):
+            pick(g_first[:, i, 0 : WIDTHS[0]], i, spans[0])
+            pick(g_next[:, i, :], i, slice(WIDTHS[0], split))
+        late = []
 
         def stage_pick(u):
-            first, last = (0, AHEAD) if u < AHEAD else (AHEAD, len(WIDTHS))
-            origin, end = starts[first], spans[last - 1].stop
-            if u == first:
-                batches[first] = sb(f"g{first}", [P, PACK, end - origin], F32)
+            if u == AHEAD:
+                late.append(slot("g_ring", "g_late", [P, PACK, ring_width], F32))
                 for i in range(PACK - 1):
-                    pick(batches[first], i, slice(origin, end), origin)
-            g = batches[first]
-            pick(g, PACK - 1, spans[u], origin)
+                    pick(late[0][:, i, 0 : J - split], i, slice(split, J))
+            g, origin = (g_first, 0) if u == 0 else (g_next, WIDTHS[0]) if u < AHEAD else (late[0], split)
+            local = slice(spans[u].start - origin, spans[u].stop - origin)
+            pick(g[:, PACK - 1, local], PACK - 1, spans[u])
             nc.scalar.copy(
                 out=x_il[u][:].rearrange("p (c i) t -> p c t i", i=PACK),
-                in_=g[:, :, spans[u].start - origin : spans[u].stop - origin].rearrange("p t (c i) -> p c t i", i=PACK),
+                in_=g[:, :, local].rearrange("p t (c i) -> p c t i", i=PACK),
             )
 
         def quantise(name, src, width):
@@ -224,7 +228,8 @@ def tile_list_htabg_max_biasP_kernel(
         y_scales = sb("y_scales", [P, J], U8)
         y_rows = out_0.rearrange("(p t) j -> p t j", t=PACK)
         code_rows = out_1[0].rearrange("p j i -> p (j i)").bitcast(I32)
-        ya, h_il, y_il = {}, {}, {}
+        ya, h_il = {}, {}
+        y_il = sb("y_il", [P, J, PACK], BF16)
 
         wa = []
         wd = (wd_w, wd_sc)
@@ -262,27 +267,31 @@ def tile_list_htabg_max_biasP_kernel(
                         out=bank[:, e, :], rhs=q[0][:].bitcast(FP8X4), rhs_scale=q[1][:],
                         start=True, stop=True, **stationary(*wd, k * per_bank + e),
                     )
-                if u == len(WIDTHS) - 1:
-                    nc.vector.tensor_tensor(y[:], bank[:], bias[:].unsqueeze(2).to_broadcast([P, PACK, width]), ALU.add)
-                else:
-                    for e in range(per_bank):
-                        t = k * per_bank + e
-                        nc.scalar.activation(out=y[:, t, :], in_=bank[:, e, :], func=IDENTITY, bias=bias[:, t : t + 1])
+                for e in range(per_bank):
+                    t = k * per_bank + e
+                    nc.scalar.activation(out=y[:, t, :], in_=bank[:, e, :], func=IDENTITY, bias=bias[:, t : t + 1])
             nc.sync.dma_start(out=y_rows[:, :, spans[u]], in_=y[:])
-            y_il[u] = sb(f"y_il{u}", [P, width, PACK], BF16)
-            dst = y_il[u][:].rearrange("p (c i) t -> p c t i", i=PACK)
-            src = y[:].rearrange("p t (c i) -> p c t i", i=PACK)
-            if u >= WOVEN_BY_SCALAR:
-                nc.vector.tensor_copy(out=dst, in_=src)
-            else:
-                nc.scalar.copy(out=dst, in_=src)
+            parts = 2 if u < AHEAD else 1
+            for h in range(parts):
+                half = cols(h, width // parts)
+                nc.vector.tensor_copy(
+                    out=y_il[:, spans[u], :][:, half, :].rearrange("p (c i) t -> p c t i", i=PACK),
+                    in_=y[:, :, half].rearrange("p t (c i) -> p c t i", i=PACK),
+                )
+
+        def planes(span):
+            nc.vector.quantize_mx(
+                out=y_codes[:, span].bitcast(FP8X4), scales=y_scales[:, span],
+                in_=y_il[:, span, :].rearrange("p j t -> p (j t)"),
+            )
 
         def stage_planes(u):
-            nc.vector.quantize_mx(
-                out=y_codes[:, spans[u]].bitcast(FP8X4), scales=y_scales[:, spans[u]],
-                in_=y_il[u][:].rearrange("p j t -> p (j t)"),
-            )
-            nc.sync.dma_start(out=code_rows[:, spans[u]], in_=y_codes[:, spans[u]])
+            ends = [s.stop - (UNIT if v < AHEAD else 0) for v, s in enumerate(spans)]
+            window = slice(ends[u - 1] if u else 0, ends[u])
+            planes(window)
+            if u in (1, 2, 4):
+                stored = slice({1: 0, 2: ends[1], 4: ends[2]}[u], ends[u])
+                nc.sync.dma_start(out=code_rows[:, stored], in_=y_codes[:, stored])
 
         stages = (stage_pick, stage_ya, stage_max, stage_y, stage_planes)
         for step in range(len(WIDTHS) + len(stages) - 1):

@@ -23,7 +23,8 @@ UNIT = 128
 UNITS = J // UNIT
 WIDE = 512
 AHEAD = 3
-STAGED = 2
+STAGED = (0, 2,)
+WOVEN = 0
 WIDTHS = (256, 256, 256, 128, 128)
 
 
@@ -67,16 +68,16 @@ def tile_list_htabg_max_biasP_kernel(
         at_x3 = at_tab + plane_bytes - 64
         at_wgt = at_x3 + plane_bytes
         at_x0 = at_wgt + 4 * split
-        at_x1 = at_x0 + plane_bytes
+        at_x1 = at_x0 + plane_bytes + R
+        at_picked = at_x1 + plane_bytes
         at_zeros = at_x3 - 64
-        tab_sc = zeroed(nc.vector, placed(at_x1, "tab_sc", [P, T], U8))
+        tab_sc = zeroed(nc.vector, placed(at_x1 - R, "tab_sc", [P, T], U8))
         zeros = placed(at_zeros, "zeros", [P, at_x0 + 64 - at_zeros], U8)
         nc.gpsimd.memset(zeros[:, 0:J].bitcast(I32), 0)
         sc1 = sb("sc1", [P, J], U8)
         nc.vector.tensor_copy(out=sc1[:].bitcast(I32), in_=zeros[:, 0:J].bitcast(I32))
         tab_w = placed(at_tab, "tab_w", [P, T], I32)
         wb_sc_raw = zeroed(nc.vector, sb("wb_sc_raw", [P, 2 * R], U8))
-        late_sc_raw = zeroed(nc.gpsimd, sb("late_sc_raw", [P, R], U8))
 
         def load_words(t, words, passes):
             nc.sync.dma_start(
@@ -84,12 +85,11 @@ def tile_list_htabg_max_biasP_kernel(
                 in_=words.bitcast(I32).rearrange("a p c -> p a c"),
             )
 
-        def load_scales(engine, t, scales, first):
-            rows = 4 * scales.shape[0]
+        def load_scales(t, scales, engine=nc.sync):
             for q in range(QUADS):
                 engine.dma_start(
-                    out=t[32 * q + first : 32 * q + first + rows, :].bitcast(I32),
-                    in_=scales[:, 4 * q : 4 * q + 4, :].bitcast(I32),
+                    out=t[32 * q : 32 * q + 4, :].bitcast(I32),
+                    in_=scales[0, 4 * q : 4 * q + 4, :].bitcast(I32),
                 )
 
         x_planes = []
@@ -117,11 +117,11 @@ def tile_list_htabg_max_biasP_kernel(
             )
         wgt_first = placed(at_wgt, "wgt_first", [P, split], F32)
         nc.sync.dma_start(out=wgt_first[:], in_=wgt2[:, 0:split])
+
+        wd_sc_raw = zeroed(nc.gpsimd, sb("wd_sc_raw", [P, R], U8))
+        load_scales(wd_sc_raw, wd_scales, nc.gpsimd)
         bias = sb("bias", [P, PACK], F32)
-        load_scales(nc.gpsimd, late_sc_raw, wa_scales, 0)
-        load_scales(nc.gpsimd, late_sc_raw, wd_scales, 4)
         nc.gpsimd.dma_start(out=bias[:], in_=b.rearrange("(p t) -> p t", t=PACK))
-        wd_sc = zeroed(nc.gpsimd, sb("wd_sc", [P, R], U8))
 
         def deal(dealt, raw, passes, dtype):
             nc.vector.tensor_copy(
@@ -138,16 +138,24 @@ def tile_list_htabg_max_biasP_kernel(
         nc.vector.tensor_copy(out=sc0[:], in_=tab_sc[:].indirect(tab_list[:]))
         nc.sync.dma_start(out=sc1[0:112, :].bitcast(I32), in_=sc0[16:128, :].bitcast(I32))
         load_plane(1)
+        wa_sc_raw = zeroed(nc.gpsimd, placed(at_x1 - R, "wa_sc_raw", [P, R], U8))
+        load_scales(wa_sc_raw, wa_scales)
         wb_sc = deal(sb("wb_sc", [P, 2 * R], U8), wb_sc_raw[:], 2, U8)
 
         yb = sb("yb", [P, J, PACK], BF16)
         picks = []
         for c in range(J // WIDE):
-            picked = sb(f"picked{c}", [P, WIDE], U32)
+            picked = placed(at_picked + c * 4 * WIDE, f"picked{c}", [P, WIDE], U32)
             nc.vector.tensor_copy(out=picked[:], in_=tab_w[:].bitcast(U32).indirect(tab_list[:, entries(c, WIDE)]))
             picks.append(picked)
         load_plane(2)
         load_plane(3)
+        wa_raw = placed(at_late, "wa_raw", [P, 2 * R], U8)
+        load_words(wa_raw[:], wa_words, 1)
+        wd_raw = placed(at_late + 2 * R, "wd_raw", [P, 2 * R], U8)
+        load_words(wd_raw[:], wd_words, 1)
+        wgt_rest = placed(at_late + 4 * R, "wgt_rest", [P, J - split], F32)
+        nc.sync.dma_start(out=wgt_rest[:], in_=wgt2[:, split:J])
         for c, picked in enumerate(picks):
             parted = slot(f"parted{c}", f"parted{c}", [P, 2 * 2 * WIDE], U8)
             nc.vector.tensor_copy(
@@ -168,17 +176,11 @@ def tile_list_htabg_max_biasP_kernel(
                         )
                 nc.scalar.activation(out=yb[:, cols(u, UNIT), :], in_=bank[:].rearrange("p t j -> p j t"), func=IDENTITY)
 
-        wa_raw = placed(at_late, "wa_raw", [P, 2 * R], U8)
-        load_words(wa_raw[:], wa_words, 1)
-        wd_raw = placed(at_late + 2 * R, "wd_raw", [P, 2 * R], U8)
-        load_words(wd_raw[:], wd_words, 1)
-        wa_w = deal(sb("wa", [P, 2 * R], U8), wa_raw[:], 1, U16)
-        wd_w = deal(sb("wd", [P, 2 * R], U8), wd_raw[:], 1, U16)
-        wgt_rest = placed(at_late + 4 * R, "wgt_rest", [P, J - split], F32)
-        nc.sync.dma_start(out=wgt_rest[:], in_=wgt2[:, split:J])
+        at_last = at_picked + 4 * WIDE
         starts = [sum(WIDTHS[:u]) for u in range(len(WIDTHS))]
         spans = [slice(s, s + w) for s, w in zip(starts, WIDTHS)]
-        x_il = [slot(f"x_il{u}", f"x_il{u}", [P, w, PACK], BF16) for u, w in enumerate(WIDTHS)]
+        at_il0 = at_last + 4 * WIDE
+        x_il = [placed(at_il0 + 2 * PACK * s.start, f"x_il{u}", [P, s.stop - s.start, PACK], BF16) for u, s in enumerate(spans)]
 
         def pick(g, i, span):
             origin = 0 if span.start < split else split
@@ -228,22 +230,24 @@ def tile_list_htabg_max_biasP_kernel(
         y_scales = sb("y_scales", [P, J], U8)
         y_rows = out_0.rearrange("(p t) j -> p t j", t=PACK)
         code_rows = out_1[0].rearrange("p j i -> p (j i)").bitcast(I32)
-        ya, h_il = {}, {}
+        ya, h_il, ys = {}, {}, {}
         y_il = sb("y_il", [P, J, PACK], BF16)
 
         wa = []
-        wd = (wd_w, wd_sc)
+        wd = []
 
         def stage_ya(u):
             if u == 0:
-                wa.extend((wa_w, deal(placed(at_wgt, "wa_sc", [P, R], U8), late_sc_raw[:], 1, U8)))
-                nc.sync.dma_start(out=wd_sc[0:112, :].bitcast(I32), in_=wa[1][4:116, :].bitcast(I32))
+                wa.append(deal(sb("wa", [P, 2 * R], U8), wa_raw[:], 1, U16))
+                wa.append(deal(sb("wa_sc", [P, R], U8), wa_sc_raw[:], 1, U8))
+                wd.append(deal(sb("wd", [P, 2 * R], U8), wd_raw[:], 1, U16))
+                wd.append(deal(placed(at_wgt, "wd_sc", [P, R], U8), wd_sc_raw[:], 1, U8))
             q = quantise(f"xq{u}", x_il[u], WIDTHS[u])
             ya[u] = [project("ya_bank", 3, wa, q, s) for s in range(WIDTHS[u] // UNIT)]
 
         def stage_max(u):
             h_il[u] = sb(f"h_il{u}", [P, WIDTHS[u], PACK], BF16)
-            if u < STAGED:
+            if u in STAGED:
                 staged = sb(f"ya{u}", [P, WIDTHS[u], PACK], BF16)
                 for s, bank in enumerate(ya[u]):
                     nc.scalar.copy(out=staged[:, cols(s, UNIT), :], in_=bank[:].rearrange("p t j -> p j t"))
@@ -270,11 +274,19 @@ def tile_list_htabg_max_biasP_kernel(
                 for e in range(per_bank):
                     t = k * per_bank + e
                     nc.scalar.activation(out=y[:, t, :], in_=bank[:, e, :], func=IDENTITY, bias=bias[:, t : t + 1])
-            nc.sync.dma_start(out=y_rows[:, :, spans[u]], in_=y[:])
-            parts = 2 if u < AHEAD else 1
+                if u < 2:
+                    rows = cols(k, per_bank)
+                    nc.sync.dma_start(out=y_rows[:, rows, spans[u]], in_=y[:, rows, :])
+            if u >= 2:
+                nc.sync.dma_start(out=y_rows[:, :, spans[u]], in_=y[:])
+            ys[u] = y
+
+        def stage_weave(u):
+            y, width = ys[u], WIDTHS[u]
+            parts = 2 if WOVEN <= u < AHEAD else 1
             for h in range(parts):
                 half = cols(h, width // parts)
-                nc.vector.tensor_copy(
+                (nc.scalar.copy if u < WOVEN else nc.vector.tensor_copy)(
                     out=y_il[:, spans[u], :][:, half, :].rearrange("p (c i) t -> p c t i", i=PACK),
                     in_=y[:, :, half].rearrange("p t (c i) -> p c t i", i=PACK),
                 )
@@ -286,18 +298,16 @@ def tile_list_htabg_max_biasP_kernel(
             )
 
         def stage_planes(u):
-            ends = [s.stop - (UNIT if v < AHEAD else 0) for v, s in enumerate(spans)]
+            ends = [s.stop - (UNIT if WOVEN <= v < AHEAD else 0) for v, s in enumerate(spans)]
             window = slice(ends[u - 1] if u else 0, ends[u])
             planes(window)
             if u in (1, 2, 4):
                 stored = slice({1: 0, 2: ends[1], 4: ends[2]}[u], ends[u])
                 nc.sync.dma_start(out=code_rows[:, stored], in_=y_codes[:, stored])
 
-        stages = (stage_pick, stage_ya, stage_max, stage_y, stage_planes)
-        for step in range(len(WIDTHS) + len(stages) - 1):
-            for lag, stage in enumerate(stages):
-                if 0 <= step - lag < len(WIDTHS):
-                    stage(step - lag)
+        order = ((stage_pick, 0), (stage_pick, 1), (stage_ya, 0), (stage_max, 0), (stage_pick, 2), (stage_ya, 1), (stage_pick, 3), (stage_y, 0), (stage_ya, 2), (stage_max, 1), (stage_pick, 4), (stage_ya, 3), (stage_max, 2), (stage_y, 1), (stage_weave, 0), (stage_planes, 0), (stage_ya, 4), (stage_max, 3), (stage_y, 2), (stage_weave, 1), (stage_planes, 1), (stage_max, 4), (stage_y, 3), (stage_weave, 2), (stage_planes, 2), (stage_y, 4), (stage_weave, 3), (stage_planes, 3), (stage_weave, 4), (stage_planes, 4))
+        for stage, u in order:
+            stage(u)
 
         for q in range(QUADS):
             (nc.sync, nc.scalar)[q % 2].dma_start(

@@ -19,13 +19,18 @@ IDENTITY = mybir.ActivationFunctionType.Identity
 P = 128
 PACK = 4
 QUADS = 4
-UNIT = 128
-UNITS = J // UNIT
-WIDE = 512
-AHEAD = 3
-STAGED = (0, 2,)
-WOVEN = 0
+GROUP = 16
+BANK = 512
+UNIT = BANK // PACK
+HALF = J // 2
+EDGE = 64
+
 WIDTHS = (256, 256, 256, 128, 128)
+AHEAD = 3
+STAGED = (0, 2)
+EARLY = 2
+CODE_STORES = (1, 2, 4)
+YA_BANKS, Y_BANKS = 3, 5
 
 
 def tile_list_htabg_max_biasP_kernel(
@@ -38,276 +43,259 @@ def tile_list_htabg_max_biasP_kernel(
         arena = ctx.enter_context(tc.tile_pool(name="arena", bufs=1))
         psum = ctx.enter_context(tc.psum_pool(name="psum", bufs=1))
 
-        def sb(name, shape, dtype):
-            return keep.tile(shape, dtype, name=name, align_bytes=64)
-
-        def cols(i, width):
-            return slice(i * width, (i + 1) * width)
-
-        def entries(i, width):
-            return slice(i * width // 16, (i + 1) * width // 16)
-
-        tab_list = keep.tile([P, J // 16], U16, name="tab_list")
-        head_lists = keep.tile([P, J // 16], U16, name="head_lists")
-
-        def slot(tag, name, shape, dtype):
-            return keep.tile(shape, dtype, name=name, tag=tag, align_bytes=64)
+        def sb(name, shape, dtype, tag=None):
+            return keep.tile(shape, dtype, name=name, tag=tag or name, align_bytes=64)
 
         def placed(offset, name, shape, dtype):
             return arena.tile(shape, dtype, name=name, offset=offset, align_bytes=64)
 
-        def zeroed(engine, t):
-            engine.memset(t[:].bitcast(I32), 0)
-            return t
+        def zeroed(engine, tile):
+            engine.memset(tile[:].bitcast(I32), 0)
+            return tile
+
+        def cols(i, width):
+            return slice(i * width, (i + 1) * width)
+
+        def entries(span):
+            return slice(span.start // GROUP, span.stop // GROUP)
+
+        starts = [sum(WIDTHS[:u]) for u in range(len(WIDTHS))]
+        spans = [slice(s, s + w) for s, w in zip(starts, WIDTHS)]
+        split = starts[AHEAD]
 
         plane_bytes = 4 * T
-        split = sum(WIDTHS[:AHEAD])
-        at_x2 = 0
-        at_tab = plane_bytes - 64
-        at_late = plane_bytes
-        at_x3 = at_tab + plane_bytes - 64
-        at_wgt = at_x3 + plane_bytes
-        at_x0 = at_wgt + 4 * split
-        at_x1 = at_x0 + plane_bytes + R
-        at_picked = at_x1 + plane_bytes
-        at_zeros = at_x3 - 64
-        tab_sc = zeroed(nc.vector, placed(at_x1 - R, "tab_sc", [P, T], U8))
-        zeros = placed(at_zeros, "zeros", [P, at_x0 + 64 - at_zeros], U8)
-        nc.gpsimd.memset(zeros[:, 0:J].bitcast(I32), 0)
-        sc1 = sb("sc1", [P, J], U8)
-        nc.vector.tensor_copy(out=sc1[:].bitcast(I32), in_=zeros[:, 0:J].bitcast(I32))
-        tab_w = placed(at_tab, "tab_w", [P, T], I32)
-        wb_sc_raw = zeroed(nc.vector, sb("wb_sc_raw", [P, 2 * R], U8))
+        at_x0 = 0
+        at_tab = at_x0 + plane_bytes
+        at_zeros = at_tab - J // 2
+        at_late = at_tab + J
+        at_x3 = at_tab + plane_bytes - EDGE
+        at_x1 = at_x3 + plane_bytes
+        at_wa_sc = at_x1 + plane_bytes
+        at_tab_sc = at_wa_sc - EDGE
+        at_bias = at_wa_sc + R
+        at_x2 = at_bias + EDGE
+        at_wgt = at_x2 + plane_bytes
+        at_picked = at_wgt + 4 * split
+        at_parted = at_picked + 4 * J
+        at_woven = at_parted + 4 * J
 
-        def load_words(t, words, passes):
+        tab_list = keep.tile([P, J // GROUP], U16, name="tab_list")
+        head_lists = keep.tile([P, J // GROUP], U16, name="head_lists")
+        tab_sc = zeroed(nc.vector, placed(at_tab_sc, "tab_sc", [P, T], U8))
+        zeros = zeroed(nc.gpsimd, placed(at_zeros, "zeros", [P, J], U8))
+        sc1 = sb("sc1", [P, J], U8)
+        nc.vector.tensor_copy(out=sc1[:].bitcast(I32), in_=zeros[:].bitcast(I32))
+        wb_sc_raw = zeroed(nc.vector, placed(at_parted + 4 * HALF, "wb_sc_raw", [P, 2 * R], U8))
+
+        def load_words(tile, words):
             nc.sync.dma_start(
-                out=t.bitcast(I32).rearrange("p (a c) -> p a c", a=passes),
+                out=tile[:].bitcast(I32).rearrange("p (a c) -> p a c", a=words.shape[0]),
                 in_=words.bitcast(I32).rearrange("a p c -> p a c"),
             )
+            return tile
 
-        def load_scales(t, scales, engine=nc.sync):
+        def load_scales(tile, scales):
             for q in range(QUADS):
-                engine.dma_start(
-                    out=t[32 * q : 32 * q + 4, :].bitcast(I32),
-                    in_=scales[0, 4 * q : 4 * q + 4, :].bitcast(I32),
+                nc.sync.dma_start(
+                    out=tile[32 * q : 32 * q + 4, :].bitcast(I32).rearrange("r (a c) -> r a c", a=scales.shape[0]),
+                    in_=scales[:, 4 * q : 4 * q + 4, :].bitcast(I32).rearrange("a r c -> r a c"),
                 )
+            return tile
 
-        x_planes = []
-
-        def load_plane(i):
-            plane = placed((at_x0, at_x1, at_x2, at_x3)[i], f"x{i}", [P, T], F32)
+        def load_plane(i, offset):
+            plane = placed(offset, f"x{i}", [P, T], F32)
             nc.sync.dma_start(out=plane[:], in_=xT.rearrange("(p i) t -> p i t", i=PACK)[:, i, :])
-            x_planes.append(plane)
+            return plane
 
-        nc.sync.dma_start(tab_list[:], offs)
-        nc.sync.dma_start(head_lists[:], offs2)
-        wb_raw = sb("wb_raw", [P, 2 * 2 * R], U8)
-        load_words(wb_raw[:], wb_words, 2)
-        for r in range(4):
-            nc.sync.dma_start(
-                out=tab_sc[r:P:16, :].bitcast(I32),
-                in_=tab_scales.bitcast(I32).rearrange("a (q r) c -> r q a c", r=4)[r],
-            )
-        nc.sync.dma_start(out=tab_w[:], in_=tab_words[0].rearrange("p t b -> p (t b)").bitcast(I32))
-        load_plane(0)
-        for q in range(QUADS):
-            nc.sync.dma_start(
-                out=wb_sc_raw[32 * q : 32 * q + 4, :].bitcast(I32).rearrange("r (a c) -> r a c", a=2),
-                in_=wb_scales[:, 4 * q : 4 * q + 4, :].bitcast(I32).rearrange("a r c -> r a c"),
-            )
-        wgt_first = placed(at_wgt, "wgt_first", [P, split], F32)
-        nc.sync.dma_start(out=wgt_first[:], in_=wgt2[:, 0:split])
-
-        wd_sc_raw = zeroed(nc.gpsimd, sb("wd_sc_raw", [P, R], U8))
-        load_scales(wd_sc_raw, wd_scales, nc.gpsimd)
-        bias = sb("bias", [P, PACK], F32)
-        nc.gpsimd.dma_start(out=bias[:], in_=b.rearrange("(p t) -> p t", t=PACK))
+        def load_weights(offset, name, span):
+            tile = placed(offset, name, [P, span.stop - span.start], F32)
+            nc.sync.dma_start(out=tile[:], in_=wgt2[:, span])
+            return tile
 
         def deal(dealt, raw, passes, dtype):
             nc.vector.tensor_copy(
                 out=dealt[:].bitcast(dtype).rearrange("p (a t m) -> p a t m", a=passes, t=PACK),
-                in_=raw.bitcast(dtype).rearrange("p (a m t) -> p a t m", a=passes, t=PACK),
+                in_=raw[:].bitcast(dtype).rearrange("p (a m t) -> p a t m", a=passes, t=PACK),
             )
             return dealt
 
         def stationary(words, scales, t):
             return dict(lhsT=words[:, cols(t, 2 * P)].bitcast(FP4X4), lhsT_scale=scales[:, cols(t, P)])
 
-        wb = deal(sb("wb", [P, 4 * R], U8), wb_raw[:], 2, U16)
+        nc.sync.dma_start(tab_list[:], offs)
+        nc.sync.dma_start(head_lists[:], offs2)
+        wb_raw = load_words(placed(at_wgt, "wb_raw", [P, 2 * 2 * R], U8), wb_words)
+        for r in range(4):
+            nc.sync.dma_start(
+                out=tab_sc[r:P:16, :].bitcast(I32),
+                in_=tab_scales.bitcast(I32).rearrange("a (q r) c -> r q a c", r=4)[r],
+            )
+        tab_w = placed(at_tab, "tab_w", [P, T], I32)
+        nc.sync.dma_start(out=tab_w[:], in_=tab_words[0].rearrange("p t b -> p (t b)").bitcast(I32))
+        x_planes = [load_plane(0, at_x0)]
+        load_scales(wb_sc_raw, wb_scales)
+
+        wb = deal(sb("wb", [P, 2 * 2 * R], U8), wb_raw, 2, U16)
+        wgt_first = load_weights(at_wgt, "wgt_first", slice(0, split))
         sc0 = sb("sc0", [P, J], U8)
         nc.vector.tensor_copy(out=sc0[:], in_=tab_sc[:].indirect(tab_list[:]))
-        nc.sync.dma_start(out=sc1[0:112, :].bitcast(I32), in_=sc0[16:128, :].bitcast(I32))
-        load_plane(1)
-        wa_sc_raw = zeroed(nc.gpsimd, placed(at_x1 - R, "wa_sc_raw", [P, R], U8))
-        load_scales(wa_sc_raw, wa_scales)
-        wb_sc = deal(sb("wb_sc", [P, 2 * R], U8), wb_sc_raw[:], 2, U8)
+        nc.sync.dma_start(out=sc1[0 : P - 16, :].bitcast(I32), in_=sc0[16:P, :].bitcast(I32))
+        x_planes.append(load_plane(1, at_x1))
+        x_planes.append(load_plane(2, at_x2))
+        wa_sc_raw = load_scales(zeroed(nc.gpsimd, placed(at_wa_sc, "wa_sc_raw", [P, R], U8)), wa_scales)
+        bias = placed(at_bias, "bias", [P, PACK], F32)
+        nc.sync.dma_start(out=bias[:], in_=b.rearrange("(p t) -> p t", t=PACK))
+        wb_sc = deal(sb("wb_sc", [P, 2 * R], U8), wb_sc_raw, 2, U8)
+
+        picked = [placed(at_picked + 4 * HALF * c, f"picked{c}", [P, HALF], U32) for c in range(2)]
+        for c in range(2):
+            nc.vector.tensor_copy(out=picked[c][:], in_=tab_w[:].bitcast(U32).indirect(tab_list[:, entries(cols(c, HALF))]))
+        x_planes.append(load_plane(3, at_x3))
+        wa_raw = load_words(placed(at_late, "wa_raw", [P, 2 * R], U8), wa_words)
+        wgt_rest = load_weights(at_late + 2 * R, "wgt_rest", slice(split, J))
+        wd_raw = load_words(placed(at_late + 2 * R + 4 * (J - split), "wd_raw", [P, 2 * R], U8), wd_words)
 
         yb = sb("yb", [P, J, PACK], BF16)
-        picks = []
-        for c in range(J // WIDE):
-            picked = placed(at_picked + c * 4 * WIDE, f"picked{c}", [P, WIDE], U32)
-            nc.vector.tensor_copy(out=picked[:], in_=tab_w[:].bitcast(U32).indirect(tab_list[:, entries(c, WIDE)]))
-            picks.append(picked)
-        load_plane(2)
-        load_plane(3)
-        wa_raw = placed(at_late, "wa_raw", [P, 2 * R], U8)
-        load_words(wa_raw[:], wa_words, 1)
-        wd_raw = placed(at_late + 2 * R, "wd_raw", [P, 2 * R], U8)
-        load_words(wd_raw[:], wd_words, 1)
-        wgt_rest = placed(at_late + 4 * R, "wgt_rest", [P, J - split], F32)
-        nc.sync.dma_start(out=wgt_rest[:], in_=wgt2[:, split:J])
-        for c, picked in enumerate(picks):
-            parted = slot(f"parted{c}", f"parted{c}", [P, 2 * 2 * WIDE], U8)
+        for c in range(2):
+            parted = placed(at_parted + 4 * HALF * c, f"parted{c}", [P, 2 * 2 * HALF], U8)
             nc.vector.tensor_copy(
-                out=parted[:].bitcast(U16).rearrange("p (d j) -> p d j", d=2),
-                in_=picked[:].bitcast(U16).rearrange("p (j d) -> p d j", d=2),
+                out=parted[:].bitcast(U16).rearrange("p (a j) -> p a j", a=2),
+                in_=picked[c][:].bitcast(U16).rearrange("p (j a) -> p a j", a=2),
             )
-            for s in range(WIDE // UNIT):
-                u = c * (WIDE // UNIT) + s
-                bank = psum.tile([P, PACK, UNIT], F32, name="yb_bank", tag="y_bank", bufs=5)
+            for s in range(HALF // UNIT):
+                places = cols(c * (HALF // UNIT) + s, UNIT)
+                bank = psum.tile([P, PACK, UNIT], F32, name="yb_bank", tag="y_bank", bufs=Y_BANKS)
                 for t in range(PACK):
                     for a in (1, 0):
                         nc.tensor.matmul_mx(
                             out=bank[:, t, :],
-                            rhs=parted[:, cols(a * (WIDE // UNIT) + s, 2 * UNIT)].bitcast(FP4X4),
-                            rhs_scale=(sc0, sc1)[a][:, cols(u, UNIT)],
+                            rhs=parted[:, cols(a * (HALF // UNIT) + s, 2 * UNIT)].bitcast(FP4X4),
+                            rhs_scale=(sc0, sc1)[a][:, places],
                             start=(a == 1), stop=(a == 0),
                             **stationary(wb[:, cols(a, 2 * R)], wb_sc[:, cols(a, R)], t),
                         )
-                nc.scalar.activation(out=yb[:, cols(u, UNIT), :], in_=bank[:].rearrange("p t j -> p j t"), func=IDENTITY)
-
-        at_last = at_picked + 4 * WIDE
-        starts = [sum(WIDTHS[:u]) for u in range(len(WIDTHS))]
-        spans = [slice(s, s + w) for s, w in zip(starts, WIDTHS)]
-        at_il0 = at_last + 4 * WIDE
-        x_il = [placed(at_il0 + 2 * PACK * s.start, f"x_il{u}", [P, s.stop - s.start, PACK], BF16) for u, s in enumerate(spans)]
+                nc.scalar.activation(out=yb[:, places, :], in_=bank[:].rearrange("p t j -> p j t"), func=IDENTITY)
+        wd_sc_raw = load_scales(zeroed(nc.gpsimd, placed(at_picked + 4 * HALF, "wd_sc_raw", [P, R], U8)), wd_scales)
 
         def pick(g, i, span):
-            origin = 0 if span.start < split else split
+            weights, origin = (wgt_first, 0) if span.start < split else (wgt_rest, split)
             nc.vector.tensor_tensor(
-                g,
-                x_planes[i][:].indirect(head_lists[:, span.start // 16 : span.stop // 16]),
-                (wgt_first if origin == 0 else wgt_rest)[:, span.start - origin : span.stop - origin], ALU.mult,
+                g, x_planes[i][:].indirect(head_lists[:, entries(span)]),
+                weights[:, span.start - origin : span.stop - origin], ALU.mult,
             )
 
-        ring_width = max(WIDTHS[0], J - split)
-        g_first = slot("g_ring", "g_first", [P, PACK, ring_width], F32)
-        g_next = sb("g_next", [P, PACK, split - WIDTHS[0]], F32)
-        for i in range(PACK - 1):
-            pick(g_first[:, i, 0 : WIDTHS[0]], i, spans[0])
-            pick(g_next[:, i, :], i, slice(WIDTHS[0], split))
-        late = []
-
-        def stage_pick(u):
-            if u == AHEAD:
-                late.append(slot("g_ring", "g_late", [P, PACK, ring_width], F32))
-                for i in range(PACK - 1):
-                    pick(late[0][:, i, 0 : J - split], i, slice(split, J))
-            g, origin = (g_first, 0) if u == 0 else (g_next, WIDTHS[0]) if u < AHEAD else (late[0], split)
-            local = slice(spans[u].start - origin, spans[u].stop - origin)
-            pick(g[:, PACK - 1, local], PACK - 1, spans[u])
-            nc.scalar.copy(
-                out=x_il[u][:].rearrange("p (c i) t -> p c t i", i=PACK),
-                in_=g[:, :, local].rearrange("p t (c i) -> p c t i", i=PACK),
+        def weave(copy, woven, planar):
+            copy(
+                out=woven.rearrange("p (c i) t -> p c t i", i=PACK),
+                in_=planar.rearrange("p t (c i) -> p c t i", i=PACK),
             )
 
-        def quantise(name, src, width):
+        def quantise(codes, scales, woven):
+            nc.vector.quantize_mx(out=codes.bitcast(FP8X4), scales=scales, in_=woven.rearrange("p j t -> p (j t)"))
+
+        def quantised(name, woven, width):
             codes = sb(name, [P, width], U32)
             scales = sb(name + "_sc", [P, width], U8)
-            nc.vector.quantize_mx(out=codes[:].bitcast(FP8X4), scales=scales[:], in_=src[:].rearrange("p j t -> p (j t)"))
+            quantise(codes[:], scales[:], woven[:])
             return codes, scales
 
-        def project(name, bufs, w, q, s):
-            bank = psum.tile([P, PACK, UNIT], F32, name=name, bufs=bufs)
-            for t in range(PACK):
-                nc.tensor.matmul_mx(
-                    out=bank[:, t, :], rhs=q[0][:, cols(s, UNIT)].bitcast(FP8X4), rhs_scale=q[1][:, cols(s, UNIT)],
-                    start=True, stop=True, **stationary(*w, t),
-                )
-            return bank
+        g_first = sb("g_first", [P, PACK, WIDTHS[0]], F32, tag="g_ring")
+        g_next = sb("g_next", [P, PACK, split - WIDTHS[0]], F32)
+        for i in range(PACK - 1):
+            pick(g_first[:, i, :], i, spans[0])
+            pick(g_next[:, i, :], i, slice(WIDTHS[0], split))
+        batches = {u: (g_next, WIDTHS[0]) for u in range(1, AHEAD)}
+        batches[0] = (g_first, 0)
 
+        x_woven = [placed(at_woven + 2 * PACK * s, f"x_woven{u}", [P, w, PACK], BF16) for u, (s, w) in enumerate(zip(starts, WIDTHS))]
+        y_woven = sb("y_woven", [P, J, PACK], BF16)
         y_codes = sb("y_codes", [P, J], I32)
         y_scales = sb("y_scales", [P, J], U8)
         y_rows = out_0.rearrange("(p t) j -> p t j", t=PACK)
         code_rows = out_1[0].rearrange("p j i -> p (j i)").bitcast(I32)
-        ya, h_il, ys = {}, {}, {}
-        y_il = sb("y_il", [P, J, PACK], BF16)
+        weights, ya, h_woven, y = {}, {}, {}, {}
 
-        wa = []
-        wd = []
+        def stage_pick(u):
+            if u == AHEAD:
+                g_late = sb("g_late", [P, PACK, J - split], F32, tag="g_ring")
+                for i in range(PACK - 1):
+                    pick(g_late[:, i, :], i, slice(split, J))
+                for v in range(AHEAD, len(WIDTHS)):
+                    batches[v] = (g_late, split)
+            g, origin = batches[u]
+            local = slice(spans[u].start - origin, spans[u].stop - origin)
+            pick(g[:, PACK - 1, local], PACK - 1, spans[u])
+            weave(nc.scalar.copy, x_woven[u][:], g[:, :, local])
 
         def stage_ya(u):
             if u == 0:
-                wa.append(deal(sb("wa", [P, 2 * R], U8), wa_raw[:], 1, U16))
-                wa.append(deal(sb("wa_sc", [P, R], U8), wa_sc_raw[:], 1, U8))
-                wd.append(deal(sb("wd", [P, 2 * R], U8), wd_raw[:], 1, U16))
-                wd.append(deal(placed(at_wgt, "wd_sc", [P, R], U8), wd_sc_raw[:], 1, U8))
-            q = quantise(f"xq{u}", x_il[u], WIDTHS[u])
-            ya[u] = [project("ya_bank", 3, wa, q, s) for s in range(WIDTHS[u] // UNIT)]
+                weights["wa"] = (deal(sb("wa", [P, 2 * R], U8), wa_raw, 1, U16), deal(sb("wa_sc", [P, R], U8), wa_sc_raw, 1, U8))
+            codes, scales = quantised(f"xq{u}", x_woven[u], WIDTHS[u])
+            ya[u] = []
+            for s in range(WIDTHS[u] // UNIT):
+                bank = psum.tile([P, PACK, UNIT], F32, name="ya_bank", bufs=YA_BANKS)
+                for t in range(PACK):
+                    nc.tensor.matmul_mx(
+                        out=bank[:, t, :], rhs=codes[:, cols(s, UNIT)].bitcast(FP8X4), rhs_scale=scales[:, cols(s, UNIT)],
+                        start=True, stop=True, **stationary(*weights["wa"], t),
+                    )
+                ya[u].append(bank[:].rearrange("p t j -> p j t"))
 
         def stage_max(u):
-            h_il[u] = sb(f"h_il{u}", [P, WIDTHS[u], PACK], BF16)
+            h_woven[u] = sb(f"h_woven{u}", [P, WIDTHS[u], PACK], BF16)
             if u in STAGED:
                 staged = sb(f"ya{u}", [P, WIDTHS[u], PACK], BF16)
                 for s, bank in enumerate(ya[u]):
-                    nc.scalar.copy(out=staged[:, cols(s, UNIT), :], in_=bank[:].rearrange("p t j -> p j t"))
-                nc.vector.tensor_tensor(h_il[u][:], staged[:], yb[:, spans[u], :], ALU.max)
+                    nc.scalar.copy(out=staged[:, cols(s, UNIT), :], in_=bank)
+                nc.vector.tensor_tensor(h_woven[u][:], staged[:], yb[:, spans[u], :], ALU.max)
             else:
                 for s, bank in enumerate(ya[u]):
                     nc.vector.tensor_tensor(
-                        h_il[u][:, cols(s, UNIT), :], bank[:].rearrange("p t j -> p j t"),
-                        yb[:, cols(starts[u] // UNIT + s, UNIT), :], ALU.max,
+                        h_woven[u][:, cols(s, UNIT), :], bank, yb[:, spans[u], :][:, cols(s, UNIT), :], ALU.max,
                     )
 
         def stage_y(u):
-            q = quantise(f"hq{u}", h_il[u], WIDTHS[u])
-            y = sb(f"y{u}", [P, PACK, WIDTHS[u]], F32)
-            width = WIDTHS[u]
-            per_bank = 512 // width
-            for k in range(PACK // per_bank):
-                bank = psum.tile([P, per_bank, width], F32, name="y_bank", tag="y_bank", bufs=5)
-                for e in range(per_bank):
-                    nc.tensor.matmul_mx(
-                        out=bank[:, e, :], rhs=q[0][:].bitcast(FP8X4), rhs_scale=q[1][:],
-                        start=True, stop=True, **stationary(*wd, k * per_bank + e),
-                    )
-                for e in range(per_bank):
-                    t = k * per_bank + e
-                    nc.scalar.activation(out=y[:, t, :], in_=bank[:, e, :], func=IDENTITY, bias=bias[:, t : t + 1])
-                if u < 2:
-                    rows = cols(k, per_bank)
-                    nc.sync.dma_start(out=y_rows[:, rows, spans[u]], in_=y[:, rows, :])
-            if u >= 2:
-                nc.sync.dma_start(out=y_rows[:, :, spans[u]], in_=y[:])
-            ys[u] = y
-
-        def stage_weave(u):
-            y, width = ys[u], WIDTHS[u]
-            parts = 2 if WOVEN <= u < AHEAD else 1
-            for h in range(parts):
-                half = cols(h, width // parts)
-                (nc.scalar.copy if u < WOVEN else nc.vector.tensor_copy)(
-                    out=y_il[:, spans[u], :][:, half, :].rearrange("p (c i) t -> p c t i", i=PACK),
-                    in_=y[:, :, half].rearrange("p t (c i) -> p c t i", i=PACK),
+            if u == 0:
+                weights["wd"] = (
+                    deal(placed(at_woven, "wd", [P, 2 * R], U8), wd_raw, 1, U16),
+                    deal(placed(at_woven + 2 * R, "wd_sc", [P, R], U8), wd_sc_raw, 1, U8),
                 )
+            width = WIDTHS[u]
+            codes, scales = quantised(f"hq{u}", h_woven[u], width)
+            y[u] = sb(f"y{u}", [P, PACK, width], F32)
+            per_bank = BANK // width
+            for k in range(PACK // per_bank):
+                rows = range(PACK)[cols(k, per_bank)]
+                bank = psum.tile([P, per_bank, width], F32, name="y_bank", tag="y_bank", bufs=Y_BANKS)
+                for e, t in enumerate(rows):
+                    nc.tensor.matmul_mx(
+                        out=bank[:, e, :], rhs=codes[:].bitcast(FP8X4), rhs_scale=scales[:],
+                        start=True, stop=True, **stationary(*weights["wd"], t),
+                    )
+                for e, t in enumerate(rows):
+                    nc.scalar.activation(out=y[u][:, t, :], in_=bank[:, e, :], func=IDENTITY, bias=bias[:, t : t + 1])
+                if u < EARLY:
+                    nc.sync.dma_start(out=y_rows[:, cols(k, per_bank), spans[u]], in_=y[u][:, cols(k, per_bank), :])
+            if u >= EARLY:
+                nc.sync.dma_start(out=y_rows[:, :, spans[u]], in_=y[u][:])
 
-        def planes(span):
-            nc.vector.quantize_mx(
-                out=y_codes[:, span].bitcast(FP8X4), scales=y_scales[:, span],
-                in_=y_il[:, span, :].rearrange("p j t -> p (j t)"),
-            )
+        ends = [span.stop - (UNIT if width > UNIT else 0) for span, width in zip(spans, WIDTHS)]
 
-        def stage_planes(u):
-            ends = [s.stop - (UNIT if WOVEN <= v < AHEAD else 0) for v, s in enumerate(spans)]
+        def stage_out(u):
+            for s in range(WIDTHS[u] // UNIT):
+                weave(nc.vector.tensor_copy, y_woven[:, spans[u], :][:, cols(s, UNIT), :], y[u][:, :, cols(s, UNIT)])
             window = slice(ends[u - 1] if u else 0, ends[u])
-            planes(window)
-            if u in (1, 2, 4):
-                stored = slice({1: 0, 2: ends[1], 4: ends[2]}[u], ends[u])
+            quantise(y_codes[:, window], y_scales[:, window], y_woven[:, window, :])
+            if u in CODE_STORES:
+                before = [ends[v] for v in CODE_STORES if v < u]
+                stored = slice(max(before, default=0), ends[u])
                 nc.sync.dma_start(out=code_rows[:, stored], in_=y_codes[:, stored])
 
-        order = ((stage_pick, 0), (stage_pick, 1), (stage_ya, 0), (stage_max, 0), (stage_pick, 2), (stage_ya, 1), (stage_pick, 3), (stage_y, 0), (stage_ya, 2), (stage_max, 1), (stage_pick, 4), (stage_ya, 3), (stage_max, 2), (stage_y, 1), (stage_weave, 0), (stage_planes, 0), (stage_ya, 4), (stage_max, 3), (stage_y, 2), (stage_weave, 1), (stage_planes, 1), (stage_max, 4), (stage_y, 3), (stage_weave, 2), (stage_planes, 2), (stage_y, 4), (stage_weave, 3), (stage_planes, 3), (stage_weave, 4), (stage_planes, 4))
-        for stage, u in order:
-            stage(u)
+        stages = ((stage_pick, 0), (stage_ya, 1), (stage_max, 1), (stage_y, 3), (stage_out, 4))
+        for step in range(len(WIDTHS) + stages[-1][1]):
+            for stage, lag in stages:
+                if 0 <= step - lag < len(WIDTHS):
+                    stage(step - lag)
 
         for q in range(QUADS):
             (nc.sync, nc.scalar)[q % 2].dma_start(

@@ -1,6 +1,7 @@
 from contextlib import ExitStack
 
 import concourse.mybir as mybir
+from concourse.masks import make_identity
 
 K, L, R, N, T, J = 512, 1024, 512, 512, 2048, 1024
 FLOPS = 2 * J * (K * R + L * R + R * N)
@@ -30,7 +31,8 @@ AHEAD = 3
 STAGED = (0, 2)
 EARLY = 2
 CODE_STORES = (1, 2, 4)
-YA_BANKS, Y_BANKS = 3, 5
+YA_AT = (6, 2, 4, 6, 7)
+Y_AT = (0, 2, 4, 6, 7)
 
 
 def tile_list_htabg_max_biasP_kernel(
@@ -53,6 +55,14 @@ def tile_list_htabg_max_biasP_kernel(
             engine.memset(tile[:].bitcast(I32), 0)
             return tile
 
+        taken = {}
+        names = []
+
+        def next_bank(kind, count):
+            taken[kind] = taken.get(kind, -1) + 1
+            names.append(kind)
+            return taken[kind] % count
+
         def cols(i, width):
             return slice(i * width, (i + 1) * width)
 
@@ -64,28 +74,18 @@ def tile_list_htabg_max_biasP_kernel(
         split = starts[AHEAD]
 
         plane_bytes = 4 * T
-        at_x0 = 0
-        at_tab = at_x0 + plane_bytes
-        at_zeros = at_tab - J // 2
-        at_late = at_tab + J
-        at_x3 = at_tab + plane_bytes - EDGE
-        at_x1 = at_x3 + plane_bytes
-        at_wa_sc = at_x1 + plane_bytes
-        at_tab_sc = at_wa_sc - EDGE
-        at_bias = at_wa_sc + R
-        at_x2 = at_bias + EDGE
-        at_wgt = at_x2 + plane_bytes
-        at_picked = at_wgt + 4 * split
-        at_parted = at_picked + 4 * J
-        at_woven = at_parted + 4 * J
+        at_wb_sc = 0
+        at_picked = at_wb_sc + R - EDGE
+        at_woven = at_picked + 4 * J + R
 
         tab_list = keep.tile([P, J // GROUP], U16, name="tab_list")
         head_lists = keep.tile([P, J // GROUP], U16, name="head_lists")
-        tab_sc = zeroed(nc.vector, placed(at_tab_sc, "tab_sc", [P, T], U8))
-        zeros = zeroed(nc.gpsimd, placed(at_zeros, "zeros", [P, J], U8))
-        sc1 = sb("sc1", [P, J], U8)
-        nc.vector.tensor_copy(out=sc1[:].bitcast(I32), in_=zeros[:].bitcast(I32))
-        wb_sc_raw = zeroed(nc.vector, placed(at_parted + 4 * HALF, "wb_sc_raw", [P, 2 * R], U8))
+        tab_sc = zeroed(nc.gpsimd, sb("tab_sc", [P, T], U8))
+        wb_sc_raw = zeroed(nc.vector, placed(at_wb_sc, "wb_sc_raw", [P, R], U8))
+        wb_sc1 = zeroed(nc.vector, sb("wb_sc1", [P, R], U8))
+        sc1 = zeroed(nc.vector, sb("sc1", [P, J], U8))
+        wad_sc_raw = zeroed(nc.vector, sb("wad_sc_raw", [P, R], U8))
+        wd_sc = zeroed(nc.vector, sb("wd_sc", [P, R], U8))
 
         def load_words(tile, words):
             nc.sync.dma_start(
@@ -94,23 +94,30 @@ def tile_list_htabg_max_biasP_kernel(
             )
             return tile
 
-        def load_scales(tile, scales):
+        def load_scales(tile, first, scales):
             for q in range(QUADS):
                 nc.sync.dma_start(
-                    out=tile[32 * q : 32 * q + 4, :].bitcast(I32).rearrange("r (a c) -> r a c", a=scales.shape[0]),
-                    in_=scales[:, 4 * q : 4 * q + 4, :].bitcast(I32).rearrange("a r c -> r a c"),
+                    out=tile[32 * q + first : 32 * q + first + 4, :].bitcast(I32),
+                    in_=scales[0, 4 * q : 4 * q + 4, :].bitcast(I32),
                 )
-            return tile
 
-        def load_plane(i, offset):
-            plane = placed(offset, f"x{i}", [P, T], F32)
+        def load_scale_pair(tile, scales):
+            for r in range(4):
+                nc.sync.dma_start(
+                    out=tile[r:P:16, :].bitcast(I32),
+                    in_=scales.bitcast(I32).rearrange("a (q r) c -> r q a c", r=4)[r],
+                )
+
+        def move_up(upper, pair):
+            nc.sync.dma_start(out=upper[0 : P - 16, :].bitcast(I32), in_=pair[16:P, :].bitcast(I32))
+
+        def load_plane(i):
+            plane = sb(f"x{i}", [P, T], F32)
             nc.sync.dma_start(out=plane[:], in_=xT.rearrange("(p i) t -> p i t", i=PACK)[:, i, :])
             return plane
 
-        def load_weights(offset, name, span):
-            tile = placed(offset, name, [P, span.stop - span.start], F32)
-            nc.sync.dma_start(out=tile[:], in_=wgt2[:, span])
-            return tile
+        def load_part(i, tokens):
+            nc.sync.dma_start(out=x_planes[i][:, tokens], in_=xT.rearrange("(p i) t -> p i t", i=PACK)[:, i, tokens])
 
         def deal(dealt, raw, passes, dtype):
             nc.vector.tensor_copy(
@@ -122,67 +129,79 @@ def tile_list_htabg_max_biasP_kernel(
         def stationary(words, scales, t):
             return dict(lhsT=words[:, cols(t, 2 * P)].bitcast(FP4X4), lhsT_scale=scales[:, cols(t, P)])
 
+        wb_raw = load_words(sb("wb_raw", [P, 2 * 2 * R], U8), wb_words)
         nc.sync.dma_start(tab_list[:], offs)
-        nc.sync.dma_start(head_lists[:], offs2)
-        wb_raw = load_words(placed(at_wgt, "wb_raw", [P, 2 * 2 * R], U8), wb_words)
-        for r in range(4):
-            nc.sync.dma_start(
-                out=tab_sc[r:P:16, :].bitcast(I32),
-                in_=tab_scales.bitcast(I32).rearrange("a (q r) c -> r q a c", r=4)[r],
-            )
-        tab_w = placed(at_tab, "tab_w", [P, T], I32)
+        wgt_rows = sb("wgt_rows", [P, P], F32)
+        nc.sync.dma_start(out=wgt_rows[:], in_=wgt2.rearrange("(g u) (c j) -> u g c j", u=8, j=P)[0])
+        load_scale_pair(tab_sc, tab_scales)
+        tab_w = sb("tab_w", [P, T], I32)
         nc.sync.dma_start(out=tab_w[:], in_=tab_words[0].rearrange("p t b -> p (t b)").bitcast(I32))
-        x_planes = [load_plane(0, at_x0)]
-        load_scales(wb_sc_raw, wb_scales)
+        load_scale_pair(wb_sc_raw, wb_scales)
 
+        x_planes = [load_plane(0)]
+        wad_raw = sb("wad_raw", [P, 2 * 2 * R], U8)
+        x_planes.append(sb("x1", [P, T], F32))
+        load_part(1, slice(0, T // 2))
+        nc.sync.dma_start(head_lists[:], offs2)
+        identity = sb("identity", [P, P], F32)
+        make_identity(nc, identity[:])
+        turned = psum.tile([P, P], F32, name="turned", offset=2048 * 7)
+        nc.tensor.transpose(turned[:], wgt_rows[:], identity[:])
+        spread = sb("spread", [P, J // P, 16, 8], F32)
+        nc.scalar.copy(out=spread[:], in_=turned[:].rearrange("j (g c) -> j c g", c=8).unsqueeze(3).to_broadcast([P, J // P, 16, 8]))
+        wgt = sb("wgt", [P, J], F32)
+        for k in range(J // BANK):
+            bank = psum.tile([P, PACK, P], F32, name=f"wgt_bank{k}", offset=2048 * (5 + k))
+            for c in range(PACK):
+                nc.tensor.transpose(bank[:, c, :], spread[:, PACK * k + c].rearrange("j g u -> j (g u)"), identity[:])
+            nc.scalar.copy(out=wgt[:, cols(k, BANK)], in_=bank[:].rearrange("p c j -> p (c j)"))
         wb = deal(sb("wb", [P, 2 * 2 * R], U8), wb_raw, 2, U16)
-        wgt_first = load_weights(at_wgt, "wgt_first", slice(0, split))
         sc0 = sb("sc0", [P, J], U8)
         nc.vector.tensor_copy(out=sc0[:], in_=tab_sc[:].indirect(tab_list[:]))
-        nc.sync.dma_start(out=sc1[0 : P - 16, :].bitcast(I32), in_=sc0[16:P, :].bitcast(I32))
-        x_planes.append(load_plane(1, at_x1))
-        x_planes.append(load_plane(2, at_x2))
-        wa_sc_raw = load_scales(zeroed(nc.gpsimd, placed(at_wa_sc, "wa_sc_raw", [P, R], U8)), wa_scales)
-        bias = placed(at_bias, "bias", [P, PACK], F32)
+        move_up(sc1, sc0)
+        wb_sc0 = deal(sb("wb_sc0", [P, R], U8), wb_sc_raw, 1, U8)
+        move_up(wb_sc1, wb_sc0)
+        load_part(1, slice(T // 2, T))
+        load_scales(wad_sc_raw, 0, wa_scales)
+        x_planes.append(load_plane(2))
+        load_scales(wad_sc_raw, 16, wd_scales)
+        x_planes.append(load_plane(3))
+        load_words(wad_raw[:, cols(0, 2 * R)], wa_words)
+        load_words(wad_raw[:, cols(1, 2 * R)], wd_words)
+        bias = sb("bias", [P, PACK], F32)
         nc.sync.dma_start(out=bias[:], in_=b.rearrange("(p t) -> p t", t=PACK))
-        wb_sc = deal(sb("wb_sc", [P, 2 * R], U8), wb_sc_raw, 2, U8)
-
-        picked = [placed(at_picked + 4 * HALF * c, f"picked{c}", [P, HALF], U32) for c in range(2)]
-        for c in range(2):
-            nc.vector.tensor_copy(out=picked[c][:], in_=tab_w[:].bitcast(U32).indirect(tab_list[:, entries(cols(c, HALF))]))
-        x_planes.append(load_plane(3, at_x3))
-        wa_raw = load_words(placed(at_late, "wa_raw", [P, 2 * R], U8), wa_words)
-        wgt_rest = load_weights(at_late + 2 * R, "wgt_rest", slice(split, J))
-        wd_raw = load_words(placed(at_late + 2 * R + 4 * (J - split), "wd_raw", [P, 2 * R], U8), wd_words)
 
         yb = sb("yb", [P, J, PACK], BF16)
+        picked = placed(at_picked, "picked", [P, J], U32)
         for c in range(2):
-            parted = placed(at_parted + 4 * HALF * c, f"parted{c}", [P, 2 * 2 * HALF], U8)
+            half = cols(c, HALF)
+            nc.vector.tensor_copy(out=picked[:, half], in_=tab_w[:].bitcast(U32).indirect(tab_list[:, entries(half)]))
+
+        def table_half(c):
+            parted = sb(f"parted{c}", [P, 2 * 2 * HALF], U8)
             nc.vector.tensor_copy(
                 out=parted[:].bitcast(U16).rearrange("p (a j) -> p a j", a=2),
-                in_=picked[c][:].bitcast(U16).rearrange("p (j a) -> p a j", a=2),
+                in_=picked[:, cols(c, HALF)].bitcast(U16).rearrange("p (j a) -> p a j", a=2),
             )
             for s in range(HALF // UNIT):
                 places = cols(c * (HALF // UNIT) + s, UNIT)
-                bank = psum.tile([P, PACK, UNIT], F32, name="yb_bank", tag="y_bank", bufs=Y_BANKS)
-                for t in range(PACK):
-                    for a in (1, 0):
+                bank = psum.tile([P, PACK, UNIT], F32, name=f"yb_bank{len(names)}", offset=2048 * next_bank("yb", 5))
+                for a in (1, 0):
+                    for t in range(PACK):
                         nc.tensor.matmul_mx(
                             out=bank[:, t, :],
                             rhs=parted[:, cols(a * (HALF // UNIT) + s, 2 * UNIT)].bitcast(FP4X4),
                             rhs_scale=(sc0, sc1)[a][:, places],
-                            start=(a == 1), stop=(a == 0),
-                            **stationary(wb[:, cols(a, 2 * R)], wb_sc[:, cols(a, R)], t),
+                            start=(a == 1 and t == 0), stop=(a == 0 and t == PACK - 1),
+                            **stationary(wb[:, cols(a, 2 * R)], (wb_sc0, wb_sc1)[a], t),
                         )
                 nc.scalar.activation(out=yb[:, places, :], in_=bank[:].rearrange("p t j -> p j t"), func=IDENTITY)
-        wd_sc_raw = load_scales(zeroed(nc.gpsimd, placed(at_picked + 4 * HALF, "wd_sc_raw", [P, R], U8)), wd_scales)
+
+        table_half(0)
+        table_half(1)
 
         def pick(g, i, span):
-            weights, origin = (wgt_first, 0) if span.start < split else (wgt_rest, split)
-            nc.vector.tensor_tensor(
-                g, x_planes[i][:].indirect(head_lists[:, entries(span)]),
-                weights[:, span.start - origin : span.stop - origin], ALU.mult,
-            )
+            nc.vector.tensor_tensor(g, x_planes[i][:].indirect(head_lists[:, entries(span)]), wgt[:, span], ALU.mult)
 
         def weave(copy, woven, planar):
             copy(
@@ -193,13 +212,12 @@ def tile_list_htabg_max_biasP_kernel(
         def quantise(codes, scales, woven):
             nc.vector.quantize_mx(out=codes.bitcast(FP8X4), scales=scales, in_=woven.rearrange("p j t -> p (j t)"))
 
-        def quantised(name, woven, width):
-            codes = sb(name, [P, width], U32)
-            scales = sb(name + "_sc", [P, width], U8)
-            quantise(codes[:], scales[:], woven[:])
-            return codes, scales
-
-        g_first = sb("g_first", [P, PACK, WIDTHS[0]], F32, tag="g_ring")
+        at_g0 = at_woven
+        at_xw = at_g0 + 4 * PACK * WIDTHS[0]
+        at_xq0 = at_xw + 2 * PACK * J
+        at_hq0 = at_xq0 + 4 * WIDTHS[0]
+        at_staged = at_hq0 + 4 * WIDTHS[0]
+        g_first = placed(at_g0, "g_first", [P, PACK, WIDTHS[0]], F32)
         g_next = sb("g_next", [P, PACK, split - WIDTHS[0]], F32)
         for i in range(PACK - 1):
             pick(g_first[:, i, :], i, spans[0])
@@ -207,33 +225,45 @@ def tile_list_htabg_max_biasP_kernel(
         batches = {u: (g_next, WIDTHS[0]) for u in range(1, AHEAD)}
         batches[0] = (g_first, 0)
 
-        x_woven = [placed(at_woven + 2 * PACK * s, f"x_woven{u}", [P, w, PACK], BF16) for u, (s, w) in enumerate(zip(starts, WIDTHS))]
         y_woven = sb("y_woven", [P, J, PACK], BF16)
         y_codes = sb("y_codes", [P, J], I32)
         y_scales = sb("y_scales", [P, J], U8)
         y_rows = out_0.rearrange("(p t) j -> p t j", t=PACK)
         code_rows = out_1[0].rearrange("p j i -> p (j i)").bitcast(I32)
-        weights, ya, h_woven, y = {}, {}, {}, {}
+        weights, x_woven, ya, staged, h_woven, y = {}, {}, {}, {}, {}, {}
+
+        def stage_late(u):
+            g_late = placed(at_g0, "g_late", [P, PACK, J - split], F32)
+            for i in range(PACK - 1):
+                pick(g_late[:, i, :], i, slice(split, J))
+            for v in range(AHEAD, len(WIDTHS)):
+                batches[v] = (g_late, split)
 
         def stage_pick(u):
-            if u == AHEAD:
-                g_late = sb("g_late", [P, PACK, J - split], F32, tag="g_ring")
-                for i in range(PACK - 1):
-                    pick(g_late[:, i, :], i, slice(split, J))
-                for v in range(AHEAD, len(WIDTHS)):
-                    batches[v] = (g_late, split)
             g, origin = batches[u]
             local = slice(spans[u].start - origin, spans[u].stop - origin)
             pick(g[:, PACK - 1, local], PACK - 1, spans[u])
+            x_woven[u] = placed(at_xw + 2 * PACK * starts[u], f"x_woven{u}", [P, WIDTHS[u], PACK], BF16)
             weave(nc.scalar.copy, x_woven[u][:], g[:, :, local])
 
+        def deal_wa(u):
+            wad = deal(sb("wad", [P, 2 * 2 * R], U8), wad_raw, 2, U16)
+            wa_sc = deal(sb("wa_sc", [P, R], U8), wad_sc_raw, 1, U8)
+            move_up(wd_sc, wa_sc)
+            weights["wa"] = (wad[:, cols(0, 2 * R)], wa_sc)
+            weights["wd"] = (wad[:, cols(1, 2 * R)], wd_sc)
+
+        def quantised(name, woven, width, offset):
+            codes = placed(offset, name, [P, width], U32) if offset else sb(name, [P, width], U32)
+            scales = sb(name + "_sc", [P, width], U8)
+            quantise(codes[:], scales[:], woven[:])
+            return codes, scales
+
         def stage_ya(u):
-            if u == 0:
-                weights["wa"] = (deal(sb("wa", [P, 2 * R], U8), wa_raw, 1, U16), deal(sb("wa_sc", [P, R], U8), wa_sc_raw, 1, U8))
-            codes, scales = quantised(f"xq{u}", x_woven[u], WIDTHS[u])
+            codes, scales = quantised(f"xq{u}", x_woven[u], WIDTHS[u], at_xq0 if u == 0 else None)
             ya[u] = []
             for s in range(WIDTHS[u] // UNIT):
-                bank = psum.tile([P, PACK, UNIT], F32, name="ya_bank", bufs=YA_BANKS)
+                bank = psum.tile([P, PACK, UNIT], F32, name=f"ya_bank{u}_{s}", offset=2048 * (YA_AT[u] + s))
                 for t in range(PACK):
                     nc.tensor.matmul_mx(
                         out=bank[:, t, :], rhs=codes[:, cols(s, UNIT)].bitcast(FP8X4), rhs_scale=scales[:, cols(s, UNIT)],
@@ -241,13 +271,15 @@ def tile_list_htabg_max_biasP_kernel(
                     )
                 ya[u].append(bank[:].rearrange("p t j -> p j t"))
 
+        def stage_stage(u):
+            staged[u] = placed(at_staged + 2 * PACK * starts[u], f"ya{u}", [P, WIDTHS[u], PACK], BF16)
+            for s, bank in enumerate(ya[u]):
+                nc.scalar.copy(out=staged[u][:, cols(s, UNIT), :], in_=bank)
+
         def stage_max(u):
-            h_woven[u] = sb(f"h_woven{u}", [P, WIDTHS[u], PACK], BF16)
-            if u in STAGED:
-                staged = sb(f"ya{u}", [P, WIDTHS[u], PACK], BF16)
-                for s, bank in enumerate(ya[u]):
-                    nc.scalar.copy(out=staged[:, cols(s, UNIT), :], in_=bank)
-                nc.vector.tensor_tensor(h_woven[u][:], staged[:], yb[:, spans[u], :], ALU.max)
+            h_woven[u] = placed(at_staged, f"h_woven{u}", [P, WIDTHS[u], PACK], BF16) if u == 1 else sb(f"h_woven{u}", [P, WIDTHS[u], PACK], BF16)
+            if u in staged:
+                nc.vector.tensor_tensor(h_woven[u][:], staged[u][:], yb[:, spans[u], :], ALU.max)
             else:
                 for s, bank in enumerate(ya[u]):
                     nc.vector.tensor_tensor(
@@ -255,18 +287,13 @@ def tile_list_htabg_max_biasP_kernel(
                     )
 
         def stage_y(u):
-            if u == 0:
-                weights["wd"] = (
-                    deal(placed(at_woven, "wd", [P, 2 * R], U8), wd_raw, 1, U16),
-                    deal(placed(at_woven + 2 * R, "wd_sc", [P, R], U8), wd_sc_raw, 1, U8),
-                )
             width = WIDTHS[u]
-            codes, scales = quantised(f"hq{u}", h_woven[u], width)
+            codes, scales = quantised(f"hq{u}", h_woven[u], width, at_hq0 if u == 0 else None)
             y[u] = sb(f"y{u}", [P, PACK, width], F32)
             per_bank = BANK // width
             for k in range(PACK // per_bank):
                 rows = range(PACK)[cols(k, per_bank)]
-                bank = psum.tile([P, per_bank, width], F32, name="y_bank", tag="y_bank", bufs=Y_BANKS)
+                bank = psum.tile([P, per_bank, width], F32, name=f"y_bank{u}_{k}", offset=2048 * (Y_AT[u] + k))
                 for e, t in enumerate(rows):
                     nc.tensor.matmul_mx(
                         out=bank[:, e, :], rhs=codes[:].bitcast(FP8X4), rhs_scale=scales[:],
@@ -291,11 +318,40 @@ def tile_list_htabg_max_biasP_kernel(
                 stored = slice(max(before, default=0), ends[u])
                 nc.sync.dma_start(out=code_rows[:, stored], in_=y_codes[:, stored])
 
-        stages = ((stage_pick, 0), (stage_ya, 1), (stage_max, 1), (stage_y, 3), (stage_out, 4))
-        for step in range(len(WIDTHS) + stages[-1][1]):
-            for stage, lag in stages:
-                if 0 <= step - lag < len(WIDTHS):
-                    stage(step - lag)
+        order = (
+            (stage_pick, 0),
+            (stage_pick, 1),
+            (stage_pick, 2),
+            (deal_wa, 0),
+            (stage_ya, 0),
+            (stage_ya, 1),
+            (stage_stage, 0),
+            (stage_late, 0),
+            (stage_pick, 3),
+            (stage_pick, 4),
+            (stage_ya, 2),
+            (stage_max, 0),
+            (stage_ya, 3),
+            (stage_y, 0),
+            (stage_stage, 2),
+            (stage_max, 1),
+            (stage_ya, 4),
+            (stage_y, 1),
+            (stage_stage, 3),
+            (stage_max, 2),
+            (stage_max, 3),
+            (stage_y, 2),
+            (stage_max, 4),
+            (stage_y, 3),
+            (stage_out, 0),
+            (stage_y, 4),
+            (stage_out, 1),
+            (stage_out, 2),
+            (stage_out, 3),
+            (stage_out, 4),
+        )
+        for stage, u in order:
+            stage(u)
 
         for q in range(QUADS):
             (nc.sync, nc.scalar)[q % 2].dma_start(

@@ -51,6 +51,9 @@ def tile_list_htabg_max_biasP_kernel(
         def placed(offset, name, shape, dtype):
             return arena.tile(shape, dtype, name=name, offset=offset, align_bytes=64)
 
+        def held(name, shape, dtype):
+            return placed(where[name], name, shape, dtype) if name in where else sb(name, shape, dtype)
+
         def zeroed(engine, tile):
             engine.memset(tile[:].bitcast(I32), 0)
             return tile
@@ -76,7 +79,12 @@ def tile_list_htabg_max_biasP_kernel(
         plane_bytes = 4 * T
         at_wb_sc = 0
         at_picked = at_wb_sc + R - EDGE
-        at_woven = at_picked + 4 * J + R
+        wide = WIDTHS[0]
+        at_g0 = at_picked + 4 * J
+        at_xw0 = at_g0 + 4 * PACK * wide
+        at_ya0 = at_xw0 + 2 * PACK * wide
+        where = {"g_first": at_g0, "g_late": at_g0, "x_woven0": at_xw0, "wd": at_xw0, "wd_sc": at_xw0 + 2 * R,
+                 "ya0": at_ya0, "h_woven1": at_ya0}
 
         tab_list = keep.tile([P, J // GROUP], U16, name="tab_list")
         head_lists = keep.tile([P, J // GROUP], U16, name="head_lists")
@@ -84,8 +92,8 @@ def tile_list_htabg_max_biasP_kernel(
         wb_sc_raw = zeroed(nc.vector, placed(at_wb_sc, "wb_sc_raw", [P, R], U8))
         wb_sc1 = zeroed(nc.vector, sb("wb_sc1", [P, R], U8))
         sc1 = zeroed(nc.vector, sb("sc1", [P, J], U8))
-        wad_sc_raw = zeroed(nc.vector, sb("wad_sc_raw", [P, R], U8))
-        wd_sc = zeroed(nc.vector, sb("wd_sc", [P, R], U8))
+        wa_sc_raw = zeroed(nc.vector, sb("wa_sc_raw", [P, R], U8))
+        wd_sc_raw = zeroed(nc.vector, sb("wd_sc_raw", [P, R], U8))
 
         def load_words(tile, words):
             nc.sync.dma_start(
@@ -94,10 +102,10 @@ def tile_list_htabg_max_biasP_kernel(
             )
             return tile
 
-        def load_scales(tile, first, scales):
-            for q in range(QUADS):
+        def load_scales(tile, scales, quads=range(QUADS)):
+            for q in quads:
                 nc.sync.dma_start(
-                    out=tile[32 * q + first : 32 * q + first + 4, :].bitcast(I32),
+                    out=tile[32 * q : 32 * q + 4, :].bitcast(I32),
                     in_=scales[0, 4 * q : 4 * q + 4, :].bitcast(I32),
                 )
 
@@ -138,11 +146,12 @@ def tile_list_htabg_max_biasP_kernel(
         nc.sync.dma_start(out=tab_w[:], in_=tab_words[0].rearrange("p t b -> p (t b)").bitcast(I32))
         load_scale_pair(wb_sc_raw, wb_scales)
 
+        load_scales(wa_sc_raw, wa_scales, range(2))
         x_planes = [load_plane(0)]
-        wad_raw = sb("wad_raw", [P, 2 * 2 * R], U8)
         x_planes.append(sb("x1", [P, T], F32))
         load_part(1, slice(0, T // 2))
         nc.sync.dma_start(head_lists[:], offs2)
+        load_scales(wa_sc_raw, wa_scales, range(2, QUADS))
         identity = sb("identity", [P, P], F32)
         make_identity(nc, identity[:])
         turned = psum.tile([P, P], F32, name="turned", offset=2048 * 7)
@@ -162,12 +171,11 @@ def tile_list_htabg_max_biasP_kernel(
         wb_sc0 = deal(sb("wb_sc0", [P, R], U8), wb_sc_raw, 1, U8)
         move_up(wb_sc1, wb_sc0)
         load_part(1, slice(T // 2, T))
-        load_scales(wad_sc_raw, 0, wa_scales)
         x_planes.append(load_plane(2))
-        load_scales(wad_sc_raw, 16, wd_scales)
         x_planes.append(load_plane(3))
-        load_words(wad_raw[:, cols(0, 2 * R)], wa_words)
-        load_words(wad_raw[:, cols(1, 2 * R)], wd_words)
+        wa_raw = load_words(sb("wa_raw", [P, 2 * R], U8), wa_words)
+        wd_raw = load_words(sb("wd_raw", [P, 2 * R], U8), wd_words)
+        load_scales(wd_sc_raw, wd_scales)
         bias = sb("bias", [P, PACK], F32)
         nc.sync.dma_start(out=bias[:], in_=b.rearrange("(p t) -> p t", t=PACK))
 
@@ -212,12 +220,7 @@ def tile_list_htabg_max_biasP_kernel(
         def quantise(codes, scales, woven):
             nc.vector.quantize_mx(out=codes.bitcast(FP8X4), scales=scales, in_=woven.rearrange("p j t -> p (j t)"))
 
-        at_g0 = at_woven
-        at_xw = at_g0 + 4 * PACK * WIDTHS[0]
-        at_xq0 = at_xw + 2 * PACK * J
-        at_hq0 = at_xq0 + 4 * WIDTHS[0]
-        at_staged = at_hq0 + 4 * WIDTHS[0]
-        g_first = placed(at_g0, "g_first", [P, PACK, WIDTHS[0]], F32)
+        g_first = held("g_first", [P, PACK, WIDTHS[0]], F32)
         g_next = sb("g_next", [P, PACK, split - WIDTHS[0]], F32)
         for i in range(PACK - 1):
             pick(g_first[:, i, :], i, spans[0])
@@ -233,7 +236,7 @@ def tile_list_htabg_max_biasP_kernel(
         weights, x_woven, ya, staged, h_woven, y = {}, {}, {}, {}, {}, {}
 
         def stage_late(u):
-            g_late = placed(at_g0, "g_late", [P, PACK, J - split], F32)
+            g_late = held("g_late", [P, PACK, J - split], F32)
             for i in range(PACK - 1):
                 pick(g_late[:, i, :], i, slice(split, J))
             for v in range(AHEAD, len(WIDTHS)):
@@ -243,24 +246,23 @@ def tile_list_htabg_max_biasP_kernel(
             g, origin = batches[u]
             local = slice(spans[u].start - origin, spans[u].stop - origin)
             pick(g[:, PACK - 1, local], PACK - 1, spans[u])
-            x_woven[u] = placed(at_xw + 2 * PACK * starts[u], f"x_woven{u}", [P, WIDTHS[u], PACK], BF16)
+            x_woven[u] = held(f"x_woven{u}", [P, WIDTHS[u], PACK], BF16)
             weave(nc.scalar.copy, x_woven[u][:], g[:, :, local])
 
         def deal_wa(u):
-            wad = deal(sb("wad", [P, 2 * 2 * R], U8), wad_raw, 2, U16)
-            wa_sc = deal(sb("wa_sc", [P, R], U8), wad_sc_raw, 1, U8)
-            move_up(wd_sc, wa_sc)
-            weights["wa"] = (wad[:, cols(0, 2 * R)], wa_sc)
-            weights["wd"] = (wad[:, cols(1, 2 * R)], wd_sc)
+            weights["wa"] = (deal(sb("wa", [P, 2 * R], U8), wa_raw, 1, U16), deal(sb("wa_sc", [P, R], U8), wa_sc_raw, 1, U8))
 
-        def quantised(name, woven, width, offset):
-            codes = placed(offset, name, [P, width], U32) if offset else sb(name, [P, width], U32)
+        def deal_wd(u):
+            weights["wd"] = (deal(held("wd", [P, 2 * R], U8), wd_raw, 1, U16), deal(held("wd_sc", [P, R], U8), wd_sc_raw, 1, U8))
+
+        def quantised(name, woven, width):
+            codes = held(name, [P, width], U32)
             scales = sb(name + "_sc", [P, width], U8)
             quantise(codes[:], scales[:], woven[:])
             return codes, scales
 
         def stage_ya(u):
-            codes, scales = quantised(f"xq{u}", x_woven[u], WIDTHS[u], at_xq0 if u == 0 else None)
+            codes, scales = quantised(f"xq{u}", x_woven[u], WIDTHS[u])
             ya[u] = []
             for s in range(WIDTHS[u] // UNIT):
                 bank = psum.tile([P, PACK, UNIT], F32, name=f"ya_bank{u}_{s}", offset=2048 * (YA_AT[u] + s))
@@ -272,12 +274,12 @@ def tile_list_htabg_max_biasP_kernel(
                 ya[u].append(bank[:].rearrange("p t j -> p j t"))
 
         def stage_stage(u):
-            staged[u] = placed(at_staged + 2 * PACK * starts[u], f"ya{u}", [P, WIDTHS[u], PACK], BF16)
+            staged[u] = held(f"ya{u}", [P, WIDTHS[u], PACK], BF16)
             for s, bank in enumerate(ya[u]):
                 nc.scalar.copy(out=staged[u][:, cols(s, UNIT), :], in_=bank)
 
         def stage_max(u):
-            h_woven[u] = placed(at_staged, f"h_woven{u}", [P, WIDTHS[u], PACK], BF16) if u == 1 else sb(f"h_woven{u}", [P, WIDTHS[u], PACK], BF16)
+            h_woven[u] = held(f"h_woven{u}", [P, WIDTHS[u], PACK], BF16)
             if u in staged:
                 nc.vector.tensor_tensor(h_woven[u][:], staged[u][:], yb[:, spans[u], :], ALU.max)
             else:
@@ -288,7 +290,7 @@ def tile_list_htabg_max_biasP_kernel(
 
         def stage_y(u):
             width = WIDTHS[u]
-            codes, scales = quantised(f"hq{u}", h_woven[u], width, at_hq0 if u == 0 else None)
+            codes, scales = quantised(f"hq{u}", h_woven[u], width)
             y[u] = sb(f"y{u}", [P, PACK, width], F32)
             per_bank = BANK // width
             for k in range(PACK // per_bank):
@@ -325,6 +327,7 @@ def tile_list_htabg_max_biasP_kernel(
             (deal_wa, 0),
             (stage_ya, 0),
             (stage_ya, 1),
+            (deal_wd, 0),
             (stage_stage, 0),
             (stage_late, 0),
             (stage_pick, 3),

@@ -29,8 +29,8 @@ EDGE = 64
 WIDTHS = (256, 256, 256, 128, 128)
 AHEAD = 3
 STAGED = (0, 2)
-EARLY = 2
-CODE_STORES = (1, 2, 4)
+EARLY = 3
+CODE_STORES = (2, 4)
 YA_AT = (6, 2, 4, 6, 7)
 Y_AT = (0, 2, 4, 6, 7)
 
@@ -205,6 +205,12 @@ def tile_list_htabg_max_biasP_kernel(
                         )
                 nc.scalar.activation(out=yb[:, places, :], in_=bank[:].rearrange("p t j -> p j t"), func=IDENTITY)
 
+        idle = psum.tile([P, BANK], F32, name="idle", offset=2048 * 7)
+        for t in range(3):
+            nc.tensor.matmul_mx(
+                out=idle[:], rhs=picked[:, 0 : BANK // 2].bitcast(FP4X4), rhs_scale=sc0[:, 0:BANK],
+                start=True, stop=True, **stationary(wb, wb_sc0, t),
+            )
         table_half(0)
         table_half(1)
 

@@ -22,17 +22,16 @@ PACK = 4
 QUADS = 4
 GROUP = 16
 BANK = 512
+BANKS = 8
 UNIT = BANK // PACK
 HALF = J // 2
+QUARTER = J // 4
 EDGE = 64
 
-WIDTHS = (256, 256, 256, 128, 128)
-AHEAD = 3
-STAGED = (0, 2)
-EARLY = 3
-CODE_STORES = (2, 4)
-YA_AT = (6, 2, 4, 6, 7)
-Y_AT = (0, 2, 4, 6, 7)
+WIDTHS = (128, 256, 256, 128, 128, 128)
+AHEAD = 4
+STAGED = (1, 2, 3)
+CODE_STORES = (2, 4, 5)
 
 
 def tile_list_htabg_max_biasP_kernel(
@@ -45,26 +44,18 @@ def tile_list_htabg_max_biasP_kernel(
         arena = ctx.enter_context(tc.tile_pool(name="arena", bufs=1))
         psum = ctx.enter_context(tc.psum_pool(name="psum", bufs=1))
 
-        def sb(name, shape, dtype, tag=None):
-            return keep.tile(shape, dtype, name=name, tag=tag or name, align_bytes=64)
+        def sb(name, shape, dtype):
+            return keep.tile(shape, dtype, name=name, align_bytes=64)
 
         def placed(offset, name, shape, dtype):
             return arena.tile(shape, dtype, name=name, offset=offset, align_bytes=64)
 
-        def held(name, shape, dtype):
-            return placed(where[name], name, shape, dtype) if name in where else sb(name, shape, dtype)
+        def bank_tile(name, bank, shape):
+            return psum.tile(shape, F32, name=name, offset=4 * BANK * bank)
 
         def zeroed(engine, tile):
             engine.memset(tile[:].bitcast(I32), 0)
             return tile
-
-        taken = {}
-        names = []
-
-        def next_bank(kind, count):
-            taken[kind] = taken.get(kind, -1) + 1
-            names.append(kind)
-            return taken[kind] % count
 
         def cols(i, width):
             return slice(i * width, (i + 1) * width)
@@ -75,39 +66,41 @@ def tile_list_htabg_max_biasP_kernel(
         starts = [sum(WIDTHS[:u]) for u in range(len(WIDTHS))]
         spans = [slice(s, s + w) for s, w in zip(starts, WIDTHS)]
         split = starts[AHEAD]
-
-        plane_bytes = 4 * T
-        at_wb_sc = 0
-        at_picked = at_wb_sc + R - EDGE
-        wide = WIDTHS[0]
-        at_g0 = at_picked + 4 * J
-        at_xw0 = at_g0 + 4 * PACK * wide
-        at_ya0 = at_xw0 + 2 * PACK * wide
-        where = {"g_first": at_g0, "g_late": at_g0, "x_woven0": at_xw0, "wd": at_xw0, "wd_sc": at_xw0 + 2 * R,
-                 "ya0": at_ya0, "h_woven1": at_ya0}
+        steps = range(len(WIDTHS))
 
         tab_list = keep.tile([P, J // GROUP], U16, name="tab_list")
         head_lists = keep.tile([P, J // GROUP], U16, name="head_lists")
+        at = {"sc_raw": 0, "picked": EDGE}
+        at["bias"] = at["wb_raw"] = at["picked"] + 4 * J
+        at["x3"] = at["tab_w"] = at["wb_raw"] + 4 * R
+        at["spread"] = at["x3"] + 4 * T
+        at["x2"] = at["spread"] + 4 * J - EDGE
+        for e, name in enumerate(("wa", "wd")):
+            at[name] = at["spread"] + 2 * R * e
+        for u in steps:
+            at[f"x_woven{u}"] = at["x2"] + 4 * T + 4 * PACK * (J - split) + 2 * PACK * (starts[u] - WIDTHS[0])
+
+        def held(name, shape, dtype):
+            return placed(at[name], name, shape, dtype) if name in at else sb(name, shape, dtype)
+
         tab_sc = zeroed(nc.gpsimd, sb("tab_sc", [P, T], U8))
-        wb_sc_raw = zeroed(nc.vector, placed(at_wb_sc, "wb_sc_raw", [P, R], U8))
-        wb_sc1 = zeroed(nc.vector, sb("wb_sc1", [P, R], U8))
+        sc_raw = zeroed(nc.vector, held("sc_raw", [P, 2 * R], U8))
         sc1 = zeroed(nc.vector, sb("sc1", [P, J], U8))
-        wa_sc_raw = zeroed(nc.vector, sb("wa_sc_raw", [P, R], U8))
-        wd_sc_raw = zeroed(nc.vector, sb("wd_sc_raw", [P, R], U8))
 
         def load_words(tile, words):
+            passes = words.shape[0]
             nc.sync.dma_start(
-                out=tile[:].bitcast(I32).rearrange("p (a c) -> p a c", a=words.shape[0]),
+                out=tile.bitcast(I32).rearrange("p (a c) -> p a c", a=passes),
                 in_=words.bitcast(I32).rearrange("a p c -> p a c"),
             )
             return tile
 
-        def load_scales(tile, scales, quads=range(QUADS)):
-            for q in quads:
-                nc.sync.dma_start(
-                    out=tile[32 * q : 32 * q + 4, :].bitcast(I32),
-                    in_=scales[0, 4 * q : 4 * q + 4, :].bitcast(I32),
-                )
+        def load_scales(row, first, scales):
+            passes = scales.shape[0]
+            nc.sync.dma_start(
+                out=sc_raw[row : row + 16, first * R : (first + passes) * R].bitcast(I32).rearrange("s (a c) -> s a c", a=passes),
+                in_=scales.bitcast(I32).rearrange("a s c -> s a c"),
+            )
 
         def load_scale_pair(tile, scales):
             for r in range(4):
@@ -120,99 +113,122 @@ def tile_list_htabg_max_biasP_kernel(
             nc.sync.dma_start(out=upper[0 : P - 16, :].bitcast(I32), in_=pair[16:P, :].bitcast(I32))
 
         def load_plane(i):
-            plane = sb(f"x{i}", [P, T], F32)
+            plane = held(f"x{i}", [P, T], F32)
             nc.sync.dma_start(out=plane[:], in_=xT.rearrange("(p i) t -> p i t", i=PACK)[:, i, :])
             return plane
 
         def load_part(i, tokens):
             nc.sync.dma_start(out=x_planes[i][:, tokens], in_=xT.rearrange("(p i) t -> p i t", i=PACK)[:, i, tokens])
 
-        def deal(dealt, raw, passes, dtype):
-            nc.vector.tensor_copy(
-                out=dealt[:].bitcast(dtype).rearrange("p (a t m) -> p a t m", a=passes, t=PACK),
-                in_=raw[:].bitcast(dtype).rearrange("p (a m t) -> p a t m", a=passes, t=PACK),
+        def deal(copy, dealt, raw, dtype):
+            copy(
+                out=dealt.bitcast(dtype).rearrange("p (t m) -> p t m", t=PACK),
+                in_=raw.bitcast(dtype).rearrange("p (m t) -> p t m", t=PACK),
             )
+
+        def deal_words(name, raw):
+            dealt = held(name, [P, 2 * R], U8)
+            deal(nc.scalar.copy, dealt[:], raw, U16)
             return dealt
+
+        def move_rows(upper, row, quads):
+            for q in quads:
+                nc.sync.dma_start(
+                    out=upper[32 * q : 32 * q + 4, :].bitcast(I32),
+                    in_=w_sc[row + 4 * q : row + 4 * q + 4, :].bitcast(I32),
+                )
 
         def stationary(words, scales, t):
             return dict(lhsT=words[:, cols(t, 2 * P)].bitcast(FP4X4), lhsT_scale=scales[:, cols(t, P)])
 
-        wb_raw = load_words(sb("wb_raw", [P, 2 * 2 * R], U8), wb_words)
+        wb_raw = load_words(held("wb_raw", [P, 4 * R], U8)[:], wb_words)
         nc.sync.dma_start(tab_list[:], offs)
         wgt_rows = sb("wgt_rows", [P, P], F32)
         nc.sync.dma_start(out=wgt_rows[:], in_=wgt2.rearrange("(g u) (c j) -> u g c j", u=8, j=P)[0])
         load_scale_pair(tab_sc, tab_scales)
-        tab_w = sb("tab_w", [P, T], I32)
+        tab_w = held("tab_w", [P, T], I32)
         nc.sync.dma_start(out=tab_w[:], in_=tab_words[0].rearrange("p t b -> p (t b)").bitcast(I32))
-        load_scale_pair(wb_sc_raw, wb_scales)
-
-        load_scales(wa_sc_raw, wa_scales, range(2))
-        x_planes = [load_plane(0)]
-        x_planes.append(sb("x1", [P, T], F32))
-        load_part(1, slice(0, T // 2))
+        load_scales(0, 0, wb_scales)
+        load_scales(16, 0, wa_scales)
+        load_scales(16, 1, wd_scales)
         nc.sync.dma_start(head_lists[:], offs2)
-        load_scales(wa_sc_raw, wa_scales, range(2, QUADS))
+        wa_raw = load_words(sb("wa_raw", [P, 2 * R], U8)[:], wa_words)
+        x_planes = [load_plane(0)]
+        wd_raw = load_words(sb("wd_raw", [P, 2 * R], U8)[:], wd_words)
+        x_planes.append(sb("x1", [P, T], F32))
+        load_part(1, slice(0, T // 4))
+
+        wb = [deal_words(f"wb{a}", wb_raw[:, cols(a, 2 * R)]) for a in range(2)]
         identity = sb("identity", [P, P], F32)
         make_identity(nc, identity[:])
-        turned = psum.tile([P, P], F32, name="turned", offset=2048 * 7)
+        turned = bank_tile("turned", 7, [P, P])
         nc.tensor.transpose(turned[:], wgt_rows[:], identity[:])
-        spread = sb("spread", [P, J // P, 16, 8], F32)
+        spread = placed(at["spread"], "spread", [P, J // P, 16, 8], F32)
         nc.scalar.copy(out=spread[:], in_=turned[:].rearrange("j (g c) -> j c g", c=8).unsqueeze(3).to_broadcast([P, J // P, 16, 8]))
         wgt = sb("wgt", [P, J], F32)
         for k in range(J // BANK):
-            bank = psum.tile([P, PACK, P], F32, name=f"wgt_bank{k}", offset=2048 * (5 + k))
+            bank = bank_tile(f"wgt_bank{k}", 5 + k, [P, PACK, P])
             for c in range(PACK):
                 nc.tensor.transpose(bank[:, c, :], spread[:, PACK * k + c].rearrange("j g u -> j (g u)"), identity[:])
             nc.scalar.copy(out=wgt[:, cols(k, BANK)], in_=bank[:].rearrange("p c j -> p (c j)"))
-        wb = deal(sb("wb", [P, 2 * 2 * R], U8), wb_raw, 2, U16)
+        wa = deal_words("wa", wa_raw)
+        wd = deal_words("wd", wd_raw)
         sc0 = sb("sc0", [P, J], U8)
         nc.vector.tensor_copy(out=sc0[:], in_=tab_sc[:].indirect(tab_list[:]))
         move_up(sc1, sc0)
-        wb_sc0 = deal(sb("wb_sc0", [P, R], U8), wb_sc_raw, 1, U8)
-        move_up(wb_sc1, wb_sc0)
-        load_part(1, slice(T // 2, T))
-        x_planes.append(load_plane(2))
-        x_planes.append(load_plane(3))
-        wa_raw = load_words(sb("wa_raw", [P, 2 * R], U8), wa_words)
-        wd_raw = load_words(sb("wd_raw", [P, 2 * R], U8), wd_words)
-        load_scales(wd_sc_raw, wd_scales)
-        bias = sb("bias", [P, PACK], F32)
-        nc.sync.dma_start(out=bias[:], in_=b.rearrange("(p t) -> p t", t=PACK))
+        w_sc = sb("w_sc", [P, 2 * R], U8)
+        nc.vector.tensor_copy(
+            out=w_sc[:].rearrange("p (a t m) -> p a t m", a=2, t=PACK),
+            in_=sc_raw[:].rearrange("p (a m t) -> p a t m", a=2, t=PACK),
+        )
+        move_rows(w_sc, 0, range(1, QUADS))
+        load_part(1, slice(T // 4, T))
+        wb_sc0, wb_sc1 = w_sc[:, 0:R], w_sc[:, R : 2 * R]
 
-        yb = sb("yb", [P, J, PACK], BF16)
-        picked = placed(at_picked, "picked", [P, J], U32)
-        for c in range(2):
-            half = cols(c, HALF)
-            nc.vector.tensor_copy(out=picked[:, half], in_=tab_w[:].bitcast(U32).indirect(tab_list[:, entries(half)]))
+        yb_pairs = sb("yb_pairs", [P, 2, J, 2], BF16)
+        yb = yb_pairs[:].rearrange("p u j e -> p j u e")
+        picked = held("picked", [P, J], U32)
+        parted = [held(f"parted{c}", [P, 2 * 2 * HALF], U8) for c in range(2)]
 
-        def table_half(c):
-            parted = sb(f"parted{c}", [P, 2 * 2 * HALF], U8)
+        def table_bank(c, u):
+            bank = bank_tile(f"yb_bank{c}_{u}", (2 * c + u) % 4, [P, 2, QUARTER])
+            for a in range(2):
+                for e in range(2):
+                    nc.tensor.matmul_mx(
+                        out=bank[:, e, :],
+                        rhs=parted[c // 2][:, cols(2 * a + c % 2, 2 * QUARTER)].bitcast(FP4X4),
+                        rhs_scale=(sc0, sc1)[a][:, cols(c, QUARTER)],
+                        start=(a == 0 and e == 0), stop=(a == 1 and e == 1),
+                        **stationary(wb[a], (wb_sc0, wb_sc1)[a], 2 * u + e),
+                    )
+            nc.scalar.activation(out=yb_pairs[:, u, cols(c, QUARTER), :], in_=bank[:].rearrange("p e j -> p j e"), func=IDENTITY)
+
+        for half in range(2):
             nc.vector.tensor_copy(
-                out=parted[:].bitcast(U16).rearrange("p (a j) -> p a j", a=2),
-                in_=picked[:, cols(c, HALF)].bitcast(U16).rearrange("p (j a) -> p a j", a=2),
+                out=picked[:, cols(half, HALF)],
+                in_=tab_w[:].bitcast(U32).indirect(tab_list[:, entries(cols(half, HALF))]),
             )
-            for s in range(HALF // UNIT):
-                places = cols(c * (HALF // UNIT) + s, UNIT)
-                bank = psum.tile([P, PACK, UNIT], F32, name=f"yb_bank{len(names)}", offset=2048 * next_bank("yb", 5))
-                for a in (1, 0):
-                    for t in range(PACK):
-                        nc.tensor.matmul_mx(
-                            out=bank[:, t, :],
-                            rhs=parted[:, cols(a * (HALF // UNIT) + s, 2 * UNIT)].bitcast(FP4X4),
-                            rhs_scale=(sc0, sc1)[a][:, places],
-                            start=(a == 1 and t == 0), stop=(a == 0 and t == PACK - 1),
-                            **stationary(wb[:, cols(a, 2 * R)], (wb_sc0, wb_sc1)[a], t),
-                        )
-                nc.scalar.activation(out=yb[:, places, :], in_=bank[:].rearrange("p t j -> p j t"), func=IDENTITY)
-
-        idle = psum.tile([P, BANK], F32, name="idle", offset=2048 * 7)
+        idle = bank_tile("idle", 4, [P, BANK])
         for t in range(3):
             nc.tensor.matmul_mx(
                 out=idle[:], rhs=picked[:, 0 : BANK // 2].bitcast(FP4X4), rhs_scale=sc0[:, 0:BANK],
-                start=True, stop=True, **stationary(wb, wb_sc0, t),
+                start=True, stop=True, **stationary(wb[0], sc0, t),
             )
-        table_half(0)
-        table_half(1)
+        for half in range(2):
+            nc.vector.tensor_copy(
+                out=parted[half][:].bitcast(U16).rearrange("p (a j) -> p a j", a=2),
+                in_=picked[:, cols(half, HALF)].bitcast(U16).rearrange("p (j a) -> p a j", a=2),
+            )
+            for e in range(2):
+                for u in range(2):
+                    table_bank(2 * half + e, u)
+
+        x_planes.append(load_plane(2))
+        x_planes.append(load_plane(3))
+        move_rows(wa_raw, 16, range(QUADS))
+        wa_sc, wd_sc = wa_raw[:, 0:R], wa_raw[:, R : 2 * R]
+        bias = placed(at["bias"], "bias", [P, PACK], F32)
+        nc.sync.dma_start(out=bias[:], in_=b.rearrange("(p t) -> p t", t=PACK))
 
         def pick(g, i, span):
             nc.vector.tensor_tensor(g, x_planes[i][:].indirect(head_lists[:, entries(span)]), wgt[:, span], ALU.mult)
@@ -226,40 +242,27 @@ def tile_list_htabg_max_biasP_kernel(
         def quantise(codes, scales, woven):
             nc.vector.quantize_mx(out=codes.bitcast(FP8X4), scales=scales, in_=woven.rearrange("p j t -> p (j t)"))
 
-        g_first = held("g_first", [P, PACK, WIDTHS[0]], F32)
-        g_next = sb("g_next", [P, PACK, split - WIDTHS[0]], F32)
+        picks = sb("picks", [P, WIDTHS[0] + PACK * J], F32)
+        early = picks[:, 0 : PACK * split].rearrange("p (t j) -> p t j", t=PACK)
+        late = picks[:, WIDTHS[0] :].rearrange("p (t j) -> p t j", t=PACK)[:, :, 0 : J - split]
         for i in range(PACK - 1):
-            pick(g_first[:, i, :], i, spans[0])
-            pick(g_next[:, i, :], i, slice(WIDTHS[0], split))
-        batches = {u: (g_next, WIDTHS[0]) for u in range(1, AHEAD)}
-        batches[0] = (g_first, 0)
+            pick(early[:, i, :], i, slice(0, split))
 
         y_woven = sb("y_woven", [P, J, PACK], BF16)
         y_codes = sb("y_codes", [P, J], I32)
         y_scales = sb("y_scales", [P, J], U8)
         y_rows = out_0.rearrange("(p t) j -> p t j", t=PACK)
         code_rows = out_1[0].rearrange("p j i -> p (j i)").bitcast(I32)
-        weights, x_woven, ya, staged, h_woven, y = {}, {}, {}, {}, {}, {}
-
-        def stage_late(u):
-            g_late = held("g_late", [P, PACK, J - split], F32)
-            for i in range(PACK - 1):
-                pick(g_late[:, i, :], i, slice(split, J))
-            for v in range(AHEAD, len(WIDTHS)):
-                batches[v] = (g_late, split)
+        x_woven, ya, staged, h_woven, y = {}, {}, {}, {}, {}
 
         def stage_pick(u):
-            g, origin = batches[u]
-            local = slice(spans[u].start - origin, spans[u].stop - origin)
-            pick(g[:, PACK - 1, local], PACK - 1, spans[u])
+            if u == AHEAD:
+                for i in range(PACK - 1):
+                    pick(late[:, i, :], i, slice(split, J))
+            g = early[:, :, spans[u]] if u < AHEAD else late[:, :, spans[u].start - split : spans[u].stop - split]
+            pick(g[:, PACK - 1, :], PACK - 1, spans[u])
             x_woven[u] = held(f"x_woven{u}", [P, WIDTHS[u], PACK], BF16)
-            weave(nc.scalar.copy, x_woven[u][:], g[:, :, local])
-
-        def deal_wa(u):
-            weights["wa"] = (deal(sb("wa", [P, 2 * R], U8), wa_raw, 1, U16), deal(sb("wa_sc", [P, R], U8), wa_sc_raw, 1, U8))
-
-        def deal_wd(u):
-            weights["wd"] = (deal(held("wd", [P, 2 * R], U8), wd_raw, 1, U16), deal(held("wd_sc", [P, R], U8), wd_sc_raw, 1, U8))
+            weave(nc.scalar.copy, x_woven[u][:], g)
 
         def quantised(name, woven, width):
             codes = held(name, [P, width], U32)
@@ -271,27 +274,32 @@ def tile_list_htabg_max_biasP_kernel(
             codes, scales = quantised(f"xq{u}", x_woven[u], WIDTHS[u])
             ya[u] = []
             for s in range(WIDTHS[u] // UNIT):
-                bank = psum.tile([P, PACK, UNIT], F32, name=f"ya_bank{u}_{s}", offset=2048 * (YA_AT[u] + s))
+                bank = bank_tile(f"ya_bank{u}_{s}", (4 + starts[u] // UNIT + s) % BANKS, [P, PACK, UNIT])
                 for t in range(PACK):
                     nc.tensor.matmul_mx(
                         out=bank[:, t, :], rhs=codes[:, cols(s, UNIT)].bitcast(FP8X4), rhs_scale=scales[:, cols(s, UNIT)],
-                        start=True, stop=True, **stationary(*weights["wa"], t),
+                        start=True, stop=True, **stationary(wa, wa_sc, t),
                     )
                 ya[u].append(bank[:].rearrange("p t j -> p j t"))
 
         def stage_stage(u):
+            if u not in STAGED:
+                return
             staged[u] = held(f"ya{u}", [P, WIDTHS[u], PACK], BF16)
             for s, bank in enumerate(ya[u]):
                 nc.scalar.copy(out=staged[u][:, cols(s, UNIT), :], in_=bank)
 
+        def paired(woven):
+            return woven.rearrange("p j (u e) -> p j u e", e=2)
+
         def stage_max(u):
             h_woven[u] = held(f"h_woven{u}", [P, WIDTHS[u], PACK], BF16)
             if u in staged:
-                nc.vector.tensor_tensor(h_woven[u][:], staged[u][:], yb[:, spans[u], :], ALU.max)
+                nc.vector.tensor_tensor(paired(h_woven[u][:]), paired(staged[u][:]), yb[:, spans[u]], ALU.max)
             else:
                 for s, bank in enumerate(ya[u]):
                     nc.vector.tensor_tensor(
-                        h_woven[u][:, cols(s, UNIT), :], bank, yb[:, spans[u], :][:, cols(s, UNIT), :], ALU.max,
+                        paired(h_woven[u][:, cols(s, UNIT), :]), paired(bank), yb[:, spans[u]][:, cols(s, UNIT)], ALU.max,
                     )
 
         def stage_y(u):
@@ -301,66 +309,36 @@ def tile_list_htabg_max_biasP_kernel(
             per_bank = BANK // width
             for k in range(PACK // per_bank):
                 rows = range(PACK)[cols(k, per_bank)]
-                bank = psum.tile([P, per_bank, width], F32, name=f"y_bank{u}_{k}", offset=2048 * (Y_AT[u] + k))
+                bank = bank_tile(f"y_bank{u}_{k}", (4 + starts[u] // UNIT + k) % BANKS, [P, per_bank, width])
                 for e, t in enumerate(rows):
                     nc.tensor.matmul_mx(
                         out=bank[:, e, :], rhs=codes[:].bitcast(FP8X4), rhs_scale=scales[:],
-                        start=True, stop=True, **stationary(*weights["wd"], t),
+                        start=True, stop=True, **stationary(wd, wd_sc, t),
                     )
                 for e, t in enumerate(rows):
                     nc.scalar.activation(out=y[u][:, t, :], in_=bank[:, e, :], func=IDENTITY, bias=bias[:, t : t + 1])
-                if u < EARLY:
-                    nc.sync.dma_start(out=y_rows[:, cols(k, per_bank), spans[u]], in_=y[u][:, cols(k, per_bank), :])
-            if u >= EARLY:
-                nc.sync.dma_start(out=y_rows[:, :, spans[u]], in_=y[u][:])
+                nc.sync.dma_start(out=y_rows[:, cols(k, per_bank), spans[u]], in_=y[u][:, cols(k, per_bank), :])
 
-        ends = [span.stop - (UNIT if width > UNIT else 0) for span, width in zip(spans, WIDTHS)]
+        ends = [span.stop - UNIT for span in spans[:-2]] + [J - UNIT, J]
 
         def stage_out(u):
             for s in range(WIDTHS[u] // UNIT):
                 weave(nc.vector.tensor_copy, y_woven[:, spans[u], :][:, cols(s, UNIT), :], y[u][:, :, cols(s, UNIT)])
             window = slice(ends[u - 1] if u else 0, ends[u])
-            quantise(y_codes[:, window], y_scales[:, window], y_woven[:, window, :])
+            if u:
+                quantise(y_codes[:, window], y_scales[:, window], y_woven[:, window, :])
             if u in CODE_STORES:
                 before = [ends[v] for v in CODE_STORES if v < u]
                 stored = slice(max(before, default=0), ends[u])
                 nc.sync.dma_start(out=code_rows[:, stored], in_=y_codes[:, stored])
 
-        order = (
-            (stage_pick, 0),
-            (stage_pick, 1),
-            (stage_pick, 2),
-            (deal_wa, 0),
-            (stage_ya, 0),
-            (stage_ya, 1),
-            (deal_wd, 0),
-            (stage_stage, 0),
-            (stage_late, 0),
-            (stage_pick, 3),
-            (stage_pick, 4),
-            (stage_ya, 2),
-            (stage_max, 0),
-            (stage_ya, 3),
-            (stage_y, 0),
-            (stage_stage, 2),
-            (stage_max, 1),
-            (stage_ya, 4),
-            (stage_y, 1),
-            (stage_stage, 3),
-            (stage_max, 2),
-            (stage_max, 3),
-            (stage_y, 2),
-            (stage_max, 4),
-            (stage_y, 3),
-            (stage_out, 0),
-            (stage_y, 4),
-            (stage_out, 1),
-            (stage_out, 2),
-            (stage_out, 3),
-            (stage_out, 4),
-        )
-        for stage, u in order:
-            stage(u)
+        lags = ((stage_pick, 0), (stage_ya, 1), (stage_stage, 2), (stage_max, 3), (stage_y, 3))
+        for tick in range(len(WIDTHS) + 3):
+            for stage, lag in lags:
+                if 0 <= tick - lag < len(WIDTHS):
+                    stage(tick - lag)
+        for u in steps:
+            stage_out(u)
 
         for q in range(QUADS):
             (nc.sync, nc.scalar)[q % 2].dma_start(

@@ -208,12 +208,6 @@ def tile_list_htabg_max_biasP_kernel(
                 out=picked[:, cols(half, HALF)],
                 in_=tab_w[:].bitcast(U32).indirect(tab_list[:, entries(cols(half, HALF))]),
             )
-        idle = bank_tile("idle", 4, [P, BANK])
-        for t in range(3):
-            nc.tensor.matmul_mx(
-                out=idle[:], rhs=picked[:, 0 : BANK // 2].bitcast(FP4X4), rhs_scale=sc0[:, 0:BANK],
-                start=True, stop=True, **stationary(wb[0], sc0, t),
-            )
         for half in range(2):
             nc.vector.tensor_copy(
                 out=parted[half][:].bitcast(U16).rearrange("p (a j) -> p a j", a=2),

@@ -126,9 +126,9 @@ def tile_list_htabg_max_biasP_kernel(
                 in_=raw.bitcast(dtype).rearrange("p (m t) -> p t m", t=PACK),
             )
 
-        def deal_words(name, raw):
+        def deal_words(copy, name, raw):
             dealt = held(name, [P, 2 * R], U8)
-            deal(nc.scalar.copy, dealt[:], raw, U16)
+            deal(copy, dealt[:], raw, U16)
             return dealt
 
         def move_rows(upper, row, quads):
@@ -158,7 +158,7 @@ def tile_list_htabg_max_biasP_kernel(
         x_planes.append(sb("x1", [P, T], F32))
         load_part(1, slice(0, T // 4))
 
-        wb = [deal_words(f"wb{a}", wb_raw[:, cols(a, 2 * R)]) for a in range(2)]
+        wb = [deal_words(nc.vector.tensor_copy, f"wb{a}", wb_raw[:, cols(a, 2 * R)]) for a in range(2)]
         identity = sb("identity", [P, P], F32)
         make_identity(nc, identity[:])
         turned = bank_tile("turned", 7, [P, P])
@@ -171,8 +171,8 @@ def tile_list_htabg_max_biasP_kernel(
             for c in range(PACK):
                 nc.tensor.transpose(bank[:, c, :], spread[:, PACK * k + c].rearrange("j g u -> j (g u)"), identity[:])
             nc.scalar.copy(out=wgt[:, cols(k, BANK)], in_=bank[:].rearrange("p c j -> p (c j)"))
-        wa = deal_words("wa", wa_raw)
-        wd = deal_words("wd", wd_raw)
+        wa = deal_words(nc.scalar.copy, "wa", wa_raw)
+        wd = deal_words(nc.scalar.copy, "wd", wd_raw)
         sc0 = sb("sc0", [P, J], U8)
         nc.vector.tensor_copy(out=sc0[:], in_=tab_sc[:].indirect(tab_list[:]))
         move_up(sc1, sc0)

@@ -29,8 +29,8 @@ QUARTER = J // 4
 EDGE = 64
 
 WIDTHS = (128, 256, 256, 128, 128, 128)
-AHEAD = 4
-STAGED = (1, 2, 3)
+AHEAD = 5
+STAGED = (1, 2)
 CODE_STORES = (2, 4, 5)
 
 
@@ -236,9 +236,9 @@ def tile_list_htabg_max_biasP_kernel(
         def quantise(codes, scales, woven):
             nc.vector.quantize_mx(out=codes.bitcast(FP8X4), scales=scales, in_=woven.rearrange("p j t -> p (j t)"))
 
-        picks = sb("picks", [P, WIDTHS[0] + PACK * J], F32)
+        picks = sb("picks", [P, PACK * J], F32)
         early = picks[:, 0 : PACK * split].rearrange("p (t j) -> p t j", t=PACK)
-        late = picks[:, WIDTHS[0] :].rearrange("p (t j) -> p t j", t=PACK)[:, :, 0 : J - split]
+        late = picks[:].rearrange("p (t j) -> p t j", t=PACK)[:, :, 0 : J - split]
         for i in range(PACK - 1):
             pick(early[:, i, :], i, slice(0, split))
 

@@ -83,7 +83,7 @@ def tile_list_htabg_max_biasP_kernel(
         def held(name, shape, dtype):
             return placed(at[name], name, shape, dtype) if name in at else sb(name, shape, dtype)
 
-        tab_sc = zeroed(nc.gpsimd, sb("tab_sc", [P, T], U8))
+        tab_sc = zeroed(nc.vector, sb("tab_sc", [P, T], U8))
         sc_raw = zeroed(nc.vector, held("sc_raw", [P, 2 * R], U8))
         sc1 = zeroed(nc.vector, sb("sc1", [P, J], U8))
 
@@ -158,7 +158,7 @@ def tile_list_htabg_max_biasP_kernel(
         x_planes.append(sb("x1", [P, T], F32))
         load_part(1, slice(0, T // 4))
 
-        wb = [deal_words(nc.vector.tensor_copy, f"wb{a}", wb_raw[:, cols(a, 2 * R)]) for a in range(2)]
+        wb = [deal_words(nc.scalar.copy, f"wb{a}", wb_raw[:, cols(a, 2 * R)]) for a in range(2)]
         identity = sb("identity", [P, P], F32)
         make_identity(nc, identity[:])
         turned = bank_tile("turned", 7, [P, P])

@@ -28,10 +28,10 @@ HALF = J // 2
 QUARTER = J // 4
 EDGE = 64
 
-WIDTHS = (128, 256, 256, 128, 128, 128)
-AHEAD = 5
-STAGED = (1, 2)
-CODE_STORES = (2, 4, 5)
+WIDTHS = (128, 256, 128, 128, 128, 128, 128)
+AHEAD = 6
+STAGED = (1,)
+CODE_STORES = (3, 5, 6)
 
 
 def tile_list_htabg_max_biasP_kernel(

from contextlib import ExitStack

import concourse.mybir as mybir
from concourse.masks import make_identity

K, L, R, N, T, J = 512, 1024, 512, 512, 2048, 1024
FLOPS = 2 * J * (K * R + L * R + R * N)

F32 = mybir.dt.float32
BF16 = mybir.dt.bfloat16
I32 = mybir.dt.int32
U32 = mybir.dt.uint32
U16 = mybir.dt.uint16
U8 = mybir.dt.uint8
FP8X4 = mybir.dt.float8_e4m3fn_x4
FP4X4 = mybir.dt.float4_e2m1fn_x4
ALU = mybir.AluOpType
IDENTITY = mybir.ActivationFunctionType.Identity

P = 128
PACK = 4
QUADS = 4
GROUP = 16
BANK = 512
BANKS = 8
UNIT = BANK // PACK
HALF = J // 2
QUARTER = J // 4
EDGE = 64

WIDTHS = (128, 256, 128, 128, 128, 128, 128)
AHEAD = 6
STAGED = (1,)
CODE_STORES = (3, 5, 6)


def tile_list_htabg_max_biasP_kernel(
    tc, tab_words, tab_scales, xT, wgt2, wa_words, wa_scales, wb_words, wb_scales,
    wd_words, wd_scales, b, offs, offs2, out_0, out_1, out_2,
):
    nc = tc.nc
    with ExitStack() as ctx:
        keep = ctx.enter_context(tc.tile_pool(name="keep", bufs=1))
        arena = ctx.enter_context(tc.tile_pool(name="arena", bufs=1))
        psum = ctx.enter_context(tc.psum_pool(name="psum", bufs=1))

        def sb(name, shape, dtype):
            return keep.tile(shape, dtype, name=name, align_bytes=64)

        def placed(offset, name, shape, dtype):
            return arena.tile(shape, dtype, name=name, offset=offset, align_bytes=64)

        def bank_tile(name, bank, shape):
            return psum.tile(shape, F32, name=name, offset=4 * BANK * bank)

        def zeroed(engine, tile):
            engine.memset(tile[:].bitcast(I32), 0)
            return tile

        def cols(i, width):
            return slice(i * width, (i + 1) * width)

        def entries(span):
            return slice(span.start // GROUP, span.stop // GROUP)

        starts = [sum(WIDTHS[:u]) for u in range(len(WIDTHS))]
        spans = [slice(s, s + w) for s, w in zip(starts, WIDTHS)]
        split = starts[AHEAD]
        steps = range(len(WIDTHS))

        tab_list = keep.tile([P, J // GROUP], U16, name="tab_list")
        head_lists = keep.tile([P, J // GROUP], U16, name="head_lists")
        at = {"sc_raw": 0, "picked": EDGE}
        at["bias"] = at["wb_raw"] = at["picked"] + 4 * J
        at["x3"] = at["tab_w"] = at["wb_raw"] + 4 * R
        at["spread"] = at["x3"] + 4 * T
        at["x2"] = at["spread"] + 4 * J - EDGE
        for e, name in enumerate(("wa", "wd")):
            at[name] = at["spread"] + 2 * R * e
        for u in steps:
            at[f"x_woven{u}"] = at["x2"] + 4 * T + 4 * PACK * (J - split) + 2 * PACK * (starts[u] - WIDTHS[0])

        def held(name, shape, dtype):
            return placed(at[name], name, shape, dtype) if name in at else sb(name, shape, dtype)

        tab_sc = zeroed(nc.vector, sb("tab_sc", [P, T], U8))
        sc_raw = zeroed(nc.vector, held("sc_raw", [P, 2 * R], U8))
        sc1 = zeroed(nc.vector, sb("sc1", [P, J], U8))

        def load_words(tile, words):
            passes = words.shape[0]
            nc.sync.dma_start(
                out=tile.bitcast(I32).rearrange("p (a c) -> p a c", a=passes),
                in_=words.bitcast(I32).rearrange("a p c -> p a c"),
            )
            return tile

        def load_scales(row, first, scales):
            passes = scales.shape[0]
            nc.sync.dma_start(
                out=sc_raw[row : row + 16, first * R : (first + passes) * R].bitcast(I32).rearrange("s (a c) -> s a c", a=passes),
                in_=scales.bitcast(I32).rearrange("a s c -> s a c"),
            )

        def load_scale_pair(tile, scales):
            for r in range(4):
                nc.sync.dma_start(
                    out=tile[r:P:16, :].bitcast(I32),
                    in_=scales.bitcast(I32).rearrange("a (q r) c -> r q a c", r=4)[r],
                )

        def move_up(upper, pair):
            nc.sync.dma_start(out=upper[0 : P - 16, :].bitcast(I32), in_=pair[16:P, :].bitcast(I32))

        def load_plane(i):
            plane = held(f"x{i}", [P, T], F32)
            nc.sync.dma_start(out=plane[:], in_=xT.rearrange("(p i) t -> p i t", i=PACK)[:, i, :])
            return plane

        def load_part(i, tokens):
            nc.sync.dma_start(out=x_planes[i][:, tokens], in_=xT.rearrange("(p i) t -> p i t", i=PACK)[:, i, tokens])

        def deal(copy, dealt, raw, dtype):
            copy(
                out=dealt.bitcast(dtype).rearrange("p (t m) -> p t m", t=PACK),
                in_=raw.bitcast(dtype).rearrange("p (m t) -> p t m", t=PACK),
            )

        def deal_words(copy, name, raw):
            dealt = held(name, [P, 2 * R], U8)
            deal(copy, dealt[:], raw, U16)
            return dealt

        def move_rows(upper, row, quads):
            for q in quads:
                nc.sync.dma_start(
                    out=upper[32 * q : 32 * q + 4, :].bitcast(I32),
                    in_=w_sc[row + 4 * q : row + 4 * q + 4, :].bitcast(I32),
                )

        def stationary(words, scales, t):
            return dict(lhsT=words[:, cols(t, 2 * P)].bitcast(FP4X4), lhsT_scale=scales[:, cols(t, P)])

        wb_raw = load_words(held("wb_raw", [P, 4 * R], U8)[:], wb_words)
        nc.sync.dma_start(tab_list[:], offs)
        wgt_rows = sb("wgt_rows", [P, P], F32)
        nc.sync.dma_start(out=wgt_rows[:], in_=wgt2.rearrange("(g u) (c j) -> u g c j", u=8, j=P)[0])
        load_scale_pair(tab_sc, tab_scales)
        tab_w = held("tab_w", [P, T], I32)
        nc.sync.dma_start(out=tab_w[:], in_=tab_words[0].rearrange("p t b -> p (t b)").bitcast(I32))
        load_scales(0, 0, wb_scales)
        load_scales(16, 0, wa_scales)
        load_scales(16, 1, wd_scales)
        nc.sync.dma_start(head_lists[:], offs2)
        wa_raw = load_words(sb("wa_raw", [P, 2 * R], U8)[:], wa_words)
        x_planes = [load_plane(0)]
        wd_raw = load_words(sb("wd_raw", [P, 2 * R], U8)[:], wd_words)
        x_planes.append(sb("x1", [P, T], F32))
        load_part(1, slice(0, T // 4))

        wb = [deal_words(nc.scalar.copy, f"wb{a}", wb_raw[:, cols(a, 2 * R)]) for a in range(2)]
        identity = sb("identity", [P, P], F32)
        make_identity(nc, identity[:])
        turned = bank_tile("turned", 7, [P, P])
        nc.tensor.transpose(turned[:], wgt_rows[:], identity[:])
        spread = placed(at["spread"], "spread", [P, J // P, 16, 8], F32)
        nc.scalar.copy(out=spread[:], in_=turned[:].rearrange("j (g c) -> j c g", c=8).unsqueeze(3).to_broadcast([P, J // P, 16, 8]))
        wgt = sb("wgt", [P, J], F32)
        for k in range(J // BANK):
            bank = bank_tile(f"wgt_bank{k}", 5 + k, [P, PACK, P])
            for c in range(PACK):
                nc.tensor.transpose(bank[:, c, :], spread[:, PACK * k + c].rearrange("j g u -> j (g u)"), identity[:])
            nc.scalar.copy(out=wgt[:, cols(k, BANK)], in_=bank[:].rearrange("p c j -> p (c j)"))
        wa = deal_words(nc.scalar.copy, "wa", wa_raw)
        wd = deal_words(nc.scalar.copy, "wd", wd_raw)
        sc0 = sb("sc0", [P, J], U8)
        nc.vector.tensor_copy(out=sc0[:], in_=tab_sc[:].indirect(tab_list[:]))
        move_up(sc1, sc0)
        w_sc = sb("w_sc", [P, 2 * R], U8)
        nc.vector.tensor_copy(
            out=w_sc[:].rearrange("p (a t m) -> p a t m", a=2, t=PACK),
            in_=sc_raw[:].rearrange("p (a m t) -> p a t m", a=2, t=PACK),
        )
        move_rows(w_sc, 0, range(1, QUADS))
        load_part(1, slice(T // 4, T))
        wb_sc0, wb_sc1 = w_sc[:, 0:R], w_sc[:, R : 2 * R]

        yb_pairs = sb("yb_pairs", [P, 2, J, 2], BF16)
        yb = yb_pairs[:].rearrange("p u j e -> p j u e")
        picked = held("picked", [P, J], U32)
        parted = [held(f"parted{c}", [P, 2 * 2 * HALF], U8) for c in range(2)]

        def table_bank(c, u):
            bank = bank_tile(f"yb_bank{c}_{u}", (2 * c + u) % 4, [P, 2, QUARTER])
            for a in range(2):
                for e in range(2):
                    nc.tensor.matmul_mx(
                        out=bank[:, e, :],
                        rhs=parted[c // 2][:, cols(2 * a + c % 2, 2 * QUARTER)].bitcast(FP4X4),
                        rhs_scale=(sc0, sc1)[a][:, cols(c, QUARTER)],
                        start=(a == 0 and e == 0), stop=(a == 1 and e == 1),
                        **stationary(wb[a], (wb_sc0, wb_sc1)[a], 2 * u + e),
                    )
            nc.scalar.activation(out=yb_pairs[:, u, cols(c, QUARTER), :], in_=bank[:].rearrange("p e j -> p j e"), func=IDENTITY)

        for half in range(2):
            nc.vector.tensor_copy(
                out=picked[:, cols(half, HALF)],
                in_=tab_w[:].bitcast(U32).indirect(tab_list[:, entries(cols(half, HALF))]),
            )
        for half in range(2):
            nc.vector.tensor_copy(
                out=parted[half][:].bitcast(U16).rearrange("p (a j) -> p a j", a=2),
                in_=picked[:, cols(half, HALF)].bitcast(U16).rearrange("p (j a) -> p a j", a=2),
            )
            for e in range(2):
                for u in range(2):
                    table_bank(2 * half + e, u)

        x_planes.append(load_plane(2))
        x_planes.append(load_plane(3))
        move_rows(wa_raw, 16, range(QUADS))
        wa_sc, wd_sc = wa_raw[:, 0:R], wa_raw[:, R : 2 * R]
        bias = placed(at["bias"], "bias", [P, PACK], F32)
        nc.sync.dma_start(out=bias[:], in_=b.rearrange("(p t) -> p t", t=PACK))

        def pick(g, i, span):
            nc.vector.tensor_tensor(g, x_planes[i][:].indirect(head_lists[:, entries(span)]), wgt[:, span], ALU.mult)

        def weave(copy, woven, planar):
            copy(
                out=woven.rearrange("p (c i) t -> p c t i", i=PACK),
                in_=planar.rearrange("p t (c i) -> p c t i", i=PACK),
            )

        def quantise(codes, scales, woven):
            nc.vector.quantize_mx(out=codes.bitcast(FP8X4), scales=scales, in_=woven.rearrange("p j t -> p (j t)"))

        picks = sb("picks", [P, PACK * J], F32)
        early = picks[:, 0 : PACK * split].rearrange("p (t j) -> p t j", t=PACK)
        late = picks[:].rearrange("p (t j) -> p t j", t=PACK)[:, :, 0 : J - split]
        for i in range(PACK - 1):
            pick(early[:, i, :], i, slice(0, split))

        y_woven = sb("y_woven", [P, J, PACK], BF16)
        y_codes = sb("y_codes", [P, J], I32)
        y_scales = sb("y_scales", [P, J], U8)
        y_rows = out_0.rearrange("(p t) j -> p t j", t=PACK)
        code_rows = out_1[0].rearrange("p j i -> p (j i)").bitcast(I32)
        x_woven, ya, staged, h_woven, y = {}, {}, {}, {}, {}

        def stage_pick(u):
            if u == AHEAD:
                for i in range(PACK - 1):
                    pick(late[:, i, :], i, slice(split, J))
            g = early[:, :, spans[u]] if u < AHEAD else late[:, :, spans[u].start - split : spans[u].stop - split]
            pick(g[:, PACK - 1, :], PACK - 1, spans[u])
            x_woven[u] = held(f"x_woven{u}", [P, WIDTHS[u], PACK], BF16)
            weave(nc.scalar.copy, x_woven[u][:], g)

        def quantised(name, woven, width):
            codes = held(name, [P, width], U32)
            scales = sb(name + "_sc", [P, width], U8)
            quantise(codes[:], scales[:], woven[:])
            return codes, scales

        def stage_ya(u):
            codes, scales = quantised(f"xq{u}", x_woven[u], WIDTHS[u])
            ya[u] = []
            for s in range(WIDTHS[u] // UNIT):
                bank = bank_tile(f"ya_bank{u}_{s}", (4 + starts[u] // UNIT + s) % BANKS, [P, PACK, UNIT])
                for t in range(PACK):
                    nc.tensor.matmul_mx(
                        out=bank[:, t, :], rhs=codes[:, cols(s, UNIT)].bitcast(FP8X4), rhs_scale=scales[:, cols(s, UNIT)],
                        start=True, stop=True, **stationary(wa, wa_sc, t),
                    )
                ya[u].append(bank[:].rearrange("p t j -> p j t"))

        def stage_stage(u):
            if u not in STAGED:
                return
            staged[u] = held(f"ya{u}", [P, WIDTHS[u], PACK], BF16)
            for s, bank in enumerate(ya[u]):
                nc.scalar.copy(out=staged[u][:, cols(s, UNIT), :], in_=bank)

        def paired(woven):
            return woven.rearrange("p j (u e) -> p j u e", e=2)

        def stage_max(u):
            h_woven[u] = held(f"h_woven{u}", [P, WIDTHS[u], PACK], BF16)
            if u in staged:
                nc.vector.tensor_tensor(paired(h_woven[u][:]), paired(staged[u][:]), yb[:, spans[u]], ALU.max)
            else:
                for s, bank in enumerate(ya[u]):
                    nc.vector.tensor_tensor(
                        paired(h_woven[u][:, cols(s, UNIT), :]), paired(bank), yb[:, spans[u]][:, cols(s, UNIT)], ALU.max,
                    )

        def stage_y(u):
            width = WIDTHS[u]
            codes, scales = quantised(f"hq{u}", h_woven[u], width)
            y[u] = sb(f"y{u}", [P, PACK, width], F32)
            per_bank = BANK // width
            for k in range(PACK // per_bank):
                rows = range(PACK)[cols(k, per_bank)]
                bank = bank_tile(f"y_bank{u}_{k}", (4 + starts[u] // UNIT + k) % BANKS, [P, per_bank, width])
                for e, t in enumerate(rows):
                    nc.tensor.matmul_mx(
                        out=bank[:, e, :], rhs=codes[:].bitcast(FP8X4), rhs_scale=scales[:],
                        start=True, stop=True, **stationary(wd, wd_sc, t),
                    )
                for e, t in enumerate(rows):
                    nc.scalar.activation(out=y[u][:, t, :], in_=bank[:, e, :], func=IDENTITY, bias=bias[:, t : t + 1])
                nc.sync.dma_start(out=y_rows[:, cols(k, per_bank), spans[u]], in_=y[u][:, cols(k, per_bank), :])

        ends = [span.stop - UNIT for span in spans[:-2]] + [J - UNIT, J]

        def stage_out(u):
            for s in range(WIDTHS[u] // UNIT):
                weave(nc.vector.tensor_copy, y_woven[:, spans[u], :][:, cols(s, UNIT), :], y[u][:, :, cols(s, UNIT)])
            window = slice(ends[u - 1] if u else 0, ends[u])
            if u:
                quantise(y_codes[:, window], y_scales[:, window], y_woven[:, window, :])
            if u in CODE_STORES:
                before = [ends[v] for v in CODE_STORES if v < u]
                stored = slice(max(before, default=0), ends[u])
                nc.sync.dma_start(out=code_rows[:, stored], in_=y_codes[:, stored])

        lags = ((stage_pick, 0), (stage_ya, 1), (stage_stage, 2), (stage_max, 3), (stage_y, 3))
        for tick in range(len(WIDTHS) + 3):
            for stage, lag in lags:
                if 0 <= tick - lag < len(WIDTHS):
                    stage(tick - lag)
        for u in steps:
            stage_out(u)

        for q in range(QUADS):
            (nc.sync, nc.scalar)[q % 2].dma_start(
                out=out_2[0, 4 * q : 4 * q + 4, :].bitcast(I32),
                in_=y_scales[32 * q : 32 * q + 4, :].bitcast(I32),
            )
